import numpy as np, ml_dtypes
CORES = [2,3,42,43,82,83,122,123]
N = 8
BF = ml_dtypes.bfloat16
L, W, RO, LX, M = 256, 8192, 4, 3, 32
KS = np.arange(16, dtype=np.int32)[:, None]
def places(c, u, a):
    return (((c * (2 * u + 1)) >> 5) + c + a) & (W - 1)
def pick(x, at):
    return np.take_along_axis(x, at.reshape(N, 8, 1, 16 * L), 3).reshape(N, 8, 16, 16, L)
def score(p):
    before = np.add.accumulate(p, axis=3) - p; e = np.add.reduce((16 - KS) * p, axis=3)
    return e, e[:, :, :, None] + KS * p - before
def plain(rng):
    return (rng.integers(0, 16, (N, 8, 16, W), dtype=np.int32), rng.integers(0, 4096, (N, 8, 16, L), dtype=np.int32), rng.integers(0, 64, (N, 8, 16, L), dtype=np.int32),
            rng.integers(0, 64, (N, 8, 16, 1), dtype=np.int32), rng.integers(45, 90, (N, 8, L), dtype=np.int32))
def stress(rng, mid):
    sh = (N, 8, 16, RO, L); kd = rng.integers(0, 3, (N, 8, 1, RO, L))
    near = mid + 18 * rng.standard_normal((N, 8, 1, RO, L)) + 12 * rng.standard_normal(sh)
    far = np.where(rng.random(sh) < 0.55, 200 + 56 * rng.random(sh), 40 * rng.random(sh))
    return np.clip(np.floor(np.where(kd == 0, near, np.where(kd == 1, 256 * rng.random(sh), far))), 0, 255).astype(np.int32)
def low(a):
    return np.asarray(a, np.float32).astype(BF)
def pack(x, c, s, y, wt, th):
    return {"x0": low(x.reshape(N, 128, W)), "c0": np.ascontiguousarray(c.reshape(N, 128, L)).astype(np.int32), "st": low(s.reshape(N, 128, RO * L)),
            "y0": low(y.reshape(N, 128, L)), "w": low(wt.reshape(N, 128, 1)), "th": low(th)}
def setup_inputs(rng):
    x, c, y, wt, th = plain(rng)
    return pack(x, c, stress(rng, 122), y, wt, th)
def setup_inputs_spread(rng):
    x, c, y, wt, th = plain(rng)
    x = np.minimum(np.floor(np.exp2(4 * rng.random((N, 8, 1, W), dtype=np.float32)) * rng.random((N, 8, 16, W), dtype=np.float32)), 15).astype(np.int32)
    c = np.floor(4096 * rng.random(c.shape) ** 3).astype(np.int32); y = np.floor(64 * rng.random(y.shape) ** 3).astype(np.int32)
    wt = np.floor(64 * rng.random(wt.shape) ** 2).astype(np.int32); th = np.floor(241 * rng.random(th.shape) ** 2).astype(np.int32)
    return pack(x, c, stress(rng, 15 + 40 * rng.random((N, 8, 1, 1, L))), y, wt, th)
def setup_inputs_ends(rng):
    sh = (N, 8, 16, RO, L); fz = (np.arange(N)[:, None] + np.arange(8)) & 1
    x = 15 * (rng.random((N, 8, 16, W), dtype=np.float32) < 0.5 * rng.integers(0, 3, (N, 8, 1, W))).astype(np.int32)
    c = 4095 * (rng.random((N, 8, 16, L)) < 0.5 * rng.integers(0, 3, (N, 8, 1, L))).astype(np.int32)
    y = 63 * (rng.random((N, 8, 16, L)) < 0.5 * rng.integers(0, 3, (N, 8, 1, L))).astype(np.int32)
    wt = 63 * (rng.random((N, 8, 16, 1)) < 0.6).astype(np.int32); wt[:, 7] = 63; wt[:, 0, 0] = 0; wt[:, :, 15] = 63
    th = 240 * rng.integers(0, 2, (N, 8, L))
    s = 255 * (rng.random(sh) < rng.choice(np.array([0.0, 0.45, 0.5, 0.55, 1.0]), (N, 8, 1, RO, L))).astype(np.int32)
    live = np.argsort(rng.random((N, 8, 1, L)), axis=-1) < 5 * L // 16; live[..., L - 4:] = False
    c = np.where(live, rng.integers(0, 4096, c.shape), c); s = np.where(live[:, :, :, None], stress(rng, 127), s)
    x[..., 0] = 15 * (1 - fz)[:, :, None]
    for u in (0, 1921): x[..., places(4095, u, 0)] = 15 * fz[:, :, None]
    x[..., 2:16] = 15; x[..., places(15, 1921, 0)] = 15
    full, none = 4095 * fz, 4095 * (1 - fz)
    y[..., L - 1] = 63; c[..., L - 1] = 0; s[:, :, :, 0, L - 1] = 255
    y[..., L - 4:L - 1] = 0; y[:, :, 15, L - 3] = 63
    for l in (L - 3, L - 2):
        c[..., l] = none[:, :, None]; c[:, :, 14, l] = full; c[:, :, 15, l] = 15; s[:, :, :, 0, l] = 30
    c[..., L - 4] = full[:, :, None]; c[:, :, 0, L - 4] = none; c[:, :, 2:, L - 4] = np.arange(2, 16); s[:, :, :, 0, L - 4] = 226
    return pack(x, c, s, y, wt, th)
def setup_inputs_corners(rng):
    x, c, y, wt, th = plain(rng); s = stress(rng, 150); n = np.arange(4096)
    typ = rng.integers(0, 4, (N, W)); p0 = int(places(4075, 2046, 0)); typ[:, p0] = 1; typ[:, (p0 + 1) & (W - 1)] = 0
    tb = typ[:, None, None, :]
    x = np.where(tb == 0, 0, np.where(tb == 1, 15, np.where(tb == 2, 13 + x % 3, x))).astype(np.int32)
    wt[:, :, 0] = 63; wt[:, :, 1] = 1; par = np.arange(L) & 1
    kd = np.stack([rng.permutation(L) % 8 for g in range(8)]); iu = rng.integers(0, 5, (8, L))
    top = (kd == 0) & (par == 1); fold = (kd == 0) & ((np.arange(L) & 3) == 0)
    iu = np.where(top, 3, np.where(fold, 2, iu)); ctl = (kd > 0) | top | fold
    y = np.where(ctl[:, None, :], 0, y); y[:, :, 0] = np.where(ctl, np.array([0, 0, 32, 32, 32])[iu], y[:, :, 0]); y[:, :, 1] = np.where(ctl, np.array([0, 1, 30, 31, 32])[iu], y[:, :, 1])
    c = np.where(top[:, None, :], 4095 - rng.integers(0, 3, c.shape), c)
    c = np.where(fold[:, None, :] & (rng.random(c.shape) < 0.5), 4075, c)
    th = rng.choice(np.array([0, 1, 60, 239, 240]), (N, 8, L)); th = np.where(kd == 7, rng.choice(np.array([0, 239]), (N, 8, L)), th)
    kb = kd[:, None, :]; a = rng.integers(8, 15, (8, 1, L)); b = np.minimum(15, a + 1 + rng.integers(0, 7, (8, 1, L))); z = np.zeros((8, 16, L), np.int64)
    want = np.select([kb == 1, (kb == 2) | (kb == 3), (kb == 4) | (kb == 7), kb == 5, kb == 6], [z + ((KS == a) | (KS == b)), z + (KS == b), z, z + 2, z + np.where(par == 1, KS > 0, True)], z - 1)
    eight = (7 * KS + np.arange(L)) % 16
    two = z + np.where((eight == 0) & (par == 1) & (b > a + 1), (225 + 15 * (16 - a)) >> 3, 30)
    s0 = np.select([kb == 1, kb == 2, kb == 3, kb == 4, kb == 5, kb == 6, kb == 7],
                   [two, z + 30 + (eight == 0) * par, z + 31, z + np.where(eight < 8 + par, 0, 255), 254 + rng.integers(0, 2, (8, 16, L)), z + np.where(par == 1, 226, 255), z + np.where(eight < 8, 0, 255)], z - 1)
    s[:, :, :, 0] = np.where(s0 < 0, s[:, :, :, 0], s0)
    us = np.array([0, 1, 2046, 2047, 0])
    for q in range(N):
        for i in range(5):
            kind = typ[q][places(n, us[i], 0)]
            for v in range(3):
                ix = np.flatnonzero(kind == v); ix = ix if len(ix) else n
                m = (iu == i)[:, None, :] & (want == v); c[q][m] = ix[rng.integers(0, len(ix), int(np.count_nonzero(m)))]
    for q in range(1, N, 2):
        s[q, :, :, 0] = np.where(kb == 7, 0, s[q, :, :, 0])
        for g, l in zip(*np.nonzero(kd == 7)):
            e = int(c[q - 1, g, 1, l]); kind = typ[q][(((n * e) >> 5) + n + 37 * e) & (W - 1)]; pos = (0, 14, 15, 16)[int(rng.integers(0, 4))]
            i0 = np.flatnonzero(kind == 0); i1 = np.flatnonzero(kind == 1); i0 = i0 if len(i0) else n; i1 = i1 if len(i1) else n
            zero = np.arange(16) >= pos; zero = zero & ((np.arange(16) == pos) | (rng.random(16) < 0.5))
            c[q, g, :, l] = np.where(zero, i0[rng.integers(0, len(i0), 16)], i1[rng.integers(0, len(i1), 16)])
    return pack(x, c, s, y, wt, th)
def setup_inputs_crowd(rng):
    x, c, y, wt, th = plain(rng); x = np.minimum(x, 14); s = stress(rng, 115)
    for q in range(N):
        for t in range(RO):
            kk = (q + t) % 4; g = (q + 3 * t + 7) % 8; l = (L - 1, 0)[t & 1]
            if kk < 2: s[q, :, :, t] = 255
            if kk == 1: s[q, g, :, t, l] = 0
            if kk == 3: s[q, :, :, t] = 0
            if kk == 3 and t != 1: s[q, g, :, t, l] = 255
    one = rng.integers(0, 4096, 8); one[2] = 4095; one[4] = 0
    for g in range(6):
        if g & 1: c[:, g, :, :L - 1] = one[g]
        else: c[:, g] = one[g]
    y[:, :4] = y[:, :4, :, :1].copy()
    th = np.where(rng.random(th.shape) < 0.5, th, 240 * rng.integers(0, 2, th.shape))
    return pack(x, c, s, y, wt, th)
def setup_inputs_ties(rng):
    x, c, y, wt, th = plain(rng); few = rng.integers(0, 16, (N, 8, 16, 40), dtype=np.int32); few[:, 1::2] = 8 * rng.integers(0, 2, (N, 4, 16, 40))
    x = np.ascontiguousarray(np.take_along_axis(few, rng.integers(0, 40, (N, 8, 1, W)), 3))
    c[:, 3] = rng.choice(np.array([0, 1, 2048, 4094, 4095]), (N, 16, L))
    u = np.add.reduce(wt * y, axis=2) & 2047; e, ek = score(pick(x, places(c, u[:, :, None], 0)))
    at = np.take_along_axis(ek, rng.integers(0, 16, (N, 8, 1, 1, L)), 3)[:, :, :, 0]
    s = stress(rng, 110); s[:, :, :, 0] = np.clip((at >> 3) + rng.integers(0, 2, (N, 8, 1, L)) * (rng.random(at.shape) < 0.4), 0, 255)
    th = rng.choice(np.array([0, 48, 56, 64]), (N, 8, L))
    return pack(x, c, s, y, wt, th)
def check_inputs(d):
    bad = []
    for k, hi in (("x0", 15), ("c0", 4095), ("st", 255), ("y0", 63), ("w", 63), ("th", 240)):
        v = np.asarray(d[k]).astype(np.float64)
        if not (np.min(v) >= 0 and np.max(v) <= hi): bad.append("range of " + k)
        elif np.any(v != np.floor(v)): bad.append("whole numbers in " + k)
    return bad
def reference(x0, c0, st, y0, w, th):
    x = x0.astype(np.int32).reshape(N, 8, 16, W); c = c0.astype(np.int32).reshape(N, 8, 16, L); y = y0.astype(np.int32).reshape(N, 8, 16, L)
    s = 8 * st.astype(np.int32).reshape(N, 8, 16, RO, L); wt = w.astype(np.int32).reshape(N, 8, 16, 1); bound = th.astype(np.int32)[:, :, None]
    a = np.zeros((N, 1, 1, 1), np.int64)
    for t in range(RO):
        u = (np.add.reduce(wt * y, axis=2) & 2047)[:, :, None]
        p = pick(x, places(c, u, a)); e, ek = score(p)
        g = np.add.reduce((ek >= s[:, :, :, t][:, :, :, None]).astype(np.int32), axis=2)
        best = 1 + np.argmax(g[:, :, 1:], axis=2)[:, :, None]
        g0 = g[:, :, :1]; gb = np.take_along_axis(g, best, 2)
        rest = g0 >= 9; move = ~rest & (gb > g0); go = ~rest & ~move
        name = np.take_along_axis(c, best, 2); v = np.take_along_axis(p, best[:, :, :, None], 3)[:, :, :, 0]
        fresh = (((name * u) >> 5) + u) & 4095
        down = np.concatenate([name, c[:, :, :15]], axis=2); up = np.concatenate([c[:, :, 1:], fresh], axis=2)
        c = np.where(move, np.where((KS <= best) | ((u & 1) == 1), down, c), np.where(go & (KS >= best), up, c))
        src = (np.arange(N) - 1 - t % (N - 1)) % N; ce, cv, come = name[src], v[src], go[src]
        h = (((c * ce) >> 5) + c + 37 * ce) & (W - 1)
        hit = np.add.reduce(np.abs(pick(x, h) - cv[:, :, :, None]), axis=2) <= bound
        pos = np.where(np.any(hit, axis=2), 1 + np.argmax(hit, axis=2), 0)[:, :, None]
        put = np.where(KS < pos, c, np.where(KS == pos, ce, np.concatenate([c[:, :, :1], c[:, :, :15]], axis=2)))
        c = np.where(come, put, c)
        y = e >> 5; a = np.add.reduce(go.reshape(N, -1).astype(np.int64), axis=1).reshape(N, 1, 1, 1)
        if t < LX:
            col = np.broadcast_to(M * np.arange(L) + (u & (M - 1)), (N, 8, 16, L))
            np.put_along_axis(x, col, ((np.take_along_axis(x, col, 3) + (e >> 7)) >> 1).astype(np.int32), 3)
    return {"yc": c.reshape(N, 128, L).astype(np.float32), "yy": y.reshape(N, 128, L).astype(np.float32).astype(BF)}

@@ -1,0 +1,668 @@
+from concourse.mybir import AluOpType as A, AxisListType, ActivationFunctionType as F
+
+N, L, W, RO = 8, 256, 8192, 4
+NC = 2
+CL = L // NC
+CE = 16 * CL
+NU = CL // 64
+GL = 32
+GP = CL // GL
+NB = CL // 16
+UC = 64
+NH = CL // UC
+KQ = 8
+TWO = False
+CMP_S = ()
+ABS_S = ()
+YB, WB = 160.0, 320.0
+
+f32, bf, f16, i32, u16 = "float32", "bfloat16", "float16", "int32", "uint16"
+SCRATCH = {n: ("sbuf", [128, w], d) for n, w, d in [
+    ("XA", W, bf), ("XB", W, bf), ("cin", L, i32), ("stS", RO * L, bf), ("yin", L, bf), ("wS", 1, bf), ("thS", L, bf),
+    ("cn", L, f16), ("yb", L, bf), ("ycS", L, f32), ("yyS", L, bf), ("P", NC * (CE + 16), bf),
+    ("PTs", 16 * L, bf), ("Ib", 16 * L, bf), ("x2", 16 * L, bf), ("mx", 16 * L, bf),
+    ("ui", L, i32), ("uu", L, i32), ("odd", L, i32), ("Ls", L, f32), ("L2", L, f32), ("va", L, i32), ("vb", L, i32),
+    ("off1", L, u16), ("off2", L, u16), ("offv", 16, u16), ("offr", 32, u16),
+    ("pw", L, bf), ("sg", L, bf), ("nmd", L, bf), ("mu", L, bf), ("fa", L, i32), ("fb", L, i32), ("fr", L, f16),
+    ("ts", L, f32), ("zz", L, f32), ("eta", L, bf), ("qq", L, bf), ("ez", L, f32), ("Wn", L, bf), ("nx", 2 * L, bf),
+    ("ra", 16, i32), ("rb", 16, i32), ("rc", 16, i32), ("cnt", NC, f32), ("cs", 1, f32), ("col", 32, f32),
+    ("msg", RO * L, f16), ("land", RO * L, f16), ("msgv", RO * L, bf), ("landv", RO * L, bf),
+    ("k32", 13 * 128, f32), ("kb", 17 * 128, bf), ("kh", 7 * 128, f16), ("SelL", CE, bf), ("stT", NC * 128, bf), ("i0", L, bf),
+    ("Sel", 144, bf), ("SelN", 144, bf), ("SelK", 144, bf), ("SelW", 144, bf),
+    ("crow", 9 * 128, bf), ("ln16", 16, f32), ("ln16b", 16, bf), ("ln32", 16, f32), ("ln32c", 16, f32)]}
+SCRATCH.update({"R": ("psum", [128, 2048], f32), "PTp": ("psum", [128, 1024], bf),
+                "B0": ("psum", [128, 512], f32), "B1": ("psum", [128, 512], f32), "BS": ("psum", [128, 512], f32)})
+SEMAPHORES = (["sV", "sS", "sT", "sG", "sent", "dX0", "dX1", "dXB", "dc", "dst0", "dst1", "dy", "dw", "dth", "oy"]
+              + ["oc%d" % c for c in range(NC)] + ["arr%d%s" % (i, x) for i in range(RO * NC) for x in "ab"])
+
+FIG = dict(cy=0.00100, ga=1.56, sc=3.8, pe=0.00050, lat=0.12, ov=0.02, far=3.0)
+FIGS = [FIG, dict(FIG, ga=1.1, sc=2.0, lat=0.08, far=2.5), dict(FIG, ga=2.0, sc=5.5, lat=0.2, far=5.0), dict(FIG, pe=0.0007, ov=0.05)]
+TRIES = 1500
+EARLY = 40.0
+
+
+def cost(o, e, P):
+    cy, ga, sc, pe, k, fix = o["c"][e]
+    return (cy + ga * P["ga"] + sc * P["sc"]) * P["cy"] + pe * P["pe"] + k * P["ov"] * (0.5 if e == "T" else 1) + fix
+
+
+def build(g, T, topo, core, rank):
+    ops = []
+    V, S, Pm = g.vector, g.scalar, g.tensor
+
+    def op(c, rd, wr, fn, banks=(), lat=0.0, sem=None, grp=0):
+        ops.append(dict(eng="".join(c), c=c, rd=list(rd), wr=list(wr), fn=fn, banks=list(banks), lat=lat, sem=sem, grp=grp, soft=[]))
+
+    def vop(n, rd, wr, fn, banks=(), ga=0, sc=0):
+        op({"V": (max(64, n) if n else 50, ga, sc, 0, 1, 0)}, rd, wr, lambda e: [fn()], banks)
+
+    def vops(k, n, rd, wr, fn, banks=()):
+        op({"V": (k * max(64, n), 0, 0, 0, k, 0)}, rd, wr, fn, banks)
+
+    def sop(n, rd, wr, fn, banks=()):
+        op({"S": (max(64, n), 0, 0, 0, 1, 0.05)}, rd, wr, lambda e: [fn()], banks)
+
+    def scale(nv, ns, out, in_, by, add, rd, wr, banks=()):
+        def fn(e):
+            if e == "S":
+                return [S.activation(out, in_, F.Identity, bias=add, scale=by)]
+            if by == 1.0 and add == 0.0:
+                return [V.tensor_copy(out, in_)]
+            return [V.tensor_scalar(out, in_, by, add, A.mult, A.add)]
+        op({"V": (max(64, nv), 0, 0, 0, 1, 0), "S": (max(64, ns), 0, 0, 0, 1, 0.05)}, rd, wr, fn, banks)
+
+    def gop(n, rd, wr, fn):
+        op({"G": (2 * n, 0, 0, 0, 0, 0.17)}, rd, wr, lambda e: [fn()])
+
+    def top(k, n, rd, wr, fn, banks, grp=3):
+        op({"T": (0, 0, 0, n, k, 0.0)}, rd, wr, fn, banks, grp=grp)
+
+    def mm(out, terms, rd, wr, bank, first=True, last=True, n=CL):
+        def fn(e):
+            return [Pm.matmul(out, l, r, first and i == 0, last and i == len(terms) - 1) for i, (l, r) in enumerate(terms)]
+        top(len(terms), len(terms) * max(64, n), rd, wr, fn, [bank], first + 2 * last)
+
+    lastd = []
+
+    def dma(q, out, in_, rd, wr, sem, lat):
+        op({q: (0, 0, 0, 0, 0, 0.05)}, rd, wr, lambda e: [(g.sync if q == "Y" else g.scalar).dma_start(out, in_)], lat=lat, sem=(sem, 16))
+        if q == "Y":
+            ops[-1]["soft"] = lastd[-1:]
+            lastd.append(len(ops) - 1)
+
+    def m128(buf, i):
+        return buf[:, i * 128:(i + 1) * 128]
+
+    def mcl(buf, i):
+        return buf[:, i * CL:(i + 1) * CL]
+
+    dma("Y", T.yin[:, :], T.y0[:, :], [], ["yin"], "dy", 2.0)
+    dma("Y", T.wS[:, :], T.w[:, :], [], ["wS"], "dw", 2.0)
+    dma("Y", T.cin[:, :], T.c0[:, :], [], ["cin"], "dc", 2.0)
+    dma("S", T.XA[:, 0:W // 2], T.x0[:, 0:W // 2], [], ["XA0"], "dX0", 8.0)
+    dma("Y", T.XA[:, W // 2:W], T.x0[:, W // 2:W], [], ["XA1"], "dX1", 8.0)
+    dma("Y", T.stS[:, 0:L], T.st[:, 0:L], [], ["st0"], "dst0", 8.5)
+    dma("Y", T.thS[0:8, :], T.th[:, :], [], ["th"], "dth", 8.5)
+    dma("Y", T.stS[:, L:RO * L], T.st[:, L:RO * L], [], ["st1"], "dst1", 9.0)
+    XX = [(T.XA, ["XA0", "XA1"])] * 2
+    if TWO:
+        dma("Y", T.XB[:, :], T.x0[:, :], ["XA0", "XA1"], ["XB0", "XB1"], "dXB", 8.0)
+        XX[1] = (T.XB, ["XB0", "XB1"])
+
+    k32 = {n: i for i, n in enumerate(["one", "t0", "BO", "ID", "LT", "LE", "SD", "SU", "A32", "t1", "t2", "t3", "t4"])}
+    kb = {n: i for i, n in enumerate(["ID", "Mm", "Bm", "OH", "Ld", "Vu", "Qm", "KI", "nKI", "KSD", "KIS", "Wm", "E8", "one", "BO", "BOs", "nID"])}
+    kh = {n: i for i, n in enumerate(["ID", "SD", "SU", "BO", "R0", "R15", "BO3"])}
+    cols = {n: i for i, n in enumerate(["n", "r0", "r15", "cM", "rpos", "s", "mid", "c0", "dLd", "hVu", "kw", "thr", "bVu", "bQ",
+                                        "j16", "j32", "a32", "wf", "cU", "cA", "sE", "bE"])}
+    K = lambda n: m128(T.k32, k32[n])
+    Kb = lambda n: m128(T.kb, kb[n])
+    Kh = lambda n: m128(T.kh, kh[n])
+    C = lambda n: T.col[:, cols[n]:cols[n] + 1]
+    K8 = lambda n: T.k32[:, k32[n] * 128:(k32[n] + 1) * 128:16]
+    top8 = lambda buf, i: buf[0:8, i * 128:(i + 1) * 128]
+
+    vop(128, [], ["k.one"], lambda: V.memset(K("one"), 1.0))
+
+    def asel(out, in_, pat, cmp, fill, base, cm, view=m128):
+        gop(128, ["k." + in_], ["k." + out], lambda: g.affine_select(view(T.k32, k32[out]), view(T.k32, k32[in_]), pat, cmp, fill, base, cm))
+    asel("t0", "one", [[-16, 8], [0, 16]], A.is_ge, 0.0, 0, 1)
+    asel("BO", "t0", [[16, 8], [0, 16]], A.is_ge, 0.0, 15, -1)
+    asel("LT", "BO", [[1, 128]], A.is_ge, 0.0, -1, -1)
+    asel("ID", "one", [[-1, 128]], A.is_equal, 0.0, 0, 1)
+    asel("LE", "BO", [[1, 128]], A.is_ge, 0.0, 0, -1)
+    asel("SD", "BO", [[1, 128]], A.is_equal, 0.0, -1, -1)
+    asel("SU", "BO", [[1, 128]], A.is_equal, 0.0, 1, -1)
+    gop(8, [], ["ln16"], lambda: g.iota(T.ln16[:, :], [[256, 16]], 0, 0, allow_small_or_imprecise_dtypes=True))
+    gop(16, [], ["ln32"], lambda: g.iota(T.ln32[:, :], [[512, 16]], 0, 0, allow_small_or_imprecise_dtypes=True))
+    asel("t3", "one", [[1, 128]], A.is_ge, 0.0, 0, -16, top8)
+    asel("t3", "t3", [[-1, 128]], A.is_ge, 0.0, 15, 16, top8)
+    E8 = top8(T.kb, kb["E8"])
+    scale(128, 128, E8, top8(T.k32, k32["t3"]), 1.0, 0.0, ["k.t3"], ["b.E8"])
+
+    def cts(out, in_, s1, s2, o0, o1=None):
+        if o1 is None:
+            vop(1, ["c." + in_], ["c." + out], lambda: V.tensor_scalar(C(out), C(in_), s1, None, o0))
+        elif (o0, o1) == (A.mult, A.add):
+            scale(1, 1, C(out), C(in_), s1, s2, ["c." + in_], ["c." + out])
+
+    def sc(out, otok, in_, by):
+        col = isinstance(by, str)
+        scale(128, 128, out, K(in_), C(by) if col else by, 0.0, ["k." + in_] + (["c." + by] if col else []), [otok])
+    scale(1, 1, C("wf"), T.wS[:, :], 1.0, 0.0, ["wS"], ["c.wf"])
+    sc(Kb("Wm"), "b.Wm", "BO", "wf")
+    vop(64, [], ["b.one"], lambda: V.memset(Kb("one"), 1.0))
+    vop(1, [], ["c.cA"], lambda: V.memset(C("cA"), -262144.0))
+    vop(128, ["k.LT"], ["c.n"], lambda: V.tensor_reduce(C("n"), K("LT"), AxisListType.X, A.add))
+    cts("r0", "n", 15.0, None, A.is_equal)
+    cts("r15", "n", 0.0, None, A.is_equal)
+    cts("cM", "n", 0.125, 0.125, A.mult, A.add)
+    cts("rpos", "n", 15.0, None, A.is_lt)
+    vop(1, ["c.r0", "c.r15"], ["c.s"], lambda: V.tensor_tensor(C("s"), C("r0"), C("r15"), A.add))
+    vop(1, ["c.r0", "c.r15"], ["c.dLd"], lambda: V.tensor_tensor(C("dLd"), C("r15"), C("r0"), A.subtract))
+    for out, in_, a, b in (("mid", "s", -0.5, 0.5), ("c0", "r0", -101.0, 1.0), ("hVu", "s", -0.5, 0.0), ("kw", "s", 2048.5, -0.5),
+                           ("thr", "r15", -54.6, 0.0), ("bVu", "dLd", 0.5, -0.5), ("bQ", "n", -8.5, 120.0), ("j16", "n", -16.0, 240.0),
+                           ("j32", "n", -32.0, 480.0), ("a32", "r15", 32.0, 0.0), ("sE", "r0", 4.0, 4.0), ("bE", "r0", -64.0, 0.0)):
+        cts(out, in_, a, b, A.mult, A.add)
+    for nm, in_, by in (("ID", "ID", 1.0), ("KI", "ID", 4096.0), ("nKI", "ID", -4096.0), ("KSD", "SD", 4096.0)):
+        sc(Kb(nm), "b." + nm, in_, by)
+    sc(K("A32"), "k.A32", "one", "a32")
+
+    def inblock(out, otok, prim, a, b, tmp):
+        cv = lambda x: C(x) if isinstance(x, str) else x
+        scale(128, 128, K(tmp), K(prim), cv(a), cv(b), ["k." + prim] + ["c." + x for x in (a, b) if isinstance(x, str)], ["k." + tmp])
+        vop(256, ["k." + tmp, "k.BO"], [otok], lambda: V.tensor_tensor(out, K(tmp), K("BO"), A.mult))
+    inblock(K("t1"), "k.t1", "LT", -0.125, "cM", "t1")
+    asel("t1", "t1", [[-1, 128]], A.not_equal, 2.0, 0, 1)
+    sc(Kb("Mm"), "b.Mm", "t1", 1.0)
+    inblock(K("t2"), "k.t2", "LE", 32.0, -1.0, "t2")
+    sc(Kb("Bm"), "b.Bm", "t2", "rpos")
+    bm = kb["Bm"] * 128
+    scale(8, 8, T.kb[:, bm:bm + 128:16], K8("BO"), C("c0"), 0.0, ["k.BO", "c.c0"], ["b.Bm"])
+    scale(8, 8, T.kb[:, bm + 15:bm + 128:16], K8("BO"), C("r0"), 0.0, ["k.BO", "c.r0"], ["b.Bm"])
+    vop(256, ["k.ID", "k.SD"], ["k.t0"], lambda: V.tensor_tensor(K("t0"), K("ID"), K("SD"), A.subtract))
+    sc(Kb("OH"), "b.OH", "t0", "mid")
+    sc(Kb("KIS"), "b.KIS", "t0", 4096.0)
+    inblock(Kb("Ld"), "b.Ld", "SD", "mid", "dLd", "t4")
+    inblock(Kb("Vu"), "b.Vu", "ID", "mid", "hVu", "t2")
+    inblock(Kb("Qm"), "b.Qm", "LT", 8.5, -0.5, "t4")
+    for nm in ("ID", "SD", "SU", "BO"):
+        vop(128, ["k." + nm], ["h." + nm], lambda nm=nm: V.tensor_copy(Kh(nm), K(nm)))
+    sc(Kb("BOs"), "b.BOs", "BO", -1.0 / 1024)
+    sc(Kb("BO"), "b.BO", "BO", 1.0)
+    if ABS_S:
+        sc(Kb("nID"), "b.nID", "ID", -1.0)
+    if CMP_S:
+        vop(CE // 2, [], ["SelL"], lambda: V.memset(T.SelL[:, :], -1.0))
+        vop(CL, [], ["SelL"], lambda: V.memset(T.SelL[:, 0:CE:16], 0.0))
+        gop(CE, ["SelL"], ["SelL"], lambda: g.affine_select(T.SelL[:, :], T.SelL[:, :], [[-1, CL], [0, 16]], A.is_equal, 0.0, 0, 1))
+    vop(128, ["k.BO"], ["h.BO3"], lambda: V.tensor_scalar(Kh("BO3"), K("BO"), 3232.0, None, A.mult))
+    vop(128, ["k.BO"], ["h.R0"], lambda: V.tensor_scalar(Kh("R0"), K("BO"), 0.0, None, A.mult))
+    vop(8, ["k.BO"], ["h.R0"], lambda: V.tensor_copy(T.kh[:, kh["R0"] * 128:(kh["R0"] + 1) * 128:16], K8("BO")))
+    vop(128, ["k.ID", "c.r15"], ["h.R15"], lambda: V.tensor_scalar(Kh("R15"), K("ID"), C("r15"), None, A.mult))
+    sel = lambda buf, k: buf[:, 16 - k:144 - k]
+    vop(72, [], ["Sel"], lambda: V.memset(T.Sel[:, :], 0.0))
+    scale(8, 8, T.Sel[:, 16:144:16], K8("BO"), 1.0, 0.0, ["k.BO"], ["Sel"])
+    scale(72, 144, T.SelW[:, :], T.Sel[:, :], C("wf"), 0.0, ["Sel", "c.wf"], ["SelW"])
+    scale(72, 144, T.SelK[:, :], T.Sel[:, :], C("kw"), 0.0, ["Sel", "c.kw"], ["SelK"])
+    scale(72, 144, T.SelN[:, :], T.Sel[:, :], -2.0, 0.0, ["Sel"], ["SelN"])
+    scale(16, 16, T.ln16b[:, 0:8], T.ln16[:, 0:8], 1.0, C("j16"), ["ln16", "c.j16"], ["ln16b"])
+    scale(16, 16, T.ln32c[:, :], T.ln32[:, :], 1.0, C("j32"), ["ln32", "c.j32"], ["ln32c"])
+    rows = [("OH", 0.0, {1: 0.5, 15: 0.5}), ("Ld", 2.5, {0: 2.0, 1: 2.0}), ("e32", 2080.0, {}), ("Tu", -4096.0, {}), ("L2", 1441792.0, {}),
+            ("Td", -4096.0, {0: -8192.0}), ("Te", -8192.0, {0: -4096.0}), ("TdL", -2048.0, {0: -6144.0}), ("TeL", -6144.0, {0: -2048.0})]
+    cr = {}
+    for i, (nm, val, ex) in enumerate(rows):
+        cr[nm] = T.crow[0:1, i * 128:(i + 1) * 128]
+        vop(64, [], ["r." + nm], lambda nm=nm, val=val: V.memset(cr[nm], val))
+        if ex:
+            vops(len(ex), 8, [], ["r." + nm],
+                 lambda e, i=i, ex=ex: [V.memset(T.crow[0:1, i * 128 + kk:(i + 1) * 128:16], vv) for kk, vv in ex.items()])
+    one1 = T.kb[0:1, kb["one"] * 128:kb["one"] * 128 + CL]
+    PW = CE + 16
+    vops(NC, 16, [], ["Pz"], lambda e: [V.memset(T.P[:, c * PW + CE:(c + 1) * PW], 255.0) for c in range(NC)])
+    every = lambda n: [n + str(c) for c in range(NC)]
+    parts = lambda n, cs=range(NC): ["%s%d.%d" % (n, c, h) for c in cs for h in range(NH)]
+
+    vop(L, ["cin"], every("cn"), lambda: V.tensor_scalar(T.cn[:, :], T.cin[:, :], -2048.0, None, A.add))
+    scale(L // 2, L, T.yb[:, :], T.yin[:, :], 1.0, YB, ["yin"], parts("yb"))
+    mm(T.BS[:, 480:482], [(Kb("Wm"), T.kb[:, kb["one"] * 128:kb["one"] * 128 + 2])], ["b.Wm", "b.one"], ["s.cU"], 7, n=2)
+    scale(1, 1, C("cU"), T.BS[:, 480:481], -YB, 0.0, ["s.cU"], ["c.cU"], [7])
+
+    def gather(t, out_buf, base, off, c, otok, ftok):
+        X, xt = XX[t % 2]
+        for q in range(GP):
+            def fn(e, q=q):
+                o = out_buf[:, base + q * GL * 16:base + (q + 1) * GL * 16]
+                src = X[:, 0:W].indirect(off[:, c * CL + q * GL:c * CL + (q + 1) * GL])
+                return [V.tensor_copy(o, src) if e == "V" else S.activation(o, src, F.Copy)]
+            op({"V": (50, GL * 16, 0, 0, 1, 0), "S": (65, GL * 16, 0, 0, 1, 0)}, xt + [ftok], ["%s.%d" % (otok, q)], fn)
+
+    def index(c, Fp, ftok, bank, Lb, ltok, off, otok):
+        vop(CL, [ftok, ltok], ["va%d" % c], lambda: V.tensor_tensor(mcl(T.va, c), Fp, mcl(Lb, c), A.add), [bank])
+        vop(CL, ["va%d" % c], ["vb%d" % c], lambda: V.tensor_scalar(mcl(T.vb, c), mcl(T.va, c), 5, W - 1, A.arith_shift_right, A.bitwise_and))
+        vop(CL, ["vb%d" % c], [otok], lambda: V.tensor_copy(mcl(off, c), mcl(T.vb, c)))
+
+    def tiles(c):
+        Bk = (T.B0, T.B1)[c % 2]
+        o = (c // 2) * 4 * CL
+        return ((lambda i, h=None: Bk[:, o + i * CL:o + (i + 1) * CL] if h is None else Bk[:, o + i * CL + h * UC:o + i * CL + (h + 1) * UC]),
+                (lambda i: "B%d.%d" % (c, i)), 5 + c % 2)
+
+    def select(c, bias, out, otok):
+        B, tk, bank = tiles(c)
+        sop(CL, [tk(0)], ["ts%d" % c], lambda: S.activation(mcl(T.ts, c), B(0), F.Identity, bias=bias), [bank])
+        vop(CL, [tk(2), "ts%d" % c], ["zz%d" % c], lambda: V.tensor_tensor(mcl(T.zz, c), mcl(T.ts, c), B(2), A.max), [bank])
+        vop(CL, [tk(3), "zz%d" % c], [otok], lambda: V.tensor_tensor(mcl(out, c), mcl(T.zz, c), B(3), A.max), [bank])
+
+    def phase_p(t, c):
+        B, tk, bank = tiles(c)
+        s = str(c)
+        m = lambda buf: mcl(buf, c)
+        M = m(T.BS)
+        mm(M, [(Kb("Wm"), m(T.yb))], ["b.Wm"] + parts("yb", [c]), ["s.M" + s], 7)
+        vop(CL, ["s.M" + s, "c.cU"], ["ui" + s], lambda: V.tensor_scalar(m(T.ui), M, C("cU"), None, A.add), [7])
+        vop(CL, ["ui" + s], ["uu" + s], lambda: V.tensor_scalar(m(T.uu), m(T.ui), 2047, None, A.bitwise_and))
+        vop(CL, ["uu" + s], ["s.M" + s], lambda: V.tensor_scalar(M, m(T.uu), 2.0, 33.0, A.mult, A.add), [7])
+        sop(CL, ["s.M" + s, "c.cA"], ["Ls" + s], lambda: S.activation(m(T.Ls), M, F.Identity, bias=C("cA"), scale=2048.0), [7])
+        vop(CL, ["ui" + s], ["odd" + s], lambda: V.tensor_scalar(m(T.odd), m(T.ui), 1, None, A.bitwise_and))
+        vop(CL, ["cn" + s, "s.M" + s], ["s.M" + s], lambda: V.tensor_tensor(M, m(T.cn), M, A.mult), [7])
+        index(c, M, "s.M" + s, 7, T.Ls, "Ls" + s, T.off1, "off1" + s)
+        gather(t, T.P, c * PW, T.off1, c, "P" + s, "off1" + s)
+        r0 = (c * NU) % 2
+        onS = c in CMP_S
+        if onS:
+            top(1, 128, ["b.ID", "st%d" % min(t, 1)], ["PTp"],
+                lambda e: [Pm.transpose(T.PTp[0:CL, 0:128], mcl(T.stS, t * NC + c), Kb("ID"))], [4])
+            scale(64, 128, T.stT[0:CL, c * 128:(c + 1) * 128], T.PTp[0:CL, 0:128], 1.0, 0.0, ["PTp"], ["stT" + s], [4])
+        for h in range(NU):
+            top(8, 1024, ["b.ID"] + ["P%s.%d" % (s, q) for q in range(h * 64 // GL, (h + 1) * 64 // GL)], ["PTp"],
+                lambda e, h=h: [Pm.transpose(m128(T.PTp, b), T.P[:, c * PW + (8 * h + b) * 128:c * PW + (8 * h + b + 1) * 128], Kb("ID"))
+                                for b in range(8)], [4])
+            u = c * NU + h
+            scale(512, 1024, T.PTs[:, u * 1024:(u + 1) * 1024], T.PTp[:, :], 1.0, 0.0, ["PTp"], ["PT%d" % u], [4])
+
+            def sums(e, h=h, u=u):
+                ins = []
+                for b in range(8):
+                    ins.append(Pm.matmul(m128(T.R, 8 * (r0 + h) + b), m128(T.PTs, 8 * u + b), Kb("Mm"), True, not onS))
+                    if onS:
+                        ins.append(Pm.matmul(m128(T.R, 8 * (r0 + h) + b), T.stT[0:CL, c * 128:(c + 1) * 128],
+                                             T.SelL[0:CL, (8 * h + b) * 128:(8 * h + b + 1) * 128], False, True))
+                return ins
+            top(8 + 8 * onS, 1024 + 1024 * onS, ["b.Mm", "PT%d" % u] + (["stT" + s, "SelL"] if onS else []), ["R%d" % (r0 + h)], sums,
+                [2 * (r0 + h), 2 * (r0 + h) + 1])
+        def judge(h):
+            u0 = r0 + h * UC // 64
+            RB = list(range(2 * u0, 2 * u0 + UC // 32))
+            RT = ["R%d" % (u0 + i) for i in range(UC // 64)]
+            Rk = lambda k: T.R[:, u0 * 1024 + k:u0 * 1024 + 16 * UC:16]
+            l0 = c * CL + h * UC
+            stv = T.stS[:, t * L + l0:t * L + l0 + UC]
+            Ik = lambda k: T.Ib[:, 16 * l0 + k * UC:16 * l0 + (k + 1) * UC]
+            scale(UC, UC, T.yb[:, l0:l0 + UC], Rk(0), 0.25, YB - 0.484375, RT, ["yb%s.%d" % (s, h)], RB)
+            if t < RO - 1:
+                scale(UC, UC, T.ez[:, l0:l0 + UC], Rk(0), 0.0625, WB - 1 + 1.0 / 256, RT, ["ez%s.%d" % (s, h)], RB)
+            if onS:
+                it = "I%s.%d." % (s, h)
+                vop(UC, RT + ["st%d" % min(t, 1)], [it + "a"], lambda: V.tensor_tensor(T.i0[:, l0:l0 + UC], Rk(0), stv, A.is_ge), RB)
+                sop(16 * UC, RT, [it + "0", it + "8"], lambda: S.activation(T.Ib[:, 16 * l0:16 * (l0 + UC)], T.R[:, u0 * 1024:u0 * 1024 + 16 * UC],
+                                                                         F.Sign, bias=0.0625), RB)
+                mm(B(0, h), [(sel(T.Sel, 0), T.i0[:, l0:l0 + UC])] + [(sel(T.Sel, k), T.Ib[:, 16 * l0 + k:16 * (l0 + UC):16]) for k in range(1, 16)],
+                   ["Sel", it + "a", it + "0"], [tk(0)], bank, n=UC)
+                return
+            for kq in range(0, 16, KQ):
+                it = "I%s.%d.%d" % (s, h, kq)
+                vops(KQ, UC, RT + ["st%d" % min(t, 1)], [it],
+                     lambda e, kq=kq: [V.tensor_tensor(Ik(k), Rk(k), stv, A.is_ge) for k in range(kq, kq + KQ)], RB)
+                mm(B(0, h), [(sel(T.Sel, k), Ik(k)) for k in range(kq, kq + KQ)], ["Sel", it], [tk(0)], bank, kq == 0, kq + KQ == 16, n=UC)
+        for h in range(NH):
+            judge(h)
+        sop(CL, [tk(0), "c.sE", "c.bE"], ["pw" + s],
+            lambda: S.activation(m(T.pw), B(0), F.Exp, bias=C("bE") if onS else -64.0, scale=C("sE") if onS else 8.0), [bank])
+        mm(B(1), [(Kb("Bm"), m(T.pw))], ["b.Bm", "pw" + s], [tk(1)], bank)
+        sop(CL, [tk(1), "c.thr"], ["sg" + s], lambda: S.activation(m(T.sg), B(1), F.Sign, bias=C("thr")), [bank])
+        sg, cn = m(T.sg), m(T.cn)
+        mm(B(2), [(Kb("OH"), sg), (cr["OH"], one1)], ["b.OH", "r.OH", "b.one", "sg" + s], [tk(2)], bank)
+        kB = T.BS[:, 464 + NB * c:464 + NB * (c + 1)]
+        mm(kB, [(sel(T.SelK, r), T.sg[:, c * CL + r:(c + 1) * CL:16]) for r in range(16)] + [(Kb("ID"), T.ln16b[:, 0:NB])],
+           ["SelK", "b.ID", "ln16b", "sg" + s], ["s.kB" + s], 7, n=NB)
+        mm(B(0), [(Kb("Ld"), sg), (cr["Ld"], one1)], ["b.Ld", "r.Ld", "b.one", "sg" + s], [tk(0)], bank)
+        mm(B(3), [(Kb("Vu"), sg)], ["b.Vu", "sg" + s], [tk(3)], bank)
+        mi = t * NC + c
+        mt = "msg%d" % mi
+        ohc = mcl(T.msg, mi)
+        vop(CL, [tk(2), "cn" + s], [mt + "a"], lambda: V.tensor_tensor(ohc, cn, B(2), A.mult), [bank])
+        ov = T.offv[:, NB * c:NB * (c + 1)]
+        vop(NB, ["s.kB" + s], ["offv" + s], lambda: V.tensor_scalar(ov, kB, 4104.0, float(CE), A.add, A.min), [7])
+        win = T.P[:, c * PW:(c + 1) * PW].indirect(ov)
+        op({"V": (50, CL, 0, 0, 1, 0), "S": (65, CL, 0, 0, 1, 0)}, ["offv" + s, "Pz"] + ["P%s.%d" % (s, q) for q in range(GP)], [mt + "b"],
+           lambda e: [V.tensor_copy(mcl(T.msgv, mi), win) if e == "V" else S.activation(mcl(T.msgv, mi), win, F.Copy)])
+        dst = T.cores[(rank + 1 + t % (N - 1)) % N]
+        src = T.cores[(rank - 1 - t % (N - 1)) % N]
+        rid, pid = topo.addr(dst)[0], topo.addr(dst)[1]
+        for x, out, in_ in (("a", T.land, T.msg), ("b", T.landv, T.msgv)):
+            sem = "arr%d%s" % (mi, x)
+            op({"G": (0, 0, 0, 0, 0, 0.3)}, [mt + x], ["land%d%s" % (mi, x)],
+               lambda e, out=out, in_=in_, sem=sem: [g.remote_dma(mcl(out, mi), mcl(in_, mi), T.sem[sem], T.sem.sent, pid, rid, topo.mask(core, dst))],
+               lat="far", sem=(sem, len(topo.engines(src, core))))
+            ops[-1]["sent"] = len(topo.engines(core, dst))
+        vop(CL, [tk(0), "odd" + s], ["nmd" + s], lambda: V.tensor_tensor(m(T.nmd), m(T.odd), B(0), A.is_lt), [bank])
+        sop(CL, [tk(3), "c.bVu"], ["mu" + s, "cnt" + s],
+            lambda: S.activation(m(T.mu), B(3), F.Relu, bias=C("bVu"), accum_out=T.cnt[:, c:c + 1]), [bank])
+        mm(B(1), [(Kh("BO"), ohc), (cr["e32"], one1)], ["h.BO", "r.e32", "b.one", mt + "a"], [tk(1)], bank)
+        vop(CL, [tk(1), "uu" + s], ["fa" + s], lambda: V.tensor_tensor(m(T.fa), m(T.uu), B(1), A.mult), [bank])
+        vop(CL, ["fa" + s], ["fb" + s], lambda: V.tensor_scalar(m(T.fb), m(T.fa), 5, 4095, A.arith_shift_right, A.bitwise_and))
+        vop(CL, ["fb" + s], ["fr" + s], lambda: V.tensor_scalar(m(T.fr), m(T.fb), -2048.0, None, A.add))
+        mm(B(0), [(Kh("ID"), cn), (Kb("KI"), m(T.nmd)), (Kb("nKI"), m(T.mu))],
+           ["h.ID", "b.KI", "b.nKI", "cn" + s, "nmd" + s, "mu" + s], [tk(0)], bank)
+        mm(B(2), [(Kh("SD"), cn), (Kh("R0"), ohc), (Kb("nKI"), m(T.nmd))],
+           ["h.SD", "h.R0", "b.nKI", "cn" + s, "nmd" + s, mt + "a"], [tk(2)], bank)
+        mm(B(3), [(Kh("SU"), cn), (Kb("KI"), m(T.mu)), (cr["Tu"], one1), (Kh("R15"), m(T.fr))],
+           ["h.SU", "h.R15", "b.KI", "r.Tu", "b.one", "cn" + s, "mu" + s, "fr" + s], [tk(3)], bank)
+        select(c, -4096.0, T.cn, "cn" + s)
+
+    def phase_q(t, c):
+        B, tk, bank = tiles(c)
+        s = str(c)
+        m = lambda buf: mcl(buf, c)
+        mi = t * NC + c
+        lt, lw = "land%da" % mi, "land%db" % mi
+        le, lv = mcl(T.land, mi), mcl(T.landv, mi)
+        mm(B(1), [(Kh("BO"), le), (cr["e32"], one1)], ["h.BO", "r.e32", "b.one", lt], [tk(1)], bank)
+        mm(B(2), [(Kh("BO3"), le), (cr["L2"], one1)], ["h.BO3", "r.L2", "b.one", lt], [tk(2)], bank)
+        vop(CL, ["cn" + s, tk(1)], ["L2" + s], lambda: V.tensor_tensor(m(T.L2), m(T.cn), B(1), A.mult), [bank])
+        index(c, B(2), tk(2), bank, T.L2, "L2" + s, T.off2, "off2" + s)
+        gather(t, T.x2, c * CE, T.off2, c, "x2" + s, "off2" + s)
+
+        def near(h):
+            l0 = c * CL + h * UC
+            xt = ["x2%s.%d" % (s, q) for q in range(h * UC // GL, (h + 1) * UC // GL)]
+            xk = lambda k: T.x2[:, 16 * l0 + k:16 * (l0 + UC):16]
+            mk = lambda k: T.mx[:, 16 * l0 + k * UC:16 * l0 + (k + 1) * UC]
+            vv = T.landv[:, mi * CL + h * UC:mi * CL + (h + 1) * UC]
+            if c in ABS_S:
+                u0 = (c * NU) % 2 + h * UC // 64
+                RB = list(range(2 * u0, 2 * u0 + UC // 32))
+                RT = ["R%d" % (u0 + i) for i in range(UC // 64)]
+                dk = lambda k: T.R[:, u0 * 1024 + k * UC:u0 * 1024 + (k + 1) * UC]
+                top(32, 32 * UC, ["b.ID", "b.nID", lw] + xt, RT,
+                    lambda e: [x for k in range(16) for x in (Pm.matmul(dk(k), Kb("ID"), xk(k), True, False),
+                                                              Pm.matmul(dk(k), Kb("nID"), vv, False, True))], RB)
+                it = ["mx%s.%d.%d" % (s, h, kq) for kq in range(0, 16, KQ)]
+                sop(16 * UC, RT, it, lambda: S.activation(T.mx[:, 16 * l0:16 * (l0 + UC)], T.R[:, u0 * 1024:u0 * 1024 + 16 * UC], F.Abs, scale=0.5), RB)
+                mm(B(0, h), [(E8, T.thS[0:8, l0:l0 + UC])] + [(sel(T.SelN, k), mk(k)) for k in range(16)],
+                   ["b.E8", "th", "SelN"] + it, [tk(0)], bank, n=UC)
+                return
+            vi = (c * NH + h) % (192 // UC)
+            vh, vt = T.BS[:, L + vi * UC:L + (vi + 1) * UC], "s.vP%d" % vi
+            mm(vh, [(Kb("ID"), vv)], ["b.ID", lw], [vt], 7, n=UC)
+            mm(B(0, h), [(E8, T.thS[0:8, l0:l0 + UC]), (Kb("BO"), vv)] + [(sel(T.Sel, k), xk(k)) for k in range(16)],
+               ["b.E8", "th", "b.BO", lw, "Sel"] + xt, [tk(0)], bank, True, False, n=UC)
+            for kq in range(0, 16, KQ):
+                it = "mx%s.%d.%d" % (s, h, kq)
+                vops(KQ, UC, xt + [vt], [it], lambda e, kq=kq: [V.tensor_tensor(mk(k), xk(k), vh, A.max) for k in range(kq, kq + KQ)], [7])
+                mm(B(0, h), [(sel(T.SelN, k), mk(k)) for k in range(kq, kq + KQ)], ["SelN", it], [tk(0)], bank, False, kq + KQ == 16, n=UC)
+        for h in range(NH):
+            near(h)
+        sop(CL, [tk(0)], ["eta" + s], lambda: S.activation(m(T.eta), B(0), F.Sign, bias=0.5), [bank])
+        mm(B(1), [(Kb("Qm"), m(T.eta)), (Kb("BOs"), lv)], ["b.Qm", "b.BOs", "eta" + s, lw], [tk(1)], bank)
+        sop(CL, [tk(1), "c.bQ"], ["qq" + s], lambda: S.activation(m(T.qq), B(1), F.Sign, bias=C("bQ")), [bank])
+        cn, qq = m(T.cn), m(T.qq)
+        z = "L" if t == RO - 1 else ""
+        mm(B(0), [(Kh("ID"), cn), (Kb("nKI"), qq)], ["h.ID", "b.nKI", "cn" + s, "qq" + s], [tk(0)], bank)
+        mm(B(2), [(Kh("SD"), cn), (cr["Td" + z], one1), (Kb("KSD"), qq)], ["h.SD", "b.KSD", "r.Td" + z, "b.one", "cn" + s, "qq" + s], [tk(2)], bank)
+        mm(B(3), [(Kh("BO"), le), (cr["Te" + z], one1), (Kb("KIS"), qq)], ["h.BO", "b.KIS", "r.Te" + z, "b.one", lt, "qq" + s], [tk(3)], bank)
+        if z:
+            select(c, -2048.0, T.ycS, "yc" + s)
+            dma("Y", mcl(T.yc, c), m(T.ycS), ["yc" + s], ["o.yc" + s], "oc" + s, 2.0)
+        else:
+            select(c, -4096.0, T.cn, "cn" + s)
+
+    def scatter(t, to):
+        X, xt = XX[to]
+        p = t % 2
+        vop(0, ["nx%d" % p, "offr%d" % p], xt,
+            lambda: V.tensor_copy(X[:, 0:W].indirect(T.offr[:, 16 * p:16 * p + 16]), T.nx[:, p * L:(p + 1) * L]), sc=L)
+
+    for t in range(RO):
+        p = t % 2
+        if t < RO - 1:
+            mm(T.BS[:, 448:464], [(sel(T.SelW, r), T.yb[:, r:L:16]) for r in range(16)], ["SelW"] + parts("yb"), ["s.uB"], 7, n=16)
+            vop(16, ["s.uB", "c.cU"], ["ra"], lambda: V.tensor_scalar(T.ra[:, :], T.BS[:, 448:464], C("cU"), None, A.add), [7])
+            vop(16, ["ra"], ["rb"], lambda: V.tensor_scalar(T.rb[:, :], T.ra[:, :], 31, None, A.bitwise_and))
+            vop(32, ["rb", "ln32c"], ["rc"], lambda: V.tensor_tensor(T.rc[:, :], T.rb[:, :], T.ln32c[:, :], A.add))
+            vop(16, ["rc"], ["offr%d" % p], lambda p=p: V.tensor_copy(T.offr[:, 16 * p:16 * p + 16], T.rc[:, :]))
+        for c in range(NC):
+            phase_p(t, c)
+        if t == RO - 1:
+            scale(L // 2, L, T.yyS[:, :], T.yb[:, :], 1.0, -YB, parts("yb"), ["yy"])
+            dma("Y", T.yy[:, :], T.yyS[:, :], ["yy"], ["o.yy"], "oy", 2.0)
+        else:
+            mm(T.BS[:, 480:480 + NC], [(K("A32"), T.cnt[:, :])], ["k.A32"] + every("cnt"), ["s.cU"], 7, n=256)
+            vop(1, ["s.cU"], ["cs"], lambda: V.tensor_reduce(T.cs[:, :], T.BS[:, 480:480 + NC], AxisListType.X, A.add), [7])
+            scale(1, 1, C("cA"), T.cs[:, :], 1.0, -262144.0, ["cs"], ["c.cA"])
+            vop(0, XX[p][1] + ["offr%d" % p] + parts("ez"), ["Wn"],
+                lambda p=p: V.tensor_tensor(T.Wn[:, :], XX[p][0][:, 0:W].indirect(T.offr[:, 16 * p:16 * p + 16]), T.ez[:, :], A.add), ga=L)
+            scale(L // 2, L, T.nx[:, p * L:(p + 1) * L], T.Wn[:, :], 0.5, -WB / 2, ["Wn"], ["nx%d" % p])
+            if TWO:
+                if t > 0:
+                    scatter(t - 1, 1 - p)
+                scatter(t, 1 - p)
+        for c in range(NC):
+            phase_q(t, c)
+        if not TWO and t < RO - 1:
+            scatter(t, 0)
+    return ops
+
+
+def depend(ops):
+    lastw, readers, deps = {}, {}, []
+    for i, o in enumerate(ops):
+        d = set()
+        for k in o["rd"] + o["wr"]:
+            if k in lastw:
+                d.add(lastw[k])
+        for k in o["wr"]:
+            d.update(readers.get(k, ()))
+        d.discard(i)
+        deps.append(sorted(d))
+        for k in o["rd"]:
+            readers.setdefault(k, []).append(i)
+        for k in o["wr"]:
+            lastw[k] = i
+            readers[k] = []
+    return deps
+
+
+def way(o, P):
+    return P["far"] if o["lat"] == "far" else o["lat"] + (0.06 if o["eng"] == "T" else 0.0)
+
+
+def lay(ops, deps, succ, pri, pick, hold, P):
+    n = len(ops)
+    lat = P["lat"]
+    left = [len(deps[i]) + len(ops[i]["soft"]) for i in range(n)]
+    t0 = [0.0] * n
+    ready = [i for i in range(n) if not left[i]]
+    free = {e: 0.0 for e in "VSTGY"}
+    bank = [("", 0.0)] * 8
+    opened = set()
+    order, start = [], [0.0] * n
+    while ready:
+        cand = []
+        for i in ready:
+            o, e = ops[i], pick[i]
+            if o["grp"] & 1 and o["banks"][0] in opened:
+                continue
+            t1 = max(t0[i] + hold[i], free[e])
+            for b in o["banks"]:
+                if bank[b][0] != e and bank[b][1] + lat > t1:
+                    t1 = bank[b][1] + lat
+            cand.append((t1, i))
+        tm = min(cand)[0] + 0.05
+        t1, i = max((c for c in cand if c[0] <= tm), key=lambda c: pri[c[1]])
+        o, e = ops[i], pick[i]
+        start[i] = t1
+        free[e] = t1 + cost(o, e, P)
+        for b in o["banks"]:
+            bank[b] = (e, free[e])
+        if o["grp"] == 1:
+            opened.add(o["banks"][0])
+        if o["grp"] == 2:
+            opened.discard(o["banks"][0])
+        order.append(i)
+        ready.remove(i)
+        f = free[e] + way(o, P)
+        for j, hard in succ[i]:
+            if hard:
+                t0[j] = max(t0[j], f + (0.0 if e == "T" and pick[j] == "T" else lat))
+            left[j] -= 1
+            if not left[j]:
+                ready.append(j)
+    return order, start
+
+
+def replay(ops, deps, order, pick, P):
+    free = {e: (0.0, -1) for e in "VSTGY"}
+    bank = [("", 0.0, -1)] * 8
+    fin = [0.0] * len(ops)
+    why = [(-1, False)] * len(ops)
+    lat = P["lat"]
+    for i in order:
+        o, e = ops[i], pick[i]
+        t, w = free[e]
+        w = (w, True)
+        for b in o["banks"]:
+            if bank[b][0] != e and bank[b][1] + lat > t:
+                t, w = bank[b][1] + lat, (bank[b][2], True)
+        for d in deps[i]:
+            x = fin[d] + (0.0 if e == "T" and pick[d] == "T" else lat)
+            if x >= t:
+                t, w = x, (d, False)
+        why[i] = w
+        t += cost(o, e, P)
+        free[e] = (t, i)
+        for b in o["banks"]:
+            bank[b] = (e, t, i)
+        fin[i] = t + way(o, P)
+    end = max(fin)
+    i, pairs = fin.index(end), []
+    while why[i][0] >= 0:
+        if why[i][1]:
+            pairs.append((i, why[i][0]))
+        i = why[i][0]
+    return end, pairs
+
+
+def plan(ops, deps, tries=TRIES):
+    n = len(ops)
+    succ = [[] for _ in range(n)]
+    for i in range(n):
+        for d in deps[i]:
+            succ[d].append((i, True))
+        for d in ops[i]["soft"]:
+            succ[d].append((i, False))
+    free = [i for i in range(n) if len(ops[i]["eng"]) > 1]
+    seed = [12345]
+
+    def rnd():
+        seed[0] = (seed[0] * 1103515245 + 12345) % 2147483648
+        return seed[0] / 2147483648.0
+
+    def score(pick, noise, hold):
+        pri = [0.0] * n
+        for i in range(n - 1, -1, -1):
+            pri[i] = cost(ops[i], pick[i], FIG) + way(ops[i], FIG) + max([pri[j] + FIG["lat"] for j, h in succ[i]], default=0.0)
+        order, start = lay(ops, deps, succ, [pri[i] + noise[i] for i in range(n)], pick, hold, FIG)
+        res = [replay(ops, deps, order, pick, P) for P in FIGS]
+        return sum(r[0] for r in res) / len(FIGS), order, start, [b for r in res for b in r[1]]
+    pick = [o["eng"][-1] if "PTp" not in o["rd"] else "V" for o in ops]
+    noise, hold = [EARLY if o["wr"][0][:2] in ("k.", "b.", "h.", "c.", "r.", "Se", "ln") else 0.0 for o in ops], [0.0] * n
+    cur = best = score(pick, noise, hold) + (pick,)
+    for it in range(tries):
+        p2, n2, h2 = list(pick), list(noise), list(hold)
+        for r in range(1 + int(rnd() * 2)):
+            x = rnd()
+            i, j = cur[3][int(rnd() * len(cur[3]))]
+            if x < 0.3:
+                c = [k for k in (i, j) if len(ops[k]["eng"]) > 1] or [free[int(rnd() * len(free))]]
+                k = c[int(rnd() * len(c))]
+                p2[k] = "V" if p2[k] == "S" else "S"
+            elif x < 0.55:
+                h2[j] += rnd() * 0.8
+            elif x < 0.75:
+                n2[i] += rnd() * 4
+                n2[j] -= rnd() * 4
+            elif x < 0.85:
+                k = free[int(rnd() * len(free))]
+                p2[k] = "V" if p2[k] == "S" else "S"
+            elif x < 0.92:
+                k = int(rnd() * n)
+                h2[k] = n2[k] = 0.0
+            else:
+                a, d = int(rnd() * n), (rnd() - 0.5) * 8
+                for k in range(a, min(n, a + int(rnd() * 60))):
+                    n2[k] += d
+        s2 = score(p2, n2, h2)
+        if s2[0] <= cur[0] + 0.6 * rnd() * rnd() * (1 - it / tries):
+            cur, pick, noise, hold = s2 + (p2,), p2, n2, h2
+            if cur[0] < best[0]:
+                best = cur
+    return best[1], best[4], best[2], best[0]
+
+
+PLAN = {}
+
+
+def rank_program(g, core, T, topo):
+    rank = T.rank_of(core)
+    if rank is None:
+        return
+    ops = build(g, T, topo, core, rank)
+    deps = depend(ops)
+    if "p" not in PLAN:
+        PLAN["p"] = plan(ops, deps)
+    order, eng = PLAN["p"][0], PLAN["p"][1]
+    Q = {"V": g.vector, "S": g.scalar, "T": g.tensor, "G": g, "Y": g.sync}
+    count = {"sV": 0, "sS": 0, "sT": 0, "sG": 0, "sent": 0}
+    known = {e: {} for e in Q}
+    mark, clock = {}, {}
+    lastb = {}
+    for i in order:
+        o, e = ops[i], eng[i]
+        need = set(deps[i])
+        for b in o["banks"]:
+            if b in lastb and eng[lastb[b]] != e:
+                need.add(lastb[b])
+            lastb[b] = i
+        kn = known[e]
+        for d in sorted(need, key=lambda d: -clock[d]["#"]):
+            if e == "T" and eng[d] == "T":
+                continue
+            sem, val = mark[d]
+            if kn.get(sem, 0) >= val:
+                continue
+            Q[e].wait_ge(T.sem[sem], val)
+            for k, v in clock[d].items():
+                if k != "#" and kn.get(k, 0) < v:
+                    kn[k] = v
+        ins = o["fn"](e)
+        if o["sem"] is None:
+            sem = "s" + e
+            for x in ins:
+                x.then_inc(T.sem[sem], 1)
+            count[sem] += len(ins)
+            mark[i] = (sem, count[sem])
+        else:
+            mark[i] = o["sem"]
+            count[o["sem"][0]] = o["sem"][1]
+            if "sent" in o:
+                count["sent"] += o["sent"]
+            else:
+                ins[0].then_inc(T.sem[o["sem"][0]], 16)
+        ck = {} if "sent" in o else dict(kn)
+        ck[mark[i][0]] = mark[i][1]
+        ck["#"] = len(clock)
+        clock[i] = ck
+    for sem, val in count.items():
+        if val:
+            g.wait_ge(T.sem[sem], val)

@@ -11,6 +11,8 @@ NB = CL // 16
 UC = 64
 NH = CL // UC
 KQ = 8
+SIDE = (0, 0, 0, 0)
+QS = 32768.0
 TWO = False
 CMP_S = ()
 ABS_S = ()
@@ -23,21 +25,22 @@ SCRATCH = {n: ("sbuf", [128, w], d) for n, w, d in [
     ("PTs", 16 * L, bf), ("Ib", 16 * L, bf), ("x2", 16 * L, bf), ("mx", 16 * L, bf),
     ("ui", L, i32), ("uu", L, i32), ("odd", L, i32), ("Ls", L, f32), ("L2", L, f32), ("va", L, i32), ("vb", L, i32),
     ("off1", L, u16), ("off2", L, u16), ("offv", 16, u16), ("offr", 32, u16),
-    ("pw", L, bf), ("sg", L, bf), ("nmd", L, bf), ("mu", L, bf), ("fa", L, i32), ("fb", L, i32), ("fr", L, f16),
+    ("pw", L, bf), ("sg", L, bf), ("nmd", L, bf), ("mu", L, bf), ("fa", L, i32), ("fb", L, i32), ("Ms", L, f32),
     ("ts", L, f32), ("zz", L, f32), ("eta", L, bf), ("qq", L, bf), ("ez", L, f32), ("Wn", L, bf), ("nx", 2 * L, bf),
     ("ra", 16, i32), ("rb", 16, i32), ("rc", 16, i32), ("cnt", NC, f32), ("cs", 1, f32), ("col", 32, f32),
     ("msg", RO * L, f16), ("land", RO * L, f16), ("msgv", RO * L, bf), ("landv", RO * L, bf),
     ("k32", 13 * 128, f32), ("kb", 17 * 128, bf), ("kh", 7 * 128, f16), ("SelL", CE, bf), ("stT", NC * 128, bf), ("i0", L, bf),
     ("Sel", 144, bf), ("SelN", 144, bf), ("SelK", 144, bf), ("SelW", 144, bf),
-    ("crow", 9 * 128, bf), ("ln16", 16, f32), ("ln16b", 16, bf), ("ln32", 16, f32), ("ln32c", 16, f32)]}
+    ("crow", 11 * 128, bf), ("rQ", 128, bf), ("rQi", 128, f32), ("ln16", 16, f32), ("ln16b", 16, bf), ("ln32", 16, f32), ("ln32c", 16, f32)]}
 SCRATCH.update({"R": ("psum", [128, 2048], f32), "PTp": ("psum", [128, 1024], bf),
-                "B0": ("psum", [128, 512], f32), "B1": ("psum", [128, 512], f32), "BS": ("psum", [128, 512], f32)})
+                "B0": ("psum", [128, 512], f32), "B1": ("psum", [128, 512], f32), "PTq": ("psum", [128, 1024], bf)})
 SEMAPHORES = (["sV", "sS", "sT", "sG", "sent", "dX0", "dX1", "dXB", "dc", "dst0", "dst1", "dy", "dw", "dth", "oy"]
               + ["oc%d" % c for c in range(NC)] + ["arr%d%s" % (i, x) for i in range(RO * NC) for x in "ab"])
 
-FIG = dict(cy=0.00100, ga=1.56, sc=3.8, pe=0.00050, lat=0.12, ov=0.02, far=3.0)
-FIGS = [FIG, dict(FIG, ga=1.1, sc=2.0, lat=0.08, far=2.5), dict(FIG, ga=2.0, sc=5.5, lat=0.2, far=5.0), dict(FIG, pe=0.0007, ov=0.05)]
-TRIES = 1500
+FIG = dict(cy=0.00083, ga=1.56, sc=3.8, pe=0.00042, lat=0.18, ov=0.005, far=3.0)
+FIGS = [FIG, dict(FIG, lat=0.08, ov=0.025), dict(FIG, cy=0.0011, pe=0.00055, ga=1.2, sc=2.5, lat=0.15, ov=0.01, far=4.0),
+        dict(FIG, cy=0.0011, pe=0.00055, ga=1.9, sc=5.0, far=4.0)]
+TRIES, SWAPS, HEAT = 400, 5000, 0.3
 EARLY = 40.0
 
 
@@ -51,6 +54,8 @@ def build(g, T, topo, core, rank):
     V, S, Pm = g.vector, g.scalar, g.tensor
 
     def op(c, rd, wr, fn, banks=(), lat=0.0, sem=None, grp=0):
+        if list(banks) == [5]:
+            banks = sorted(set(5 + (int(k[1]) + SIDE[int(k[3])]) % 2 for k in list(rd) + list(wr) if k[0] == "B"))
         ops.append(dict(eng="".join(c), c=c, rd=list(rd), wr=list(wr), fn=fn, banks=list(banks), lat=lat, sem=sem, grp=grp, soft=[]))
 
     def vop(n, rd, wr, fn, banks=(), ga=0, sc=0):
@@ -160,7 +165,7 @@ def build(g, T, topo, core, rank):
     vop(1, ["c.r0", "c.r15"], ["c.s"], lambda: V.tensor_tensor(C("s"), C("r0"), C("r15"), A.add))
     vop(1, ["c.r0", "c.r15"], ["c.dLd"], lambda: V.tensor_tensor(C("dLd"), C("r15"), C("r0"), A.subtract))
     for out, in_, a, b in (("mid", "s", -0.5, 0.5), ("c0", "r0", -101.0, 1.0), ("hVu", "s", -0.5, 0.0), ("kw", "s", 2048.5, -0.5),
-                           ("thr", "r15", -54.6, 0.0), ("bVu", "dLd", 0.5, -0.5), ("bQ", "n", -8.5, 120.0), ("j16", "n", -16.0, 240.0),
+                           ("thr", "r15", -54.6, 0.0), ("bVu", "dLd", 0.5, -0.5), ("j16", "n", -16.0, 240.0),
                            ("j32", "n", -32.0, 480.0), ("a32", "r15", 32.0, 0.0), ("sE", "r0", 4.0, 4.0), ("bE", "r0", -64.0, 0.0)):
         cts(out, in_, a, b, A.mult, A.add)
     for nm, in_, by in (("ID", "ID", 1.0), ("KI", "ID", 4096.0), ("nKI", "ID", -4096.0), ("KSD", "SD", 4096.0)):
@@ -184,10 +189,10 @@ def build(g, T, topo, core, rank):
     sc(Kb("KIS"), "b.KIS", "t0", 4096.0)
     inblock(Kb("Ld"), "b.Ld", "SD", "mid", "dLd", "t4")
     inblock(Kb("Vu"), "b.Vu", "ID", "mid", "hVu", "t2")
-    inblock(Kb("Qm"), "b.Qm", "LT", 8.5, -0.5, "t4")
+    inblock(Kb("Qm"), "b.Qm", "LT", -8.5 * QS, 0.5 * QS, "t4")
     for nm in ("ID", "SD", "SU", "BO"):
         vop(128, ["k." + nm], ["h." + nm], lambda nm=nm: V.tensor_copy(Kh(nm), K(nm)))
-    sc(Kb("BOs"), "b.BOs", "BO", -1.0 / 1024)
+    sc(Kb("BOs"), "b.BOs", "BO", QS / 1024)
     sc(Kb("BO"), "b.BO", "BO", 1.0)
     if ABS_S:
         sc(Kb("nID"), "b.nID", "ID", -1.0)
@@ -198,7 +203,10 @@ def build(g, T, topo, core, rank):
     vop(128, ["k.BO"], ["h.BO3"], lambda: V.tensor_scalar(Kh("BO3"), K("BO"), 3232.0, None, A.mult))
     vop(128, ["k.BO"], ["h.R0"], lambda: V.tensor_scalar(Kh("R0"), K("BO"), 0.0, None, A.mult))
     vop(8, ["k.BO"], ["h.R0"], lambda: V.tensor_copy(T.kh[:, kh["R0"] * 128:(kh["R0"] + 1) * 128:16], K8("BO")))
-    vop(128, ["k.ID", "c.r15"], ["h.R15"], lambda: V.tensor_scalar(Kh("R15"), K("ID"), C("r15"), None, A.mult))
+    vop(128, ["k.BO"], ["h.R15"], lambda: V.tensor_scalar(Kh("R15"), K("BO"), 0.0, None, A.mult))
+    vop(8, ["k.BO"], ["h.R15"], lambda: V.tensor_copy(T.kh[:, kh["R15"] * 128 + 15:(kh["R15"] + 1) * 128:16], K8("BO")))
+    gop(128, [], ["r.Qi"], lambda: g.iota(T.rQi[0:1, :], [[0, 8], [17, 16]], -15, 0, allow_small_or_imprecise_dtypes=True))
+    scale(128, 128, T.rQ[0:1, :], T.rQi[0:1, :], -QS / 2, 0.0, ["r.Qi"], ["r.Q"])
     sel = lambda buf, k: buf[:, 16 - k:144 - k]
     vop(72, [], ["Sel"], lambda: V.memset(T.Sel[:, :], 0.0))
     scale(8, 8, T.Sel[:, 16:144:16], K8("BO"), 1.0, 0.0, ["k.BO"], ["Sel"])
@@ -207,7 +215,7 @@ def build(g, T, topo, core, rank):
     scale(72, 144, T.SelN[:, :], T.Sel[:, :], -2.0, 0.0, ["Sel"], ["SelN"])
     scale(16, 16, T.ln16b[:, 0:8], T.ln16[:, 0:8], 1.0, C("j16"), ["ln16", "c.j16"], ["ln16b"])
     scale(16, 16, T.ln32c[:, :], T.ln32[:, :], 1.0, C("j32"), ["ln32", "c.j32"], ["ln32c"])
-    rows = [("OH", 0.0, {1: 0.5, 15: 0.5}), ("Ld", 2.5, {0: 2.0, 1: 2.0}), ("e32", 2080.0, {}), ("Tu", -4096.0, {}), ("L2", 1441792.0, {}),
+    rows = [("OH", 0.0, {1: 0.5, 15: 0.5}), ("Ld", 2.5, {0: 2.0, 1: 2.0}), ("e32", 2080.0, {}), ("Tu", -4096.0, {15: -6144.0}), ("Ts", -4096.0, {}), ("e15", 0.0, {15: 2080.0}), ("L2", 1441792.0, {}),
             ("Td", -4096.0, {0: -8192.0}), ("Te", -8192.0, {0: -4096.0}), ("TdL", -2048.0, {0: -6144.0}), ("TeL", -6144.0, {0: -2048.0})]
     cr = {}
     for i, (nm, val, ex) in enumerate(rows):
@@ -224,8 +232,8 @@ def build(g, T, topo, core, rank):
 
     vop(L, ["cin"], every("cn"), lambda: V.tensor_scalar(T.cn[:, :], T.cin[:, :], -2048.0, None, A.add))
     scale(L // 2, L, T.yb[:, :], T.yin[:, :], 1.0, YB, ["yin"], parts("yb"))
-    mm(T.BS[:, 480:482], [(Kb("Wm"), T.kb[:, kb["one"] * 128:kb["one"] * 128 + 2])], ["b.Wm", "b.one"], ["s.cU"], 7, n=2)
-    scale(1, 1, C("cU"), T.BS[:, 480:481], -YB, 0.0, ["s.cU"], ["c.cU"], [7])
+    mm(T.R[:, 0:2], [(Kb("Wm"), T.kb[:, kb["one"] * 128:kb["one"] * 128 + 2])], ["b.Wm", "b.one"], ["R0"], 0, n=2)
+    scale(1, 1, C("cU"), T.R[:, 0:1], -YB, 0.0, ["R0"], ["c.cU"], [0])
 
     def gather(t, out_buf, base, off, c, otok, ftok):
         X, xt = XX[t % 2]
@@ -242,30 +250,35 @@ def build(g, T, topo, core, rank):
         vop(CL, ["vb%d" % c], [otok], lambda: V.tensor_copy(mcl(off, c), mcl(T.vb, c)))
 
     def tiles(c):
-        Bk = (T.B0, T.B1)[c % 2]
-        o = (c // 2) * 4 * CL
-        return ((lambda i, h=None: Bk[:, o + i * CL:o + (i + 1) * CL] if h is None else Bk[:, o + i * CL + h * UC:o + i * CL + (h + 1) * UC]),
-                (lambda i: "B%d.%d" % (c, i)), 5 + c % 2)
+        def B(i, h=None):
+            Bk, o = (T.B0, T.B1)[(c + SIDE[i]) % 2], ((c // 2) * 4 + i) * CL
+            return Bk[:, o:o + CL] if h is None else Bk[:, o + h * UC:o + (h + 1) * UC]
+        return B, (lambda i: "B%d.%d" % (c, i)), 5
 
-    def select(c, bias, out, otok):
+    def select(c, a, b, out, otok):
         B, tk, bank = tiles(c)
-        sop(CL, [tk(0)], ["ts%d" % c], lambda: S.activation(mcl(T.ts, c), B(0), F.Identity, bias=bias), [bank])
-        vop(CL, [tk(2), "ts%d" % c], ["zz%d" % c], lambda: V.tensor_tensor(mcl(T.zz, c), mcl(T.ts, c), B(2), A.max), [bank])
-        vop(CL, [tk(3), "zz%d" % c], [otok], lambda: V.tensor_tensor(mcl(out, c), mcl(T.zz, c), B(3), A.max), [bank])
+        vop(CL, [tk(a), "ts%d" % c], ["zz%d" % c], lambda: V.tensor_tensor(mcl(T.zz, c), mcl(T.ts, c), B(a), A.max), [bank])
+        vop(CL, [tk(b), "zz%d" % c], [otok], lambda: V.tensor_tensor(mcl(out, c), mcl(T.zz, c), B(b), A.max), [bank])
+
+    def engines(a):
+        to = [T.cores[(T.rank_of(a) + 1 + t % (N - 1)) % N] for t in range(RO)]
+        return [q for q in topo.engines(a, to[0]) if all(q in topo.engines(a, b) for b in to)]
 
     def phase_p(t, c):
         B, tk, bank = tiles(c)
         s = str(c)
         m = lambda buf: mcl(buf, c)
-        M = m(T.BS)
-        mm(M, [(Kb("Wm"), m(T.yb))], ["b.Wm"] + parts("yb", [c]), ["s.M" + s], 7)
-        vop(CL, ["s.M" + s, "c.cU"], ["ui" + s], lambda: V.tensor_scalar(m(T.ui), M, C("cU"), None, A.add), [7])
-        vop(CL, ["ui" + s], ["uu" + s], lambda: V.tensor_scalar(m(T.uu), m(T.ui), 2047, None, A.bitwise_and))
-        vop(CL, ["uu" + s], ["s.M" + s], lambda: V.tensor_scalar(M, m(T.uu), 2.0, 33.0, A.mult, A.add), [7])
-        sop(CL, ["s.M" + s, "c.cA"], ["Ls" + s], lambda: S.activation(m(T.Ls), M, F.Identity, bias=C("cA"), scale=2048.0), [7])
-        vop(CL, ["ui" + s], ["odd" + s], lambda: V.tensor_scalar(m(T.odd), m(T.ui), 1, None, A.bitwise_and))
-        vop(CL, ["cn" + s, "s.M" + s], ["s.M" + s], lambda: V.tensor_tensor(M, m(T.cn), M, A.mult), [7])
-        index(c, M, "s.M" + s, 7, T.Ls, "Ls" + s, T.off1, "off1" + s)
+        def numbers():
+            mm(B(1), [(Kb("Wm"), m(T.yb))], ["b.Wm"] + parts("yb", [c]), [tk(1)], bank)
+            vop(CL, [tk(1), "c.cU"], ["ui" + s], lambda: V.tensor_scalar(m(T.ui), B(1), C("cU"), None, A.add), [bank])
+            vop(CL, ["ui" + s], ["uu" + s], lambda: V.tensor_scalar(m(T.uu), m(T.ui), 2047, None, A.bitwise_and))
+            vop(CL, ["uu" + s], ["Ms" + s], lambda: V.tensor_scalar(m(T.Ms), m(T.uu), 2.0, 33.0, A.mult, A.add))
+            vop(CL, ["ui" + s], ["odd" + s], lambda: V.tensor_scalar(m(T.odd), m(T.ui), 1, None, A.bitwise_and))
+        if t == 0:
+            numbers()
+        scale(CL, CL, m(T.Ls), m(T.Ms), 2048.0, C("cA"), ["Ms" + s, "c.cA"], ["Ls" + s])
+        vop(2 * CL, ["cn" + s, "Ms" + s], [tk(1)], lambda: V.tensor_tensor(B(1), m(T.cn), m(T.Ms), A.mult), [bank])
+        index(c, B(1), tk(1), bank, T.Ls, "Ls" + s, T.off1, "off1" + s)
         gather(t, T.P, c * PW, T.off1, c, "P" + s, "off1" + s)
         r0 = (c * NU) % 2
         onS = c in CMP_S
@@ -274,11 +287,12 @@ def build(g, T, topo, core, rank):
                 lambda e: [Pm.transpose(T.PTp[0:CL, 0:128], mcl(T.stS, t * NC + c), Kb("ID"))], [4])
             scale(64, 128, T.stT[0:CL, c * 128:(c + 1) * 128], T.PTp[0:CL, 0:128], 1.0, 0.0, ["PTp"], ["stT" + s], [4])
         for h in range(NU):
-            top(8, 1024, ["b.ID"] + ["P%s.%d" % (s, q) for q in range(h * 64 // GL, (h + 1) * 64 // GL)], ["PTp"],
-                lambda e, h=h: [Pm.transpose(m128(T.PTp, b), T.P[:, c * PW + (8 * h + b) * 128:c * PW + (8 * h + b + 1) * 128], Kb("ID"))
-                                for b in range(8)], [4])
             u = c * NU + h
-            scale(512, 1024, T.PTs[:, u * 1024:(u + 1) * 1024], T.PTp[:, :], 1.0, 0.0, ["PTp"], ["PT%d" % u], [4])
+            pp, pt, pb = ((T.PTp, "PTp", 4), (T.PTq, "PTq", 7))[u % 2]
+            top(8, 1024, ["b.ID"] + ["P%s.%d" % (s, q) for q in range(h * 64 // GL, (h + 1) * 64 // GL)], [pt],
+                lambda e, h=h, pp=pp: [Pm.transpose(m128(pp, b), T.P[:, c * PW + (8 * h + b) * 128:c * PW + (8 * h + b + 1) * 128], Kb("ID"))
+                                       for b in range(8)], [pb])
+            scale(512, 1024, T.PTs[:, u * 1024:(u + 1) * 1024], pp[:, :], 1.0, 0.0, [pt], ["PT%d" % u], [pb])
 
             def sums(e, h=h, u=u):
                 ins = []
@@ -322,9 +336,6 @@ def build(g, T, topo, core, rank):
         sop(CL, [tk(1), "c.thr"], ["sg" + s], lambda: S.activation(m(T.sg), B(1), F.Sign, bias=C("thr")), [bank])
         sg, cn = m(T.sg), m(T.cn)
         mm(B(2), [(Kb("OH"), sg), (cr["OH"], one1)], ["b.OH", "r.OH", "b.one", "sg" + s], [tk(2)], bank)
-        kB = T.BS[:, 464 + NB * c:464 + NB * (c + 1)]
-        mm(kB, [(sel(T.SelK, r), T.sg[:, c * CL + r:(c + 1) * CL:16]) for r in range(16)] + [(Kb("ID"), T.ln16b[:, 0:NB])],
-           ["SelK", "b.ID", "ln16b", "sg" + s], ["s.kB" + s], 7, n=NB)
         mm(B(0), [(Kb("Ld"), sg), (cr["Ld"], one1)], ["b.Ld", "r.Ld", "b.one", "sg" + s], [tk(0)], bank)
         mm(B(3), [(Kb("Vu"), sg)], ["b.Vu", "sg" + s], [tk(3)], bank)
         mi = t * NC + c
@@ -332,33 +343,39 @@ def build(g, T, topo, core, rank):
         ohc = mcl(T.msg, mi)
         vop(CL, [tk(2), "cn" + s], [mt + "a"], lambda: V.tensor_tensor(ohc, cn, B(2), A.mult), [bank])
         ov = T.offv[:, NB * c:NB * (c + 1)]
-        vop(NB, ["s.kB" + s], ["offv" + s], lambda: V.tensor_scalar(ov, kB, 4104.0, float(CE), A.add, A.min), [7])
+        kB = (T.B0, T.B1)[(c + SIDE[2]) % 2][:, ((c // 2) * 4 + 2) * CL:((c // 2) * 4 + 2) * CL + NB]
+        mm(kB, [(sel(T.SelK, r), T.sg[:, c * CL + r:(c + 1) * CL:16]) for r in range(16)] + [(Kb("ID"), T.ln16b[:, 0:NB])],
+           ["SelK", "b.ID", "ln16b", "sg" + s], [tk(2)], bank, n=NB)
+        vop(NB, [tk(2)], ["offv" + s], lambda: V.tensor_scalar(ov, kB, 4104.0, float(CE), A.add, A.min), [bank])
         win = T.P[:, c * PW:(c + 1) * PW].indirect(ov)
         op({"V": (50, CL, 0, 0, 1, 0), "S": (65, CL, 0, 0, 1, 0)}, ["offv" + s, "Pz"] + ["P%s.%d" % (s, q) for q in range(GP)], [mt + "b"],
            lambda e: [V.tensor_copy(mcl(T.msgv, mi), win) if e == "V" else S.activation(mcl(T.msgv, mi), win, F.Copy)])
         dst = T.cores[(rank + 1 + t % (N - 1)) % N]
         src = T.cores[(rank - 1 - t % (N - 1)) % N]
         rid, pid = topo.addr(dst)[0], topo.addr(dst)[1]
+        mask, far = engines(core), engines(src)
         for x, out, in_ in (("a", T.land, T.msg), ("b", T.landv, T.msgv)):
             sem = "arr%d%s" % (mi, x)
             op({"G": (0, 0, 0, 0, 0, 0.3)}, [mt + x], ["land%d%s" % (mi, x)],
-               lambda e, out=out, in_=in_, sem=sem: [g.remote_dma(mcl(out, mi), mcl(in_, mi), T.sem[sem], T.sem.sent, pid, rid, topo.mask(core, dst))],
-               lat="far", sem=(sem, len(topo.engines(src, core))))
-            ops[-1]["sent"] = len(topo.engines(core, dst))
+               lambda e, out=out, in_=in_, sem=sem: [g.remote_dma(mcl(out, mi), mcl(in_, mi), T.sem[sem], T.sem.sent, pid, rid, sum(1 << q for q in mask))],
+               lat="far", sem=(sem, len(far)))
+            ops[-1]["sent"] = len(mask)
         vop(CL, [tk(0), "odd" + s], ["nmd" + s], lambda: V.tensor_tensor(m(T.nmd), m(T.odd), B(0), A.is_lt), [bank])
         sop(CL, [tk(3), "c.bVu"], ["mu" + s, "cnt" + s],
             lambda: S.activation(m(T.mu), B(3), F.Relu, bias=C("bVu"), accum_out=T.cnt[:, c:c + 1]), [bank])
-        mm(B(1), [(Kh("BO"), ohc), (cr["e32"], one1)], ["h.BO", "r.e32", "b.one", mt + "a"], [tk(1)], bank)
+        mm(B(1), [(cr["e15"], one1), (Kh("R15"), ohc)], ["h.R15", "r.e15", "b.one", mt + "a"], [tk(1)], bank)
         vop(CL, [tk(1), "uu" + s], ["fa" + s], lambda: V.tensor_tensor(m(T.fa), m(T.uu), B(1), A.mult), [bank])
         vop(CL, ["fa" + s], ["fb" + s], lambda: V.tensor_scalar(m(T.fb), m(T.fa), 5, 4095, A.arith_shift_right, A.bitwise_and))
-        vop(CL, ["fb" + s], ["fr" + s], lambda: V.tensor_scalar(m(T.fr), m(T.fb), -2048.0, None, A.add))
-        mm(B(0), [(Kh("ID"), cn), (Kb("KI"), m(T.nmd)), (Kb("nKI"), m(T.mu))],
-           ["h.ID", "b.KI", "b.nKI", "cn" + s, "nmd" + s, "mu" + s], [tk(0)], bank)
+        mm(B(0), [(Kh("ID"), cn), (cr["Ts"], one1), (Kb("KI"), m(T.nmd)), (Kb("nKI"), m(T.mu))],
+           ["h.ID", "b.KI", "b.nKI", "r.Ts", "b.one", "cn" + s, "nmd" + s, "mu" + s], [tk(0)], bank)
         mm(B(2), [(Kh("SD"), cn), (Kh("R0"), ohc), (Kb("nKI"), m(T.nmd))],
            ["h.SD", "h.R0", "b.nKI", "cn" + s, "nmd" + s, mt + "a"], [tk(2)], bank)
-        mm(B(3), [(Kh("SU"), cn), (Kb("KI"), m(T.mu)), (cr["Tu"], one1), (Kh("R15"), m(T.fr))],
-           ["h.SU", "h.R15", "b.KI", "r.Tu", "b.one", "cn" + s, "mu" + s, "fr" + s], [tk(3)], bank)
-        select(c, -4096.0, T.cn, "cn" + s)
+        mm(B(3), [(Kh("SU"), cn), (cr["Tu"], one1), (Kb("KI"), m(T.mu))],
+           ["h.SU", "b.KI", "r.Tu", "b.one", "cn" + s, "mu" + s], [tk(3)], bank)
+        vop(CL, [tk(3), "fb" + s], ["ts" + s], lambda: V.tensor_tensor(m(T.ts), m(T.fb), B(3), A.add), [bank])
+        select(c, 2, 0, T.cn, "cn" + s)
+        if t < RO - 1:
+            numbers()
 
     def phase_q(t, c):
         B, tk, bank = tiles(c)
@@ -373,7 +390,7 @@ def build(g, T, topo, core, rank):
         index(c, B(2), tk(2), bank, T.L2, "L2" + s, T.off2, "off2" + s)
         gather(t, T.x2, c * CE, T.off2, c, "x2" + s, "off2" + s)
 
-        def near(h):
+        def near(h, part):
             l0 = c * CL + h * UC
             xt = ["x2%s.%d" % (s, q) for q in range(h * UC // GL, (h + 1) * UC // GL)]
             xk = lambda k: T.x2[:, 16 * l0 + k:16 * (l0 + UC):16]
@@ -392,30 +409,36 @@ def build(g, T, topo, core, rank):
                 mm(B(0, h), [(E8, T.thS[0:8, l0:l0 + UC])] + [(sel(T.SelN, k), mk(k)) for k in range(16)],
                    ["b.E8", "th", "SelN"] + it, [tk(0)], bank, n=UC)
                 return
-            vi = (c * NH + h) % (192 // UC)
-            vh, vt = T.BS[:, L + vi * UC:L + (vi + 1) * UC], "s.vP%d" % vi
-            mm(vh, [(Kb("ID"), vv)], ["b.ID", lw], [vt], 7, n=UC)
-            mm(B(0, h), [(E8, T.thS[0:8, l0:l0 + UC]), (Kb("BO"), vv)] + [(sel(T.Sel, k), xk(k)) for k in range(16)],
-               ["b.E8", "th", "b.BO", lw, "Sel"] + xt, [tk(0)], bank, True, False, n=UC)
+            vi = (c * NH + h) % 2
+            vh, vt = T.R[:, vi * 1024:vi * 1024 + UC], "R%d" % vi
+            if part == 0:
+                mm(vh, [(Kb("ID"), vv)], ["b.ID", lw], [vt], 2 * vi, n=UC)
+                mm(B(0, h), [(sel(T.Sel, k), xk(k)) for k in range(16)], ["Sel"] + xt, [tk(0)], bank, False, False, n=UC)
+                return
             for kq in range(0, 16, KQ):
                 it = "mx%s.%d.%d" % (s, h, kq)
-                vops(KQ, UC, xt + [vt], [it], lambda e, kq=kq: [V.tensor_tensor(mk(k), xk(k), vh, A.max) for k in range(kq, kq + KQ)], [7])
-                mm(B(0, h), [(sel(T.SelN, k), mk(k)) for k in range(kq, kq + KQ)], ["SelN", it], [tk(0)], bank, False, kq + KQ == 16, n=UC)
-        for h in range(NH):
-            near(h)
+                vops(KQ, UC, xt + [vt], [it], lambda e, kq=kq: [V.tensor_tensor(mk(k), xk(k), vh, A.max) for k in range(kq, kq + KQ)], [2 * vi])
+                mm(B(0, h), [(sel(T.SelN, k), mk(k)) for k in range(kq, kq + KQ)], ["SelN", it], [tk(0)], bank, False,
+                   kq + KQ == 16 and h == NH - 1, n=UC)
+        mm(B(0), [(E8, T.thS[0:8, c * CL:(c + 1) * CL]), (Kb("BO"), lv)], ["b.E8", "th", "b.BO", lw], [tk(0)], bank, True, False)
+        for part in range(2):
+            for h in range(NH):
+                near(h, part)
         sop(CL, [tk(0)], ["eta" + s], lambda: S.activation(m(T.eta), B(0), F.Sign, bias=0.5), [bank])
-        mm(B(1), [(Kb("Qm"), m(T.eta)), (Kb("BOs"), lv)], ["b.Qm", "b.BOs", "eta" + s, lw], [tk(1)], bank)
-        sop(CL, [tk(1), "c.bQ"], ["qq" + s], lambda: S.activation(m(T.qq), B(1), F.Sign, bias=C("bQ")), [bank])
+        mm(B(1), [(T.rQ[0:1, :], one1), (Kb("BOs"), lv), (Kb("Qm"), m(T.eta))], ["b.Qm", "b.BOs", "r.Q", "b.one", "eta" + s, lw], [tk(1)], bank)
+        sop(CL, [tk(1)], ["qq" + s], lambda: S.activation(m(T.qq), B(1), F.Sign, scale=-1.0), [bank])
         cn, qq = m(T.cn), m(T.qq)
         z = "L" if t == RO - 1 else ""
-        mm(B(0), [(Kh("ID"), cn), (Kb("nKI"), qq)], ["h.ID", "b.nKI", "cn" + s, "qq" + s], [tk(0)], bank)
+        vop(CL, [tk(1), "cn" + s], ["ts" + s], lambda: V.tensor_tensor(m(T.ts), cn, B(1), A.min), [bank])
+        if z:
+            scale(CL, CL, m(T.ts), m(T.ts), 1.0, 2048.0, ["ts" + s], ["ts" + s])
         mm(B(2), [(Kh("SD"), cn), (cr["Td" + z], one1), (Kb("KSD"), qq)], ["h.SD", "b.KSD", "r.Td" + z, "b.one", "cn" + s, "qq" + s], [tk(2)], bank)
         mm(B(3), [(Kh("BO"), le), (cr["Te" + z], one1), (Kb("KIS"), qq)], ["h.BO", "b.KIS", "r.Te" + z, "b.one", lt, "qq" + s], [tk(3)], bank)
         if z:
-            select(c, -2048.0, T.ycS, "yc" + s)
+            select(c, 2, 3, T.ycS, "yc" + s)
             dma("Y", mcl(T.yc, c), m(T.ycS), ["yc" + s], ["o.yc" + s], "oc" + s, 2.0)
         else:
-            select(c, -4096.0, T.cn, "cn" + s)
+            select(c, 2, 3, T.cn, "cn" + s)
 
     def scatter(t, to):
         X, xt = XX[to]
@@ -426,8 +449,8 @@ def build(g, T, topo, core, rank):
     for t in range(RO):
         p = t % 2
         if t < RO - 1:
-            mm(T.BS[:, 448:464], [(sel(T.SelW, r), T.yb[:, r:L:16]) for r in range(16)], ["SelW"] + parts("yb"), ["s.uB"], 7, n=16)
-            vop(16, ["s.uB", "c.cU"], ["ra"], lambda: V.tensor_scalar(T.ra[:, :], T.BS[:, 448:464], C("cU"), None, A.add), [7])
+            mm(T.R[:, 1024:1040], [(sel(T.SelW, r), T.yb[:, r:L:16]) for r in range(16)], ["SelW"] + parts("yb"), ["R1"], 2, n=16)
+            vop(16, ["R1", "c.cU"], ["ra"], lambda: V.tensor_scalar(T.ra[:, :], T.R[:, 1024:1040], C("cU"), None, A.add), [2])
             vop(16, ["ra"], ["rb"], lambda: V.tensor_scalar(T.rb[:, :], T.ra[:, :], 31, None, A.bitwise_and))
             vop(32, ["rb", "ln32c"], ["rc"], lambda: V.tensor_tensor(T.rc[:, :], T.rb[:, :], T.ln32c[:, :], A.add))
             vop(16, ["rc"], ["offr%d" % p], lambda p=p: V.tensor_copy(T.offr[:, 16 * p:16 * p + 16], T.rc[:, :]))
@@ -437,8 +460,8 @@ def build(g, T, topo, core, rank):
             scale(L // 2, L, T.yyS[:, :], T.yb[:, :], 1.0, -YB, parts("yb"), ["yy"])
             dma("Y", T.yy[:, :], T.yyS[:, :], ["yy"], ["o.yy"], "oy", 2.0)
         else:
-            mm(T.BS[:, 480:480 + NC], [(K("A32"), T.cnt[:, :])], ["k.A32"] + every("cnt"), ["s.cU"], 7, n=256)
-            vop(1, ["s.cU"], ["cs"], lambda: V.tensor_reduce(T.cs[:, :], T.BS[:, 480:480 + NC], AxisListType.X, A.add), [7])
+            mm(T.R[:, 1538:1538 + NC], [(K("A32"), T.cnt[:, :])], ["k.A32", "R1"] + every("cnt"), ["s.cnt"], 3, n=256)
+            vop(1, ["s.cnt", "R1"], ["cs"], lambda: V.tensor_reduce(T.cs[:, :], T.R[:, 1538:1538 + NC], AxisListType.X, A.add), [3])
             scale(1, 1, C("cA"), T.cs[:, :], 1.0, -262144.0, ["cs"], ["c.cA"])
             vop(0, XX[p][1] + ["offr%d" % p] + parts("ez"), ["Wn"],
                 lambda p=p: V.tensor_tensor(T.Wn[:, :], XX[p][0][:, 0:W].indirect(T.offr[:, 16 * p:16 * p + 16]), T.ez[:, :], A.add), ga=L)
@@ -526,6 +549,10 @@ def replay(ops, deps, order, pick, P):
     bank = [("", 0.0, -1)] * 8
     fin = [0.0] * len(ops)
     why = [(-1, False)] * len(ops)
+    key = ("tab", len(ops)) + tuple(P.values())
+    if key not in PLAN:
+        PLAN[key] = [dict({e: cost(o, e, P) for e in o["eng"]}, way=way(o, P)) for o in ops]
+    tab = PLAN[key]
     lat = P["lat"]
     for i in order:
         o, e = ops[i], pick[i]
@@ -539,11 +566,11 @@ def replay(ops, deps, order, pick, P):
             if x >= t:
                 t, w = x, (d, False)
         why[i] = w
-        t += cost(o, e, P)
+        t += tab[i][e]
         free[e] = (t, i)
         for b in o["banks"]:
             bank[b] = (e, t, i)
-        fin[i] = t + way(o, P)
+        fin[i] = t + tab[i]["way"]
     end = max(fin)
     i, pairs = fin.index(end), []
     while why[i][0] >= 0:
@@ -553,7 +580,7 @@ def replay(ops, deps, order, pick, P):
     return end, pairs
 
 
-def plan(ops, deps, tries=TRIES):
+def plan(ops, deps, tries=TRIES, swaps=SWAPS):
     n = len(ops)
     succ = [[] for _ in range(n)]
     for i in range(n):
@@ -575,7 +602,7 @@ def plan(ops, deps, tries=TRIES):
         order, start = lay(ops, deps, succ, [pri[i] + noise[i] for i in range(n)], pick, hold, FIG)
         res = [replay(ops, deps, order, pick, P) for P in FIGS]
         return sum(r[0] for r in res) / len(FIGS), order, start, [b for r in res for b in r[1]]
-    pick = [o["eng"][-1] if "PTp" not in o["rd"] else "V" for o in ops]
+    pick = [o["eng"][-1] if o["rd"] not in (["PTp"], ["PTq"]) else "V" for o in ops]
     noise, hold = [EARLY if o["wr"][0][:2] in ("k.", "b.", "h.", "c.", "r.", "Se", "ln") else 0.0 for o in ops], [0.0] * n
     cur = best = score(pick, noise, hold) + (pick,)
     for it in range(tries):
@@ -607,7 +634,58 @@ def plan(ops, deps, tries=TRIES):
             cur, pick, noise, hold = s2 + (p2,), p2, n2, h2
             if cur[0] < best[0]:
                 best = cur
-    return best[1], best[4], best[2], best[0]
+    pre = [list(deps[i]) + ops[i]["soft"] for i in range(n)]
+
+    def rate(order, pick):
+        opened = set()
+        for i in order:
+            o = ops[i]
+            if o["grp"]:
+                if o["grp"] & 1 and o["banks"][0] in opened:
+                    return None
+                if o["grp"] == 1:
+                    opened.add(o["banks"][0])
+                if o["grp"] == 2:
+                    opened.discard(o["banks"][0])
+        res = [replay(ops, deps, order, pick, P) for P in FIGS]
+        return sum(r[0] / w for r, w in zip(res, base)), [b for r in res for b in r[1]]
+    order, pick = best[1], best[4]
+    base = [replay(ops, deps, order, pick, P)[0] * len(FIGS) / best[0] for P in FIGS]
+    cur = rate(order, pick)
+    top = (cur[0], order, pick)
+    for it in range(swaps):
+        i, j = cur[1][int(rnd() * len(cur[1]))]
+        o2, p2, x = order, pick, rnd()
+        c = [k for k in (i, j) if len(ops[k]["eng"]) > 1]
+        if x < 0.25 and c:
+            p2 = list(pick)
+            k = c[int(rnd() * len(c))]
+            p2[k] = "V" if p2[k] == "S" else "S"
+        else:
+            a, b = order.index(j), order.index(i)
+            win = order[a:b + 1]
+            if x < 0.65:
+                mv = {i}
+                for k in reversed(win):
+                    if k in mv:
+                        mv.update(pre[k])
+                if j in mv:
+                    continue
+                o2 = order[:a] + [k for k in win if k in mv] + [k for k in win if k not in mv] + order[b + 1:]
+            else:
+                mv = {j}
+                for k in win:
+                    if any(d in mv for d in pre[k]):
+                        mv.add(k)
+                if i in mv:
+                    continue
+                o2 = order[:a] + [k for k in win if k not in mv] + [k for k in win if k in mv] + order[b + 1:]
+        s2 = rate(o2, p2)
+        if s2 and s2[0] <= cur[0] + HEAT * rnd() * rnd() * (1 - it / swaps):
+            cur, order, pick = s2, o2, p2
+            if cur[0] < top[0]:
+                top = (cur[0], order, pick)
+    return top[1], top[2], best[2], top[0]
 
 
 PLAN = {}

@@ -1,47 +1,44 @@
 from concourse.mybir import AluOpType as A, AxisListType, ActivationFunctionType as F
 
 N, L, W, RO = 8, 256, 8192, 4
-NC = 2
+NC = 4
 CL = L // NC
 CE = 16 * CL
-NU = CL // 64
-GL = 32
-GP = CL // GL
+HE = CE // 2
 NB = CL // 16
-UC = 64
-NH = CL // UC
 KQ = 8
-SIDE = (0, 0, 0, 0)
-QS = 32768.0
 TWO = False
-CMP_S = ()
-ABS_S = ()
 YB, WB = 160.0, 320.0
+U = 2048.0
 
 f32, bf, f16, i32, u16 = "float32", "bfloat16", "float16", "int32", "uint16"
+K32 = ["one", "t0", "BO", "ID", "LT", "LE", "SD", "SU", "A32", "H3", "t1", "t2", "t3", "t4"]
+KB = ["ID", "Mm", "OH", "Bm", "KW", "Ld", "Vu", "Qm", "Fl", "KI", "nKI", "Wm", "E8", "one", "BO", "BO3"]
+KH = ["ID", "IDu", "SDu", "SUu", "R0", "R15", "BOe", "Dm", "H1", "H2"]
 SCRATCH = {n: ("sbuf", [128, w], d) for n, w, d in [
-    ("XA", W, bf), ("XB", W, bf), ("cin", L, i32), ("stS", RO * L, bf), ("yin", L, bf), ("wS", 1, bf), ("thS", L, bf),
-    ("cn", L, f16), ("yb", L, bf), ("ycS", L, f32), ("yyS", L, bf), ("P", NC * (CE + 16), bf),
-    ("PTs", 16 * L, bf), ("Ib", 16 * L, bf), ("x2", 16 * L, bf), ("mx", 16 * L, bf),
+    ("XA", W, bf), ("XB", W if TWO else 16, bf), ("cin", L, i32), ("stS", RO * L, bf), ("yin", L, bf), ("wS", 1, bf), ("thS", L, bf),
+    ("cn", L, f16), ("cs", L, f16), ("yb", L, bf), ("ycS", L, f32), ("yyS", L, bf), ("P", 16 * L, bf),
+    ("PTs", 16 * L, bf), ("Ib", 16 * L, bf), ("mx", 16 * L, bf),
     ("ui", L, i32), ("uu", L, i32), ("odd", L, i32), ("Ls", L, f32), ("L2", L, f32), ("va", L, i32), ("vb", L, i32),
-    ("off1", L, u16), ("off2", L, u16), ("offv", 16, u16), ("offr", 32, u16),
-    ("pw", L, bf), ("sg", L, bf), ("nmd", L, bf), ("mu", L, bf), ("fa", L, i32), ("fb", L, i32), ("Ms", L, f32),
-    ("ts", L, f32), ("zz", L, f32), ("eta", L, bf), ("qq", L, bf), ("ez", L, f32), ("Wn", L, bf), ("nx", 2 * L, bf),
-    ("ra", 16, i32), ("rb", 16, i32), ("rc", 16, i32), ("cnt", NC, f32), ("cs", 1, f32), ("col", 32, f32),
-    ("msg", RO * L, f16), ("land", RO * L, f16), ("msgv", RO * L, bf), ("landv", RO * L, bf),
-    ("k32", 13 * 128, f32), ("kb", 17 * 128, bf), ("kh", 7 * 128, f16), ("SelL", CE, bf), ("stT", NC * 128, bf), ("i0", L, bf),
-    ("Sel", 144, bf), ("SelN", 144, bf), ("SelK", 144, bf), ("SelW", 144, bf),
-    ("crow", 11 * 128, bf), ("rQ", 128, bf), ("rQi", 128, f32), ("ln16", 16, f32), ("ln16b", 16, bf), ("ln32", 16, f32), ("ln32c", 16, f32)]}
-SCRATCH.update({"R": ("psum", [128, 2048], f32), "PTp": ("psum", [128, 1024], bf),
-                "B0": ("psum", [128, 512], f32), "B1": ("psum", [128, 512], f32), "PTq": ("psum", [128, 1024], bf)})
+    ("off1", L, u16), ("off2", L, u16), ("offv", NC * NB, u16), ("offr", 32, u16), ("sc", L, f32), ("cap", CL, f32),
+    ("pw", L, bf), ("sg", 2 * L, bf), ("md", L, bf), ("fa", L, i32), ("fb", L, i32), ("Ms", L, f32),
+    ("ts", L, f32), ("zz", L, f32), ("eta", L, bf), ("qq", L, bf), ("qd", L, f32), ("ez", L, f32), ("Wn", L, bf), ("nx", 2 * L, bf),
+    ("ra", 16, i32), ("rb", 16, i32), ("rc", 16, i32), ("cnt", NC, f32), ("cj", NC, f32), ("col", 32, f32),
+    ("msg", RO * L, f16), ("land", RO * L, f16), ("msgv", 2 * RO * L, bf), ("landv", 2 * RO * L, bf), ("x2", 16 * L, bf),
+    ("k32", len(K32) * 128, f32), ("kb", len(KB) * 128, bf), ("kh", len(KH) * 128, f16),
+    ("Sel", 144, bf), ("SelN", 144, bf), ("SelW", 144, bf),
+    ("crow", 2 * 128, bf), ("ramp", CL, bf), ("ln32", 16, f32), ("ln32c", 16, f32)]}
+SCRATCH.update({"R": ("psum", [128, 1024], f32), "Pa": ("psum", [128, 1024], bf), "Pb": ("psum", [128, 1024], bf)})
+SCRATCH.update({"B%d" % c: ("psum", [128, 512], f32) for c in range(NC)})
 SEMAPHORES = (["sV", "sS", "sT", "sG", "sent", "dX0", "dX1", "dXB", "dc", "dst0", "dst1", "dy", "dw", "dth", "oy"]
               + ["oc%d" % c for c in range(NC)] + ["arr%d%s" % (i, x) for i in range(RO * NC) for x in "ab"])
 
 FIG = dict(cy=0.00083, ga=1.56, sc=3.8, pe=0.00042, lat=0.18, ov=0.005, far=3.0)
 FIGS = [FIG, dict(FIG, lat=0.08, ov=0.025), dict(FIG, cy=0.0011, pe=0.00055, ga=1.2, sc=2.5, lat=0.15, ov=0.01, far=4.0),
         dict(FIG, cy=0.0011, pe=0.00055, ga=1.9, sc=5.0, far=4.0)]
-TRIES, SWAPS, HEAT = 400, 5000, 0.3
-EARLY = 40.0
+MID = dict(FIG, lat=0.15, ov=0.012)
+TRIES, SWAPS, HEAT, SEED = 1500, 4000, 0.3, 12345
+PRICE = (4.0, 2.5)
 
 
 def cost(o, e, P):
@@ -49,43 +46,59 @@ def cost(o, e, P):
     return (cy + ga * P["ga"] + sc * P["sc"]) * P["cy"] + pe * P["pe"] + k * P["ov"] * (0.5 if e == "T" else 1) + fix
 
 
+def bank_of(tok):
+    if tok[0] == "R" and tok[1:].isdigit():
+        return int(tok[1])
+    if tok[:2] in ("Pa", "Pb"):
+        return 2 + (tok[1] == "b")
+    if tok[0] == "B" and tok[1].isdigit():
+        return 4 + int(tok[1])
+    return None
+
+
 def build(g, T, topo, core, rank):
     ops = []
     V, S, Pm = g.vector, g.scalar, g.tensor
 
-    def op(c, rd, wr, fn, banks=(), lat=0.0, sem=None, grp=0):
-        if list(banks) == [5]:
-            banks = sorted(set(5 + (int(k[1]) + SIDE[int(k[3])]) % 2 for k in list(rd) + list(wr) if k[0] == "B"))
-        ops.append(dict(eng="".join(c), c=c, rd=list(rd), wr=list(wr), fn=fn, banks=list(banks), lat=lat, sem=sem, grp=grp, soft=[]))
+    def op(c, rd, wr, fn, lat=0.0, sem=None, grp=0):
+        banks = []
+        for k in list(wr) + list(rd):
+            if bank_of(k) is not None and bank_of(k) not in banks:
+                banks.append(bank_of(k))
+        ops.append(dict(eng="".join(c), c=c, rd=list(rd), wr=list(wr), fn=fn, banks=banks, lat=lat, sem=sem, grp=grp, soft=[]))
 
-    def vop(n, rd, wr, fn, banks=(), ga=0, sc=0):
-        op({"V": (max(64, n) if n else 50, ga, sc, 0, 1, 0)}, rd, wr, lambda e: [fn()], banks)
+    def vop(n, rd, wr, fn, ga=0, sc=0):
+        op({"V": (max(64, n) if n else 60, ga, sc, 0, 1, 0)}, rd, wr, lambda e: [fn()])
 
-    def vops(k, n, rd, wr, fn, banks=()):
-        op({"V": (k * max(64, n), 0, 0, 0, k, 0)}, rd, wr, fn, banks)
+    def vops(k, n, rd, wr, fn):
+        op({"V": (k * max(64, n), 0, 0, 0, k, 0)}, rd, wr, fn)
 
-    def sop(n, rd, wr, fn, banks=()):
-        op({"S": (max(64, n), 0, 0, 0, 1, 0.05)}, rd, wr, lambda e: [fn()], banks)
+    def sop(n, rd, wr, fn, fix=0.05):
+        op({"S": (max(64, n), 0, 0, 0, 1, fix)}, rd, wr, lambda e: [fn()])
 
-    def scale(nv, ns, out, in_, by, add, rd, wr, banks=()):
+    def scale(nv, ns, out, in_, by, add, rd, wr):
         def fn(e):
             if e == "S":
                 return [S.activation(out, in_, F.Identity, bias=add, scale=by)]
             if by == 1.0 and add == 0.0:
                 return [V.tensor_copy(out, in_)]
             return [V.tensor_scalar(out, in_, by, add, A.mult, A.add)]
-        op({"V": (max(64, nv), 0, 0, 0, 1, 0), "S": (max(64, ns), 0, 0, 0, 1, 0.05)}, rd, wr, fn, banks)
+        op({"V": (max(64, nv), 0, 0, 0, 1, 0), "S": (max(64, ns), 0, 0, 0, 1, 0.05)}, rd, wr, fn)
+
+    def pick(out, src, n, rd, wr):
+        op({"V": (60, n, 0, 0, 1, 0), "S": (78, n, 0, 0, 1, 0)}, rd, wr,
+           lambda e: [V.tensor_copy(out, src) if e == "V" else S.activation(out, src, F.Copy)])
 
     def gop(n, rd, wr, fn):
         op({"G": (2 * n, 0, 0, 0, 0, 0.17)}, rd, wr, lambda e: [fn()])
 
-    def top(k, n, rd, wr, fn, banks, grp=3):
-        op({"T": (0, 0, 0, n, k, 0.0)}, rd, wr, fn, banks, grp=grp)
+    def top(k, n, rd, wr, fn, grp=3):
+        op({"T": (0, 0, 0, n, k, 0.0)}, rd, wr, fn, grp=grp)
 
-    def mm(out, terms, rd, wr, bank, first=True, last=True, n=CL):
+    def mm(out, terms, rd, wr, first=True, last=True, n=CL, more=0):
         def fn(e):
             return [Pm.matmul(out, l, r, first and i == 0, last and i == len(terms) - 1) for i, (l, r) in enumerate(terms)]
-        top(len(terms), len(terms) * max(64, n), rd, wr, fn, [bank], first + 2 * last)
+        top(len(terms), (len(terms) + more) * max(64, n), rd, wr, fn, first + 2 * last)
 
     lastd = []
 
@@ -114,45 +127,48 @@ def build(g, T, topo, core, rank):
         dma("Y", T.XB[:, :], T.x0[:, :], ["XA0", "XA1"], ["XB0", "XB1"], "dXB", 8.0)
         XX[1] = (T.XB, ["XB0", "XB1"])
 
-    k32 = {n: i for i, n in enumerate(["one", "t0", "BO", "ID", "LT", "LE", "SD", "SU", "A32", "t1", "t2", "t3", "t4"])}
-    kb = {n: i for i, n in enumerate(["ID", "Mm", "Bm", "OH", "Ld", "Vu", "Qm", "KI", "nKI", "KSD", "KIS", "Wm", "E8", "one", "BO", "BOs", "nID"])}
-    kh = {n: i for i, n in enumerate(["ID", "SD", "SU", "BO", "R0", "R15", "BO3"])}
-    cols = {n: i for i, n in enumerate(["n", "r0", "r15", "cM", "rpos", "s", "mid", "c0", "dLd", "hVu", "kw", "thr", "bVu", "bQ",
-                                        "j16", "j32", "a32", "wf", "cU", "cA", "sE", "bE"])}
-    K = lambda n: m128(T.k32, k32[n])
-    Kb = lambda n: m128(T.kb, kb[n])
-    Kh = lambda n: m128(T.kh, kh[n])
+    cols = {n: i for i, n in enumerate(["n", "r0", "r15", "cM", "rpos", "s", "mid", "c0", "dLd", "hVu", "kw", "kx", "thr", "bVu", "bQ", "e4",
+                                        "j32", "a32", "wf", "cU", "cA", "nr0", "fl", "e32", "e3", "dm", "h2", "ra", "rb", "dif"])}
+    K = lambda n: m128(T.k32, K32.index(n))
+    Kb = lambda n: m128(T.kb, KB.index(n))
+    Kh = lambda n: m128(T.kh, KH.index(n))
     C = lambda n: T.col[:, cols[n]:cols[n] + 1]
-    K8 = lambda n: T.k32[:, k32[n] * 128:(k32[n] + 1) * 128:16]
+    K8 = lambda n: T.k32[:, K32.index(n) * 128:(K32.index(n) + 1) * 128:16]
+    kcol = lambda buf, i, k: buf[:, i * 128 + k:(i + 1) * 128:16]
     top8 = lambda buf, i: buf[0:8, i * 128:(i + 1) * 128]
 
     vop(128, [], ["k.one"], lambda: V.memset(K("one"), 1.0))
 
     def asel(out, in_, pat, cmp, fill, base, cm, view=m128):
-        gop(128, ["k." + in_], ["k." + out], lambda: g.affine_select(view(T.k32, k32[out]), view(T.k32, k32[in_]), pat, cmp, fill, base, cm))
+        gop(128, ["k." + in_], ["k." + out],
+            lambda: g.affine_select(view(T.k32, K32.index(out)), view(T.k32, K32.index(in_)), pat, cmp, fill, base, cm))
     asel("t0", "one", [[-16, 8], [0, 16]], A.is_ge, 0.0, 0, 1)
     asel("BO", "t0", [[16, 8], [0, 16]], A.is_ge, 0.0, 15, -1)
     asel("LT", "BO", [[1, 128]], A.is_ge, 0.0, -1, -1)
     asel("ID", "one", [[-1, 128]], A.is_equal, 0.0, 0, 1)
-    asel("LE", "BO", [[1, 128]], A.is_ge, 0.0, 0, -1)
+    gop(16, [], ["ln32"], lambda: g.iota(T.ln32[:, :], [[512, 16]], 0, 0, allow_small_or_imprecise_dtypes=True))
     asel("SD", "BO", [[1, 128]], A.is_equal, 0.0, -1, -1)
     asel("SU", "BO", [[1, 128]], A.is_equal, 0.0, 1, -1)
-    gop(8, [], ["ln16"], lambda: g.iota(T.ln16[:, :], [[256, 16]], 0, 0, allow_small_or_imprecise_dtypes=True))
-    gop(16, [], ["ln32"], lambda: g.iota(T.ln32[:, :], [[512, 16]], 0, 0, allow_small_or_imprecise_dtypes=True))
+    gop(CL, [], ["ramp"], lambda: g.iota(T.ramp[0:1, :], [[16, CL]], 0, 0, allow_small_or_imprecise_dtypes=True))
     asel("t3", "one", [[1, 128]], A.is_ge, 0.0, 0, -16, top8)
     asel("t3", "t3", [[-1, 128]], A.is_ge, 0.0, 15, 16, top8)
-    E8 = top8(T.kb, kb["E8"])
-    scale(128, 128, E8, top8(T.k32, k32["t3"]), 1.0, 0.0, ["k.t3"], ["b.E8"])
+    E8 = top8(T.kb, KB.index("E8"))
+    scale(128, 128, E8, top8(T.k32, K32.index("t3")), 1.0, 0.0, ["k.t3"], ["b.E8"])
+    vop(256, ["k.LT", "k.ID"], ["k.LE"], lambda: V.tensor_tensor(K("LE"), K("LT"), K("ID"), A.add))
 
     def cts(out, in_, s1, s2, o0, o1=None):
         if o1 is None:
             vop(1, ["c." + in_], ["c." + out], lambda: V.tensor_scalar(C(out), C(in_), s1, None, o0))
-        elif (o0, o1) == (A.mult, A.add):
+        else:
             scale(1, 1, C(out), C(in_), s1, s2, ["c." + in_], ["c." + out])
 
-    def sc(out, otok, in_, by):
+    def sc(out, otok, in_, by, half=False):
         col = isinstance(by, str)
-        scale(128, 128, out, K(in_), C(by) if col else by, 0.0, ["k." + in_] + (["c." + by] if col else []), [otok])
+        rd = ["k." + in_] + (["c." + by] if col else [])
+        if half:
+            vop(128, rd, [otok], lambda: V.tensor_scalar(out, K(in_), C(by) if col else by, None, A.mult))
+        else:
+            scale(128, 128, out, K(in_), C(by) if col else by, 0.0, rd, [otok])
     scale(1, 1, C("wf"), T.wS[:, :], 1.0, 0.0, ["wS"], ["c.wf"])
     sc(Kb("Wm"), "b.Wm", "BO", "wf")
     vop(64, [], ["b.one"], lambda: V.memset(Kb("one"), 1.0))
@@ -160,16 +176,27 @@ def build(g, T, topo, core, rank):
     vop(128, ["k.LT"], ["c.n"], lambda: V.tensor_reduce(C("n"), K("LT"), AxisListType.X, A.add))
     cts("r0", "n", 15.0, None, A.is_equal)
     cts("r15", "n", 0.0, None, A.is_equal)
-    cts("cM", "n", 0.125, 0.125, A.mult, A.add)
-    cts("rpos", "n", 15.0, None, A.is_lt)
     vop(1, ["c.r0", "c.r15"], ["c.s"], lambda: V.tensor_tensor(C("s"), C("r0"), C("r15"), A.add))
-    vop(1, ["c.r0", "c.r15"], ["c.dLd"], lambda: V.tensor_tensor(C("dLd"), C("r15"), C("r0"), A.subtract))
-    for out, in_, a, b in (("mid", "s", -0.5, 0.5), ("c0", "r0", -101.0, 1.0), ("hVu", "s", -0.5, 0.0), ("kw", "s", 2048.5, -0.5),
-                           ("thr", "r15", -54.6, 0.0), ("bVu", "dLd", 0.5, -0.5), ("j16", "n", -16.0, 240.0),
-                           ("j32", "n", -32.0, 480.0), ("a32", "r15", 32.0, 0.0), ("sE", "r0", 4.0, 4.0), ("bE", "r0", -64.0, 0.0)):
+    vop(1, ["c.r0", "c.r15"], ["c.dif"], lambda: V.tensor_tensor(C("dif"), C("r15"), C("r0"), A.subtract))
+    sop(1, ["c.r0"], ["c.e4"], lambda: S.activation(C("e4"), C("r0"), F.Exp, scale=4.0), 1.3)
+    row0 = lambda by, add: (add - 15 * by, by)
+    for out, in_, (a, b) in (("cM", "n", (0.125, 0.125)), ("rpos", "r0", (-1.0, 1.0)), ("mid", "s", (-0.5, 0.5)), ("c0", "r0", (-101.0, 1.0)),
+                             ("nr0", "r0", (-1.0, 0.0)), ("thr", "e4", (1.0, -1.0)), ("dLd", "s", (-1.0, 0.0)), ("hVu", "dif", (-0.5, 0.0)),
+                             ("bVu", "dif", (0.5, -0.5)), ("kx", "n", (0.5, -7.5)), ("bQ", "n", (8.5, 180.0)), ("fl", "r15", (-300.0, 0.0)),
+                             ("j32", "n", (-32.0, 480.0)), ("a32", "r15", (32.0, 0.0)), ("e32", "r0", row0(U, U + 32)),
+                             ("e3", "r0", row0(3232 * U, 1441792.0)), ("dm", "r0", row0(-U, 0.0)), ("h2", "r0", row0(U / 2, 0.0)),
+                             ("ra", "r0", row0(U, -2 * U)), ("rb", "r0", (-2 * U, 0.0))):
         cts(out, in_, a, b, A.mult, A.add)
-    for nm, in_, by in (("ID", "ID", 1.0), ("KI", "ID", 4096.0), ("nKI", "ID", -4096.0), ("KSD", "SD", 4096.0)):
+    scale(1, 1, C("kw"), C("r0"), 60.0, C("kx"), ["c.r0", "c.kx"], ["c.kw"])
+    for nm, in_, by in (("ID", "ID", 1.0), ("KI", "ID", 2 * U), ("nKI", "ID", -2 * U), ("KW", "BO", "kw"), ("Fl", "BO", "fl"),
+                        ("BO", "BO", 1.0), ("BO3", "BO", "e3")):
         sc(Kb(nm), "b." + nm, in_, by)
+    for nm, in_, by in (("IDu", "ID", U), ("SDu", "SD", U), ("SUu", "SU", U), ("ID", "ID", 1.0), ("BOe", "BO", "e32"), ("Dm", "BO", "dm"),
+                        ("R0", "BO", "rb"), ("R15", "BO", 0.0), ("H2", "BO", 0.0)):
+        sc(Kh(nm), "h." + nm, in_, by, True)
+    for nm, k, by in (("R0", 0, "ra"), ("R15", 15, "e32"), ("H2", 0, "h2")):
+        vop(8, ["k.BO", "c." + by], ["h." + nm],
+            lambda nm=nm, k=k, by=by: V.tensor_scalar(kcol(T.kh, KH.index(nm), k), K8("BO"), C(by), None, A.mult))
     sc(K("A32"), "k.A32", "one", "a32")
 
     def inblock(out, otok, prim, a, b, tmp):
@@ -179,266 +206,176 @@ def build(g, T, topo, core, rank):
     inblock(K("t1"), "k.t1", "LT", -0.125, "cM", "t1")
     asel("t1", "t1", [[-1, 128]], A.not_equal, 2.0, 0, 1)
     sc(Kb("Mm"), "b.Mm", "t1", 1.0)
+    inblock(K("t4"), "k.t4", "LT", 63.0, 1.0, "t4")
+    asel("t4", "t4", [[-1, 128]], A.not_equal, -32.0, 0, 1)
+    sc(Kb("OH"), "b.OH", "t4", "rpos")
+    vop(8, [], ["b.OH"], lambda: V.memset(kcol(T.kb, KB.index("OH"), 0), 0.0))
     inblock(K("t2"), "k.t2", "LE", 32.0, -1.0, "t2")
     sc(Kb("Bm"), "b.Bm", "t2", "rpos")
-    bm = kb["Bm"] * 128
-    scale(8, 8, T.kb[:, bm:bm + 128:16], K8("BO"), C("c0"), 0.0, ["k.BO", "c.c0"], ["b.Bm"])
-    scale(8, 8, T.kb[:, bm + 15:bm + 128:16], K8("BO"), C("r0"), 0.0, ["k.BO", "c.r0"], ["b.Bm"])
-    vop(256, ["k.ID", "k.SD"], ["k.t0"], lambda: V.tensor_tensor(K("t0"), K("ID"), K("SD"), A.subtract))
-    sc(Kb("OH"), "b.OH", "t0", "mid")
-    sc(Kb("KIS"), "b.KIS", "t0", 4096.0)
-    inblock(Kb("Ld"), "b.Ld", "SD", "mid", "dLd", "t4")
+    scale(8, 8, kcol(T.kb, KB.index("Bm"), 0), K8("BO"), C("nr0"), 0.0, ["k.BO", "c.nr0"], ["b.Bm"])
+    scale(8, 8, kcol(T.kb, KB.index("Bm"), 15), K8("BO"), C("c0"), 0.0, ["k.BO", "c.c0"], ["b.Bm"])
+    inblock(Kb("Ld"), "b.Ld", "SD", "mid", "dLd", "t0")
     inblock(Kb("Vu"), "b.Vu", "ID", "mid", "hVu", "t2")
-    inblock(Kb("Qm"), "b.Qm", "LT", -8.5 * QS, 0.5 * QS, "t4")
-    for nm in ("ID", "SD", "SU", "BO"):
-        vop(128, ["k." + nm], ["h." + nm], lambda nm=nm: V.tensor_copy(Kh(nm), K(nm)))
-    sc(Kb("BOs"), "b.BOs", "BO", QS / 1024)
-    sc(Kb("BO"), "b.BO", "BO", 1.0)
-    if ABS_S:
-        sc(Kb("nID"), "b.nID", "ID", -1.0)
-    if CMP_S:
-        vop(CE // 2, [], ["SelL"], lambda: V.memset(T.SelL[:, :], -1.0))
-        vop(CL, [], ["SelL"], lambda: V.memset(T.SelL[:, 0:CE:16], 0.0))
-        gop(CE, ["SelL"], ["SelL"], lambda: g.affine_select(T.SelL[:, :], T.SelL[:, :], [[-1, CL], [0, 16]], A.is_equal, 0.0, 0, 1))
-    vop(128, ["k.BO"], ["h.BO3"], lambda: V.tensor_scalar(Kh("BO3"), K("BO"), 3232.0, None, A.mult))
-    vop(128, ["k.BO"], ["h.R0"], lambda: V.tensor_scalar(Kh("R0"), K("BO"), 0.0, None, A.mult))
-    vop(8, ["k.BO"], ["h.R0"], lambda: V.tensor_copy(T.kh[:, kh["R0"] * 128:(kh["R0"] + 1) * 128:16], K8("BO")))
-    vop(128, ["k.BO"], ["h.R15"], lambda: V.tensor_scalar(Kh("R15"), K("BO"), 0.0, None, A.mult))
-    vop(8, ["k.BO"], ["h.R15"], lambda: V.tensor_copy(T.kh[:, kh["R15"] * 128 + 15:(kh["R15"] + 1) * 128:16], K8("BO")))
-    gop(128, [], ["r.Qi"], lambda: g.iota(T.rQi[0:1, :], [[0, 8], [17, 16]], -15, 0, allow_small_or_imprecise_dtypes=True))
-    scale(128, 128, T.rQ[0:1, :], T.rQi[0:1, :], -QS / 2, 0.0, ["r.Qi"], ["r.Q"])
+    inblock(Kb("Qm"), "b.Qm", "LT", -8.5, 0.5, "t1")
+    vop(256, ["k.ID", "k.SD"], ["k.t0"], lambda: V.tensor_tensor(K("t0"), K("ID"), K("SD"), A.add))
+    sc(Kh("H1"), "h.H1", "t0", 0.5, True)
+    vop(256, ["k.ID", "k.SD"], ["k.t2"], lambda: V.tensor_tensor(K("t2"), K("ID"), K("SD"), A.subtract))
+    sc(K("H3"), "k.H3", "t2", 0.5)
     sel = lambda buf, k: buf[:, 16 - k:144 - k]
     vop(72, [], ["Sel"], lambda: V.memset(T.Sel[:, :], 0.0))
     scale(8, 8, T.Sel[:, 16:144:16], K8("BO"), 1.0, 0.0, ["k.BO"], ["Sel"])
     scale(72, 144, T.SelW[:, :], T.Sel[:, :], C("wf"), 0.0, ["Sel", "c.wf"], ["SelW"])
-    scale(72, 144, T.SelK[:, :], T.Sel[:, :], C("kw"), 0.0, ["Sel", "c.kw"], ["SelK"])
     scale(72, 144, T.SelN[:, :], T.Sel[:, :], -2.0, 0.0, ["Sel"], ["SelN"])
-    scale(16, 16, T.ln16b[:, 0:8], T.ln16[:, 0:8], 1.0, C("j16"), ["ln16", "c.j16"], ["ln16b"])
     scale(16, 16, T.ln32c[:, :], T.ln32[:, :], 1.0, C("j32"), ["ln32", "c.j32"], ["ln32c"])
-    rows = [("OH", 0.0, {1: 0.5, 15: 0.5}), ("Ld", 2.5, {0: 2.0, 1: 2.0}), ("e32", 2080.0, {}), ("Tu", -4096.0, {15: -6144.0}), ("Ts", -4096.0, {}), ("e15", 0.0, {15: 2080.0}), ("L2", 1441792.0, {}),
-            ("Td", -4096.0, {0: -8192.0}), ("Te", -8192.0, {0: -4096.0}), ("TdL", -2048.0, {0: -6144.0}), ("TeL", -6144.0, {0: -2048.0})]
+    gop(CL, [], ["cap"], lambda: g.iota(T.cap[:, :], [[0, NB], [-1, 16]], 15, 0, allow_small_or_imprecise_dtypes=True))
+    vop(CL, ["c.n"], ["cap"], lambda: V.tensor_scalar(T.cap[:, :], T.cap[:, :], C("n"), 65536.0, A.is_equal, A.mult))
     cr = {}
-    for i, (nm, val, ex) in enumerate(rows):
+    for i, (nm, val, ex) in enumerate([("Ld", 2.5, {0: 2.0, 1: 2.0}), ("Tu", -2 * U, {15: -3 * U})]):
         cr[nm] = T.crow[0:1, i * 128:(i + 1) * 128]
         vop(64, [], ["r." + nm], lambda nm=nm, val=val: V.memset(cr[nm], val))
-        if ex:
-            vops(len(ex), 8, [], ["r." + nm],
-                 lambda e, i=i, ex=ex: [V.memset(T.crow[0:1, i * 128 + kk:(i + 1) * 128:16], vv) for kk, vv in ex.items()])
-    one1 = T.kb[0:1, kb["one"] * 128:kb["one"] * 128 + CL]
-    PW = CE + 16
-    vops(NC, 16, [], ["Pz"], lambda e: [V.memset(T.P[:, c * PW + CE:(c + 1) * PW], 255.0) for c in range(NC)])
+        vops(len(ex), 8, [], ["r." + nm],
+             lambda e, i=i, ex=ex: [V.memset(T.crow[0:1, i * 128 + kk:(i + 1) * 128:16], vv) for kk, vv in ex.items()])
+    ob = KB.index("one") * 128
+    one1 = T.kb[0:1, ob:ob + CL]
     every = lambda n: [n + str(c) for c in range(NC)]
-    parts = lambda n, cs=range(NC): ["%s%d.%d" % (n, c, h) for c in cs for h in range(NH)]
-
-    vop(L, ["cin"], every("cn"), lambda: V.tensor_scalar(T.cn[:, :], T.cin[:, :], -2048.0, None, A.add))
-    scale(L // 2, L, T.yb[:, :], T.yin[:, :], 1.0, YB, ["yin"], parts("yb"))
-    mm(T.R[:, 0:2], [(Kb("Wm"), T.kb[:, kb["one"] * 128:kb["one"] * 128 + 2])], ["b.Wm", "b.one"], ["R0"], 0, n=2)
-    scale(1, 1, C("cU"), T.R[:, 0:1], -YB, 0.0, ["R0"], ["c.cU"], [0])
-
-    def gather(t, out_buf, base, off, c, otok, ftok):
-        X, xt = XX[t % 2]
-        for q in range(GP):
-            def fn(e, q=q):
-                o = out_buf[:, base + q * GL * 16:base + (q + 1) * GL * 16]
-                src = X[:, 0:W].indirect(off[:, c * CL + q * GL:c * CL + (q + 1) * GL])
-                return [V.tensor_copy(o, src) if e == "V" else S.activation(o, src, F.Copy)]
-            op({"V": (50, GL * 16, 0, 0, 1, 0), "S": (65, GL * 16, 0, 0, 1, 0)}, xt + [ftok], ["%s.%d" % (otok, q)], fn)
-
-    def index(c, Fp, ftok, bank, Lb, ltok, off, otok):
-        vop(CL, [ftok, ltok], ["va%d" % c], lambda: V.tensor_tensor(mcl(T.va, c), Fp, mcl(Lb, c), A.add), [bank])
-        vop(CL, ["va%d" % c], ["vb%d" % c], lambda: V.tensor_scalar(mcl(T.vb, c), mcl(T.va, c), 5, W - 1, A.arith_shift_right, A.bitwise_and))
-        vop(CL, ["vb%d" % c], [otok], lambda: V.tensor_copy(mcl(off, c), mcl(T.vb, c)))
 
     def tiles(c):
-        def B(i, h=None):
-            Bk, o = (T.B0, T.B1)[(c + SIDE[i]) % 2], ((c // 2) * 4 + i) * CL
-            return Bk[:, o:o + CL] if h is None else Bk[:, o + h * UC:o + (h + 1) * UC]
-        return B, (lambda i: "B%d.%d" % (c, i)), 5
+        return (lambda i, n=1: T["B%d" % c][:, i * CL:(i + n) * CL]), (lambda i: "B%d.%d" % (c, i))
 
-    def select(c, a, b, out, otok):
-        B, tk, bank = tiles(c)
-        vop(CL, [tk(a), "ts%d" % c], ["zz%d" % c], lambda: V.tensor_tensor(mcl(T.zz, c), mcl(T.ts, c), B(a), A.max), [bank])
-        vop(CL, [tk(b), "zz%d" % c], [otok], lambda: V.tensor_tensor(mcl(out, c), mcl(T.zz, c), B(b), A.max), [bank])
+    vop(L, ["cin"], every("cs"), lambda: V.tensor_scalar(T.cs[:, :], T.cin[:, :], 1 / U, -1.0, A.mult, A.add))
+    scale(L // 2, L, T.yb[:, :], T.yin[:, :], 1.0, YB, ["yin"], every("yb"))
+    x7 = T.B2[:, 7 * CL:7 * CL + 2]
+    mm(x7, [(Kb("Wm"), T.kb[:, ob:ob + 2])], ["b.Wm", "b.one"], ["B2.7"], n=2)
+    scale(1, 1, C("cU"), T.B2[:, 7 * CL:7 * CL + 1], -YB, 0.0, ["B2.7"], ["c.cU"])
+    for c in range(NC):
+        mm(tiles(c)[0](4), [(Kh("IDu"), mcl(T.cs, c))], ["h.IDu", "cs%d" % c], ["B%d.4" % c])
+
+    def gather(t, out, off, c, otok, ftok):
+        X, xt = XX[t % 2]
+        for h in range(2):
+            pick(out(2 * c + h), X[:, 0:W].indirect(off[:, c * CL + h * CL // 2:c * CL + (h + 1) * CL // 2]),
+                 HE, xt + [ftok], ["%s.%d" % (otok, h)])
+
+    def index(c, Fp, ftok, Lb, ltok, off, otok):
+        vop(CL, [ftok, ltok], ["va%d" % c], lambda: V.tensor_tensor(mcl(T.va, c), Fp, mcl(Lb, c), A.add))
+        vop(CL, ["va%d" % c], ["vb%d" % c], lambda: V.tensor_scalar(mcl(T.vb, c), mcl(T.va, c), 5, W - 1, A.arith_shift_right, A.bitwise_and))
+        vop(CL, ["vb%d" % c], [otok], lambda: V.tensor_copy(mcl(off, c), mcl(T.vb, c)))
 
     def engines(a):
         to = [T.cores[(T.rank_of(a) + 1 + t % (N - 1)) % N] for t in range(RO)]
         return [q for q in topo.engines(a, to[0]) if all(q in topo.engines(a, b) for b in to)]
 
-    def phase_p(t, c):
-        B, tk, bank = tiles(c)
+    def numbers(c):
+        B, tk = tiles(c)
         s = str(c)
         m = lambda buf: mcl(buf, c)
-        def numbers():
-            mm(B(1), [(Kb("Wm"), m(T.yb))], ["b.Wm"] + parts("yb", [c]), [tk(1)], bank)
-            vop(CL, [tk(1), "c.cU"], ["ui" + s], lambda: V.tensor_scalar(m(T.ui), B(1), C("cU"), None, A.add), [bank])
-            vop(CL, ["ui" + s], ["uu" + s], lambda: V.tensor_scalar(m(T.uu), m(T.ui), 2047, None, A.bitwise_and))
-            vop(CL, ["uu" + s], ["Ms" + s], lambda: V.tensor_scalar(m(T.Ms), m(T.uu), 2.0, 33.0, A.mult, A.add))
-            vop(CL, ["ui" + s], ["odd" + s], lambda: V.tensor_scalar(m(T.odd), m(T.ui), 1, None, A.bitwise_and))
-        if t == 0:
-            numbers()
-        scale(CL, CL, m(T.Ls), m(T.Ms), 2048.0, C("cA"), ["Ms" + s, "c.cA"], ["Ls" + s])
-        vop(2 * CL, ["cn" + s, "Ms" + s], [tk(1)], lambda: V.tensor_tensor(B(1), m(T.cn), m(T.Ms), A.mult), [bank])
-        index(c, B(1), tk(1), bank, T.Ls, "Ls" + s, T.off1, "off1" + s)
-        gather(t, T.P, c * PW, T.off1, c, "P" + s, "off1" + s)
-        r0 = (c * NU) % 2
-        onS = c in CMP_S
-        if onS:
-            top(1, 128, ["b.ID", "st%d" % min(t, 1)], ["PTp"],
-                lambda e: [Pm.transpose(T.PTp[0:CL, 0:128], mcl(T.stS, t * NC + c), Kb("ID"))], [4])
-            scale(64, 128, T.stT[0:CL, c * 128:(c + 1) * 128], T.PTp[0:CL, 0:128], 1.0, 0.0, ["PTp"], ["stT" + s], [4])
-        for h in range(NU):
-            u = c * NU + h
-            pp, pt, pb = ((T.PTp, "PTp", 4), (T.PTq, "PTq", 7))[u % 2]
-            top(8, 1024, ["b.ID"] + ["P%s.%d" % (s, q) for q in range(h * 64 // GL, (h + 1) * 64 // GL)], [pt],
-                lambda e, h=h, pp=pp: [Pm.transpose(m128(pp, b), T.P[:, c * PW + (8 * h + b) * 128:c * PW + (8 * h + b + 1) * 128], Kb("ID"))
-                                       for b in range(8)], [pb])
-            scale(512, 1024, T.PTs[:, u * 1024:(u + 1) * 1024], pp[:, :], 1.0, 0.0, [pt], ["PT%d" % u], [pb])
+        mm(B(2), [(Kb("Wm"), m(T.yb))], ["b.Wm", "yb" + s], [tk(2)])
+        vop(CL, [tk(2), "c.cU"], ["ui" + s], lambda: V.tensor_scalar(m(T.ui), B(2), C("cU"), None, A.add))
+        vop(CL, ["ui" + s], ["uu" + s], lambda: V.tensor_scalar(m(T.uu), m(T.ui), 2047, None, A.bitwise_and))
+        vop(CL, ["uu" + s], ["Ms" + s], lambda: V.tensor_scalar(m(T.Ms), m(T.uu), 2.0, 33.0, A.mult, A.add))
+        vop(CL, ["ui" + s], ["odd" + s], lambda: V.tensor_scalar(m(T.odd), m(T.ui), 1, None, A.bitwise_and))
 
-            def sums(e, h=h, u=u):
-                ins = []
-                for b in range(8):
-                    ins.append(Pm.matmul(m128(T.R, 8 * (r0 + h) + b), m128(T.PTs, 8 * u + b), Kb("Mm"), True, not onS))
-                    if onS:
-                        ins.append(Pm.matmul(m128(T.R, 8 * (r0 + h) + b), T.stT[0:CL, c * 128:(c + 1) * 128],
-                                             T.SelL[0:CL, (8 * h + b) * 128:(8 * h + b + 1) * 128], False, True))
-                return ins
-            top(8 + 8 * onS, 1024 + 1024 * onS, ["b.Mm", "PT%d" % u] + (["stT" + s, "SelL"] if onS else []), ["R%d" % (r0 + h)], sums,
-                [2 * (r0 + h), 2 * (r0 + h) + 1])
-        def judge(h):
-            u0 = r0 + h * UC // 64
-            RB = list(range(2 * u0, 2 * u0 + UC // 32))
-            RT = ["R%d" % (u0 + i) for i in range(UC // 64)]
-            Rk = lambda k: T.R[:, u0 * 1024 + k:u0 * 1024 + 16 * UC:16]
-            l0 = c * CL + h * UC
-            stv = T.stS[:, t * L + l0:t * L + l0 + UC]
-            Ik = lambda k: T.Ib[:, 16 * l0 + k * UC:16 * l0 + (k + 1) * UC]
-            scale(UC, UC, T.yb[:, l0:l0 + UC], Rk(0), 0.25, YB - 0.484375, RT, ["yb%s.%d" % (s, h)], RB)
-            if t < RO - 1:
-                scale(UC, UC, T.ez[:, l0:l0 + UC], Rk(0), 0.0625, WB - 1 + 1.0 / 256, RT, ["ez%s.%d" % (s, h)], RB)
-            if onS:
-                it = "I%s.%d." % (s, h)
-                vop(UC, RT + ["st%d" % min(t, 1)], [it + "a"], lambda: V.tensor_tensor(T.i0[:, l0:l0 + UC], Rk(0), stv, A.is_ge), RB)
-                sop(16 * UC, RT, [it + "0", it + "8"], lambda: S.activation(T.Ib[:, 16 * l0:16 * (l0 + UC)], T.R[:, u0 * 1024:u0 * 1024 + 16 * UC],
-                                                                         F.Sign, bias=0.0625), RB)
-                mm(B(0, h), [(sel(T.Sel, 0), T.i0[:, l0:l0 + UC])] + [(sel(T.Sel, k), T.Ib[:, 16 * l0 + k:16 * (l0 + UC):16]) for k in range(1, 16)],
-                   ["Sel", it + "a", it + "0"], [tk(0)], bank, n=UC)
-                return
-            for kq in range(0, 16, KQ):
-                it = "I%s.%d.%d" % (s, h, kq)
-                vops(KQ, UC, RT + ["st%d" % min(t, 1)], [it],
-                     lambda e, kq=kq: [V.tensor_tensor(Ik(k), Rk(k), stv, A.is_ge) for k in range(kq, kq + KQ)], RB)
-                mm(B(0, h), [(sel(T.Sel, k), Ik(k)) for k in range(kq, kq + KQ)], ["Sel", it], [tk(0)], bank, kq == 0, kq + KQ == 16, n=UC)
-        for h in range(NH):
-            judge(h)
-        sop(CL, [tk(0), "c.sE", "c.bE"], ["pw" + s],
-            lambda: S.activation(m(T.pw), B(0), F.Exp, bias=C("bE") if onS else -64.0, scale=C("sE") if onS else 8.0), [bank])
-        mm(B(1), [(Kb("Bm"), m(T.pw))], ["b.Bm", "pw" + s], [tk(1)], bank)
-        sop(CL, [tk(1), "c.thr"], ["sg" + s], lambda: S.activation(m(T.sg), B(1), F.Sign, bias=C("thr")), [bank])
-        sg, cn = m(T.sg), m(T.cn)
-        mm(B(2), [(Kb("OH"), sg), (cr["OH"], one1)], ["b.OH", "r.OH", "b.one", "sg" + s], [tk(2)], bank)
-        mm(B(0), [(Kb("Ld"), sg), (cr["Ld"], one1)], ["b.Ld", "r.Ld", "b.one", "sg" + s], [tk(0)], bank)
-        mm(B(3), [(Kb("Vu"), sg)], ["b.Vu", "sg" + s], [tk(3)], bank)
-        mi = t * NC + c
-        mt = "msg%d" % mi
-        ohc = mcl(T.msg, mi)
-        vop(CL, [tk(2), "cn" + s], [mt + "a"], lambda: V.tensor_tensor(ohc, cn, B(2), A.mult), [bank])
-        ov = T.offv[:, NB * c:NB * (c + 1)]
-        kB = (T.B0, T.B1)[(c + SIDE[2]) % 2][:, ((c // 2) * 4 + 2) * CL:((c // 2) * 4 + 2) * CL + NB]
-        mm(kB, [(sel(T.SelK, r), T.sg[:, c * CL + r:(c + 1) * CL:16]) for r in range(16)] + [(Kb("ID"), T.ln16b[:, 0:NB])],
-           ["SelK", "b.ID", "ln16b", "sg" + s], [tk(2)], bank, n=NB)
-        vop(NB, [tk(2)], ["offv" + s], lambda: V.tensor_scalar(ov, kB, 4104.0, float(CE), A.add, A.min), [bank])
-        win = T.P[:, c * PW:(c + 1) * PW].indirect(ov)
-        op({"V": (50, CL, 0, 0, 1, 0), "S": (65, CL, 0, 0, 1, 0)}, ["offv" + s, "Pz"] + ["P%s.%d" % (s, q) for q in range(GP)], [mt + "b"],
-           lambda e: [V.tensor_copy(mcl(T.msgv, mi), win) if e == "V" else S.activation(mcl(T.msgv, mi), win, F.Copy)])
+    def send(t, c, x, out, in_, rd):
         dst = T.cores[(rank + 1 + t % (N - 1)) % N]
         src = T.cores[(rank - 1 - t % (N - 1)) % N]
         rid, pid = topo.addr(dst)[0], topo.addr(dst)[1]
         mask, far = engines(core), engines(src)
-        for x, out, in_ in (("a", T.land, T.msg), ("b", T.landv, T.msgv)):
-            sem = "arr%d%s" % (mi, x)
-            op({"G": (0, 0, 0, 0, 0, 0.3)}, [mt + x], ["land%d%s" % (mi, x)],
-               lambda e, out=out, in_=in_, sem=sem: [g.remote_dma(mcl(out, mi), mcl(in_, mi), T.sem[sem], T.sem.sent, pid, rid, sum(1 << q for q in mask))],
-               lat="far", sem=(sem, len(far)))
-            ops[-1]["sent"] = len(mask)
-        vop(CL, [tk(0), "odd" + s], ["nmd" + s], lambda: V.tensor_tensor(m(T.nmd), m(T.odd), B(0), A.is_lt), [bank])
-        sop(CL, [tk(3), "c.bVu"], ["mu" + s, "cnt" + s],
-            lambda: S.activation(m(T.mu), B(3), F.Relu, bias=C("bVu"), accum_out=T.cnt[:, c:c + 1]), [bank])
-        mm(B(1), [(cr["e15"], one1), (Kh("R15"), ohc)], ["h.R15", "r.e15", "b.one", mt + "a"], [tk(1)], bank)
-        vop(CL, [tk(1), "uu" + s], ["fa" + s], lambda: V.tensor_tensor(m(T.fa), m(T.uu), B(1), A.mult), [bank])
+        sem = "arr%d%s" % (t * NC + c, x)
+        op({"G": (0, 0, 0, 0, 0, 0.3)}, rd, ["land%d%s" % (t * NC + c, x)],
+           lambda e: [g.remote_dma(out, in_, T.sem[sem], T.sem.sent, pid, rid, sum(1 << q for q in mask))], lat="far", sem=(sem, len(far)))
+        ops[-1]["sent"] = len(mask)
+
+    def phase_p(t, c):
+        B, tk = tiles(c)
+        s = str(c)
+        m = lambda buf: mcl(buf, c)
+        scale(CL, CL, m(T.Ls), m(T.Ms), 2048.0, C("cA"), ["Ms" + s, "c.cA"], ["Ls" + s])
+        vop(CL, [tk(4), "Ms" + s], [tk(3)], lambda: V.tensor_tensor(B(3), B(4), m(T.Ms), A.mult))
+        if t:
+            vop(CL, [tk(4)], ["cs" + s], lambda: V.tensor_scalar(m(T.cs), B(4), 1 / U, None, A.mult))
+        index(c, B(3), tk(3), T.Ls, "Ls" + s, T.off1, "off1" + s)
+        gather(t, lambda h: T.P[:, h * HE:(h + 1) * HE], T.off1, c, "P" + s, "off1" + s)
+        for h in range(2):
+            pp, pt = (T.Pa, T.Pb)[h], ("Pa", "Pb")[h]
+            o = c * CE + h * HE
+            top(4, 512, ["b.ID", "P%s.%d" % (s, h)], [pt],
+                lambda e, o=o, pp=pp: [Pm.transpose(m128(pp, b), T.P[:, o + b * 128:o + (b + 1) * 128], Kb("ID")) for b in range(4)])
+            scale(HE // 2, HE, T.PTs[:, o:o + HE], pp[:, 0:HE], 1.0, 0.0, [pt], ["PT%s.%d" % (s, h)])
+            top(4, 512, ["b.Mm", "PT%s.%d" % (s, h)], ["R%d" % h],
+                lambda e, o=o, h=h: [Pm.matmul(m128(T.R, 4 * h + b), T.PTs[:, o + b * 128:o + (b + 1) * 128], Kb("Mm"), True, True) for b in range(4)])
+        RT = ["R0", "R1"]
+        Rk = lambda k: T.R[:, k:CE:16]
+        stv = mcl(T.stS, t * NC + c)
+        Ik = lambda k: T.Ib[:, c * CE + k * CL:c * CE + (k + 1) * CL]
+        for kq in range(0, 16, KQ):
+            it = "I%s.%d" % (s, kq)
+            vops(KQ, CL, RT + ["st%d" % min(t, 1)], [it],
+                 lambda e, kq=kq: [V.tensor_tensor(Ik(k), Rk(k), stv, A.is_ge) for k in range(kq, kq + KQ)])
+            mm(B(0), [(sel(T.Sel, k), Ik(k)) for k in range(kq, kq + KQ)], ["Sel", it], [tk(0)], kq == 0, kq + KQ == 16)
+        scale(CL, CL, m(T.yb), Rk(0), 0.25, YB - 0.484375, RT, ["yb" + s])
+        sop(CL, [tk(0)], ["pw" + s], lambda: S.activation(m(T.pw), B(0), F.Exp, bias=-64.0, scale=8.0))
+        top(2, 2 * CL, ["b.OH", "b.Bm", "pw" + s], [tk(1), tk(2)],
+            lambda e: [Pm.matmul(B(1), Kb("OH"), m(T.pw), True, True), Pm.matmul(B(2), Kb("Bm"), m(T.pw), True, True)])
+        sop(2 * CL, [tk(1), tk(2), "c.thr"], ["sg" + s], lambda: S.activation(m128(T.sg, c), B(1, 2), F.Sign, bias=C("thr")))
+        noh, sg, cs = mcl(T.sg, 2 * c), mcl(T.sg, 2 * c + 1), m(T.cs)
+        mi = t * NC + c
+        mt = "msg%d" % mi
+        ohc, mu = mcl(T.msg, mi), mcl(T.msgv, 2 * mi + 1)
+        vop(CL, ["sg" + s, "cs" + s], [mt + "a"], lambda: V.tensor_tensor(ohc, cs, noh, A.max))
+        send(t, c, "a", mcl(T.land, mi), ohc, [mt + "a"])
+        mm(B(3), [(T.kb[0:1, ob:ob + 128], T.ramp[0:1, :]), (Kb("KW"), noh)], ["b.KW", "b.one", "ramp", "sg" + s], [tk(3)])
+        vop(CL, [tk(3), "cap"], ["sc" + s], lambda: V.tensor_tensor_scan(m(T.sc), T.cap[:, :], B(3), 0.0, A.add, A.min))
+        ov = T.offv[:, NB * c:NB * (c + 1)]
+        vop(NB, ["sc" + s], ["offv" + s], lambda: V.tensor_copy(ov, T.sc[:, c * CL + 15:(c + 1) * CL:16]))
+        pick(mcl(T.msgv, 2 * mi), T.P[:, c * CE:(c + 1) * CE].indirect(ov), CL, ["offv" + s, "P%s.0" % s, "P%s.1" % s], [mt + "b"])
+        mm(B(4), [(Kb("Vu"), sg)], ["b.Vu", "sg" + s], [tk(4)])
+        sop(CL, [tk(4), "c.bVu"], [mt + "c", "cnt" + s], lambda: S.activation(mu, B(4), F.Relu, bias=C("bVu"), accum_out=T.cnt[:, c:c + 1]), 0.07)
+        send(t, c, "b", m128(T.landv, mi), m128(T.msgv, mi), [mt + "b", mt + "c"])
+        mm(B(0), [(cr["Ld"], one1), (Kb("Ld"), sg)], ["b.Ld", "r.Ld", "b.one", "sg" + s], [tk(0)])
+        vop(CL, [tk(0), "odd" + s], ["md" + s], lambda: V.tensor_tensor(m(T.md), m(T.odd), B(0), A.is_ge))
+        mm(B(5), [(Kh("R15"), ohc)], ["h.R15", mt + "a"], [tk(5)])
+        vop(CL, [tk(5), "uu" + s], ["fa" + s], lambda: V.tensor_tensor(m(T.fa), m(T.uu), B(5), A.mult))
         vop(CL, ["fa" + s], ["fb" + s], lambda: V.tensor_scalar(m(T.fb), m(T.fa), 5, 4095, A.arith_shift_right, A.bitwise_and))
-        mm(B(0), [(Kh("ID"), cn), (cr["Ts"], one1), (Kb("KI"), m(T.nmd)), (Kb("nKI"), m(T.mu))],
-           ["h.ID", "b.KI", "b.nKI", "r.Ts", "b.one", "cn" + s, "nmd" + s, "mu" + s], [tk(0)], bank)
-        mm(B(2), [(Kh("SD"), cn), (Kh("R0"), ohc), (Kb("nKI"), m(T.nmd))],
-           ["h.SD", "h.R0", "b.nKI", "cn" + s, "nmd" + s, mt + "a"], [tk(2)], bank)
-        mm(B(3), [(Kh("SU"), cn), (cr["Tu"], one1), (Kb("KI"), m(T.mu))],
-           ["h.SU", "b.KI", "r.Tu", "b.one", "cn" + s, "mu" + s], [tk(3)], bank)
-        vop(CL, [tk(3), "fb" + s], ["ts" + s], lambda: V.tensor_tensor(m(T.ts), m(T.fb), B(3), A.add), [bank])
-        select(c, 2, 0, T.cn, "cn" + s)
+        mm(B(4), [(Kh("SUu"), cs), (cr["Tu"], one1), (Kb("KI"), mu)], ["h.SUu", "b.KI", "r.Tu", "b.one", "cs" + s, mt + "c"], [tk(4)])
+        mm(B(0), [(Kh("IDu"), cs), (Kb("nKI"), mu), (Kb("nKI"), m(T.md))], ["h.IDu", "b.nKI", "cs" + s, "md" + s, mt + "c"], [tk(0)])
+        mm(B(1), [(Kh("SDu"), cs), (Kh("R0"), ohc), (Kb("KI"), m(T.md))], ["h.SDu", "h.R0", "b.KI", "cs" + s, "md" + s, mt + "a"], [tk(1)])
+        vop(CL, [tk(4), "fb" + s], ["ts" + s], lambda: V.tensor_tensor(m(T.ts), m(T.fb), B(4), A.add))
+        vop(CL, [tk(0), "ts" + s], ["zz" + s], lambda: V.tensor_tensor(m(T.zz), m(T.ts), B(0), A.max))
+        vop(CL, [tk(1), "zz" + s], ["cn" + s], lambda: V.tensor_tensor(m(T.cn), m(T.zz), B(1), A.max))
         if t < RO - 1:
-            numbers()
+            numbers(c)
 
     def phase_q(t, c):
-        B, tk, bank = tiles(c)
+        B, tk = tiles(c)
         s = str(c)
         m = lambda buf: mcl(buf, c)
         mi = t * NC + c
         lt, lw = "land%da" % mi, "land%db" % mi
-        le, lv = mcl(T.land, mi), mcl(T.landv, mi)
-        mm(B(1), [(Kh("BO"), le), (cr["e32"], one1)], ["h.BO", "r.e32", "b.one", lt], [tk(1)], bank)
-        mm(B(2), [(Kh("BO3"), le), (cr["L2"], one1)], ["h.BO3", "r.L2", "b.one", lt], [tk(2)], bank)
-        vop(CL, ["cn" + s, tk(1)], ["L2" + s], lambda: V.tensor_tensor(m(T.L2), m(T.cn), B(1), A.mult), [bank])
-        index(c, B(2), tk(2), bank, T.L2, "L2" + s, T.off2, "off2" + s)
-        gather(t, T.x2, c * CE, T.off2, c, "x2" + s, "off2" + s)
-
-        def near(h, part):
-            l0 = c * CL + h * UC
-            xt = ["x2%s.%d" % (s, q) for q in range(h * UC // GL, (h + 1) * UC // GL)]
-            xk = lambda k: T.x2[:, 16 * l0 + k:16 * (l0 + UC):16]
-            mk = lambda k: T.mx[:, 16 * l0 + k * UC:16 * l0 + (k + 1) * UC]
-            vv = T.landv[:, mi * CL + h * UC:mi * CL + (h + 1) * UC]
-            if c in ABS_S:
-                u0 = (c * NU) % 2 + h * UC // 64
-                RB = list(range(2 * u0, 2 * u0 + UC // 32))
-                RT = ["R%d" % (u0 + i) for i in range(UC // 64)]
-                dk = lambda k: T.R[:, u0 * 1024 + k * UC:u0 * 1024 + (k + 1) * UC]
-                top(32, 32 * UC, ["b.ID", "b.nID", lw] + xt, RT,
-                    lambda e: [x for k in range(16) for x in (Pm.matmul(dk(k), Kb("ID"), xk(k), True, False),
-                                                              Pm.matmul(dk(k), Kb("nID"), vv, False, True))], RB)
-                it = ["mx%s.%d.%d" % (s, h, kq) for kq in range(0, 16, KQ)]
-                sop(16 * UC, RT, it, lambda: S.activation(T.mx[:, 16 * l0:16 * (l0 + UC)], T.R[:, u0 * 1024:u0 * 1024 + 16 * UC], F.Abs, scale=0.5), RB)
-                mm(B(0, h), [(E8, T.thS[0:8, l0:l0 + UC])] + [(sel(T.SelN, k), mk(k)) for k in range(16)],
-                   ["b.E8", "th", "SelN"] + it, [tk(0)], bank, n=UC)
-                return
-            vi = (c * NH + h) % 2
-            vh, vt = T.R[:, vi * 1024:vi * 1024 + UC], "R%d" % vi
-            if part == 0:
-                mm(vh, [(Kb("ID"), vv)], ["b.ID", lw], [vt], 2 * vi, n=UC)
-                mm(B(0, h), [(sel(T.Sel, k), xk(k)) for k in range(16)], ["Sel"] + xt, [tk(0)], bank, False, False, n=UC)
-                return
-            for kq in range(0, 16, KQ):
-                it = "mx%s.%d.%d" % (s, h, kq)
-                vops(KQ, UC, xt + [vt], [it], lambda e, kq=kq: [V.tensor_tensor(mk(k), xk(k), vh, A.max) for k in range(kq, kq + KQ)], [2 * vi])
-                mm(B(0, h), [(sel(T.SelN, k), mk(k)) for k in range(kq, kq + KQ)], ["SelN", it], [tk(0)], bank, False,
-                   kq + KQ == 16 and h == NH - 1, n=UC)
-        mm(B(0), [(E8, T.thS[0:8, c * CL:(c + 1) * CL]), (Kb("BO"), lv)], ["b.E8", "th", "b.BO", lw], [tk(0)], bank, True, False)
-        for part in range(2):
-            for h in range(NH):
-                near(h, part)
-        sop(CL, [tk(0)], ["eta" + s], lambda: S.activation(m(T.eta), B(0), F.Sign, bias=0.5), [bank])
-        mm(B(1), [(T.rQ[0:1, :], one1), (Kb("BOs"), lv), (Kb("Qm"), m(T.eta))], ["b.Qm", "b.BOs", "r.Q", "b.one", "eta" + s, lw], [tk(1)], bank)
-        sop(CL, [tk(1)], ["qq" + s], lambda: S.activation(m(T.qq), B(1), F.Sign, scale=-1.0), [bank])
-        cn, qq = m(T.cn), m(T.qq)
-        z = "L" if t == RO - 1 else ""
-        vop(CL, [tk(1), "cn" + s], ["ts" + s], lambda: V.tensor_tensor(m(T.ts), cn, B(1), A.min), [bank])
-        if z:
-            scale(CL, CL, m(T.ts), m(T.ts), 1.0, 2048.0, ["ts" + s], ["ts" + s])
-        mm(B(2), [(Kh("SD"), cn), (cr["Td" + z], one1), (Kb("KSD"), qq)], ["h.SD", "b.KSD", "r.Td" + z, "b.one", "cn" + s, "qq" + s], [tk(2)], bank)
-        mm(B(3), [(Kh("BO"), le), (cr["Te" + z], one1), (Kb("KIS"), qq)], ["h.BO", "b.KIS", "r.Te" + z, "b.one", lt, "qq" + s], [tk(3)], bank)
-        if z:
-            select(c, 2, 3, T.ycS, "yc" + s)
+        le, lv, lg = mcl(T.land, mi), mcl(T.landv, 2 * mi), mcl(T.landv, 2 * mi + 1)
+        top(2, 2 * CL, ["h.BOe", "b.BO3", lt], [tk(3), tk(5)],
+            lambda e: [Pm.matmul(B(3), Kh("BOe"), le, True, True), Pm.matmul(B(5), Kb("BO3"), le, True, True)])
+        vop(CL, ["cn" + s, tk(3)], ["L2" + s], lambda: V.tensor_tensor(m(T.L2), m(T.cn), B(3), A.mult))
+        index(c, B(5), tk(5), T.L2, "L2" + s, T.off2, "off2" + s)
+        gather(t, lambda h: T.x2[:, h * HE:(h + 1) * HE], T.off2, c, "x2" + s, "off2" + s)
+        mm(B(6), [(Kh("ID"), m(T.cn)), (Kh("Dm"), le)], ["h.ID", "h.Dm", "cn" + s, lt], [tk(6)])
+        xt = ["x2%s.0" % s, "x2%s.1" % s]
+        xk = lambda k: T.x2[:, c * CE + k:(c + 1) * CE:16]
+        mk = lambda k: T.mx[:, c * CE + k * CL:c * CE + (k + 1) * CL]
+        mm(B(1), [(E8, T.thS[0:8, c * CL:(c + 1) * CL]), (Kb("BO"), lv)] + [(sel(T.Sel, k), xk(k)) for k in range(16)],
+           ["b.E8", "th", "b.BO", lw, "Sel"] + xt, [tk(1)], True, False)
+        for kq in range(0, 16, KQ):
+            it = "mx%s.%d" % (s, kq)
+            ks = range(kq, kq + KQ)
+            vops(KQ, CL, xt + [lw], [it], lambda e, ks=ks: [V.tensor_tensor(mk(k), xk(k), lv, A.max) for k in ks])
+            mm(B(1), [(sel(T.SelN, k), mk(k)) for k in ks], ["SelN", it], [tk(1)], False, kq + KQ == 16)
+        sop(CL, [tk(1)], ["eta" + s], lambda: S.activation(m(T.eta), B(1), F.Sign, bias=0.5))
+        mm(B(0), [(Kb("Fl"), lg), (Kb("Qm"), m(T.eta))], ["b.Qm", "b.Fl", "eta" + s, lw], [tk(0)])
+        sop(CL, [tk(0), "c.bQ"], ["qq" + s], lambda: S.activation(m(T.qq), B(0), F.Sign, bias=C("bQ")))
+        vop(CL, [tk(6), "qq" + s], ["qd" + s], lambda: V.tensor_tensor(m(T.qd), m(T.qq), B(6), A.mult))
+        mm(B(4), [(Kh("H1"), m(T.cn)), (Kh("H2"), le), (K("H3"), m(T.qd))], ["h.H1", "h.H2", "k.H3", "cn" + s, lt, "qd" + s], [tk(4)], more=3)
+        if t == RO - 1:
+            scale(CL, CL, m(T.ycS), B(4), 1.0, U, [tk(4)], ["yc" + s])
             dma("Y", mcl(T.yc, c), m(T.ycS), ["yc" + s], ["o.yc" + s], "oc" + s, 2.0)
-        else:
-            select(c, 2, 3, T.cn, "cn" + s)
 
     def scatter(t, to):
         X, xt = XX[to]
@@ -446,24 +383,29 @@ def build(g, T, topo, core, rank):
         vop(0, ["nx%d" % p, "offr%d" % p], xt,
             lambda: V.tensor_copy(X[:, 0:W].indirect(T.offr[:, 16 * p:16 * p + 16]), T.nx[:, p * L:(p + 1) * L]), sc=L)
 
+    for c in range(NC):
+        numbers(c)
     for t in range(RO):
         p = t % 2
         if t < RO - 1:
-            mm(T.R[:, 1024:1040], [(sel(T.SelW, r), T.yb[:, r:L:16]) for r in range(16)], ["SelW"] + parts("yb"), ["R1"], 2, n=16)
-            vop(16, ["R1", "c.cU"], ["ra"], lambda: V.tensor_scalar(T.ra[:, :], T.R[:, 1024:1040], C("cU"), None, A.add), [2])
+            r7 = T.B0[:, 7 * CL:7 * CL + 16]
+            mm(r7, [(sel(T.SelW, r), T.yb[:, r:L:16]) for r in range(16)], ["SelW"] + every("yb"), ["B0.7"], n=16)
+            vop(16, ["B0.7", "c.cU"], ["ra"], lambda: V.tensor_scalar(T.ra[:, :], r7, C("cU"), None, A.add))
             vop(16, ["ra"], ["rb"], lambda: V.tensor_scalar(T.rb[:, :], T.ra[:, :], 31, None, A.bitwise_and))
             vop(32, ["rb", "ln32c"], ["rc"], lambda: V.tensor_tensor(T.rc[:, :], T.rb[:, :], T.ln32c[:, :], A.add))
             vop(16, ["rc"], ["offr%d" % p], lambda p=p: V.tensor_copy(T.offr[:, 16 * p:16 * p + 16], T.rc[:, :]))
         for c in range(NC):
             phase_p(t, c)
         if t == RO - 1:
-            scale(L // 2, L, T.yyS[:, :], T.yb[:, :], 1.0, -YB, parts("yb"), ["yy"])
+            scale(L // 2, L, T.yyS[:, :], T.yb[:, :], 1.0, -YB, every("yb"), ["yy"])
             dma("Y", T.yy[:, :], T.yyS[:, :], ["yy"], ["o.yy"], "oy", 2.0)
         else:
-            mm(T.R[:, 1538:1538 + NC], [(K("A32"), T.cnt[:, :])], ["k.A32", "R1"] + every("cnt"), ["s.cnt"], 3, n=256)
-            vop(1, ["s.cnt", "R1"], ["cs"], lambda: V.tensor_reduce(T.cs[:, :], T.R[:, 1538:1538 + NC], AxisListType.X, A.add), [3])
-            scale(1, 1, C("cA"), T.cs[:, :], 1.0, -262144.0, ["cs"], ["c.cA"])
-            vop(0, XX[p][1] + ["offr%d" % p] + parts("ez"), ["Wn"],
+            a7 = T["B%d" % (NC - 1)][:, 7 * CL:7 * CL + NC]
+            at = "B%d.7" % (NC - 1)
+            mm(a7, [(K("A32"), T.cnt[:, :])], ["k.A32"] + every("cnt"), [at], n=256)
+            sop(NC, [at], ["c.cA"], lambda: S.activation(T.cj[:, :], a7, F.Identity, bias=-262144.0 / NC, accum_out=C("cA")), 0.07)
+            scale(L // 1, L, T.ez[:, :], T.yb[:, :], 0.25, WB - YB / 4 - 0.875, every("yb"), ["ez"])
+            vop(0, XX[p][1] + ["offr%d" % p, "ez"], ["Wn"],
                 lambda p=p: V.tensor_tensor(T.Wn[:, :], XX[p][0][:, 0:W].indirect(T.offr[:, 16 * p:16 * p + 16]), T.ez[:, :], A.add), ga=L)
             scale(L // 2, L, T.nx[:, p * L:(p + 1) * L], T.Wn[:, :], 0.5, -WB / 2, ["Wn"], ["nx%d" % p])
             if TWO:
@@ -493,6 +435,17 @@ def depend(ops):
         for k in o["wr"]:
             lastw[k] = i
             readers[k] = []
+    whole, closed = {}, {}
+    for i, o in enumerate(ops):
+        if o["eng"] == "T":
+            b = o["banks"][0]
+            if o["grp"] == 1:
+                deps[i] = sorted(set(deps[i]) | set(whole.pop(b, [])))
+            elif o["grp"] == 2:
+                closed[b] = i
+            elif o["grp"] == 3:
+                deps[i] = sorted(set(deps[i]) | ({closed[b]} if b in closed else set()))
+                whole.setdefault(b, []).append(i)
     return deps
 
 
@@ -500,48 +453,67 @@ def way(o, P):
     return P["far"] if o["lat"] == "far" else o["lat"] + (0.06 if o["eng"] == "T" else 0.0)
 
 
-def lay(ops, deps, succ, pri, pick, hold, P):
+def after(xs, t):
+    k = len(xs)
+    while k and xs[k - 1] > t:
+        k -= 1
+    return k
+
+
+def place(ops, pre, succ, cst, key, lat, price, t00):
     n = len(ops)
-    lat = P["lat"]
-    left = [len(deps[i]) + len(ops[i]["soft"]) for i in range(n)]
-    t0 = [0.0] * n
-    ready = [i for i in range(n) if not left[i]]
-    free = {e: 0.0 for e in "VSTGY"}
-    bank = [("", 0.0)] * 8
-    opened = set()
-    order, start = [], [0.0] * n
+    left = [len(p) for p in pre]
+    ready = [(key[i], i) for i in range(n) if not left[i]]
+    es = {e: ([], []) for e in "VSTGY"}
+    bs = [([], [], []) for _ in range(8)]
+    st, fin, pick = [0.0] * n, [0.0] * n, [""] * n
     while ready:
-        cand = []
-        for i in ready:
-            o, e = ops[i], pick[i]
-            if o["grp"] & 1 and o["banks"][0] in opened:
-                continue
-            t1 = max(t0[i] + hold[i], free[e])
-            for b in o["banks"]:
-                if bank[b][0] != e and bank[b][1] + lat > t1:
-                    t1 = bank[b][1] + lat
-            cand.append((t1, i))
-        tm = min(cand)[0] + 0.05
-        t1, i = max((c for c in cand if c[0] <= tm), key=lambda c: pri[c[1]])
-        o, e = ops[i], pick[i]
-        start[i] = t1
-        free[e] = t1 + cost(o, e, P)
-        for b in o["banks"]:
-            bank[b] = (e, free[e])
-        if o["grp"] == 1:
-            opened.add(o["banks"][0])
-        if o["grp"] == 2:
-            opened.discard(o["banks"][0])
-        order.append(i)
-        ready.remove(i)
-        f = free[e] + way(o, P)
-        for j, hard in succ[i]:
-            if hard:
-                t0[j] = max(t0[j], f + (0.0 if e == "T" and pick[j] == "T" else lat))
+        x = min(ready)
+        ready.remove(x)
+        i = x[1]
+        t0 = t00[i]
+        for j, gap in pre[i]:
+            if fin[j] + gap > t0:
+                t0 = fin[j] + gap
+        best = None
+        for e in ops[i]["eng"]:
+            c, t = cst[i][e], t0
+            S, Fn = es[e]
+            while True:
+                k = after(Fn, t)
+                while k < len(S) and S[k] < t + c - 1e-9:
+                    t = max(t, Fn[k])
+                    k += 1
+                t1 = t
+                for b in ops[i]["banks"]:
+                    s, f, w = bs[b]
+                    k = after(f, t - lat)
+                    while k < len(s) and s[k] < t + c + lat - 1e-9:
+                        if w[k] != e and f[k] + lat > t:
+                            t = f[k] + lat
+                        k += 1
+                if t == t1:
+                    break
+            v = t + c + price[i][e == "S"] * c
+            if best is None or v < best[0]:
+                best = (v, t, e, c)
+        v, t, e, c = best
+        st[i], fin[i], pick[i] = t, t + c, e
+        S, Fn = es[e]
+        k = after(Fn, t)
+        S.insert(k, t)
+        Fn.insert(k, t + c)
+        for b in ops[i]["banks"]:
+            s, f, w = bs[b]
+            k = after(s, t)
+            s.insert(k, t)
+            f.insert(k, t + c)
+            w.insert(k, e)
+        for j in succ[i]:
             left[j] -= 1
             if not left[j]:
-                ready.append(j)
-    return order, start
+                ready.append((key[j], j))
+    return st, fin, pick
 
 
 def replay(ops, deps, order, pick, P):
@@ -582,74 +554,62 @@ def replay(ops, deps, order, pick, P):
 
 def plan(ops, deps, tries=TRIES, swaps=SWAPS):
     n = len(ops)
-    succ = [[] for _ in range(n)]
-    for i in range(n):
-        for d in deps[i]:
-            succ[d].append((i, True))
-        for d in ops[i]["soft"]:
-            succ[d].append((i, False))
-    free = [i for i in range(n) if len(ops[i]["eng"]) > 1]
-    seed = [12345]
+    seed = [SEED]
 
     def rnd():
         seed[0] = (seed[0] * 1103515245 + 12345) % 2147483648
         return seed[0] / 2147483648.0
+    P = MID
+    lat = P["lat"]
+    cst = [{e: cost(o, e, P) for e in o["eng"]} for o in ops]
+    ways = [way(o, P) for o in ops]
+    fore, back = [[] for _ in range(n)], [[] for _ in range(n)]
+    for i in range(n):
+        for d, gap in [(d, ways[d] + (0.0 if ops[i]["eng"] == "T" == ops[d]["eng"] else lat)) for d in deps[i]] + [(d, 0.0) for d in ops[i]["soft"]]:
+            fore[i].append((d, gap))
+            back[d].append((i, gap))
+    pre, succ = [[j for j, x in p] for p in fore], [[j for j, x in p] for p in back]
 
-    def score(pick, noise, hold):
-        pri = [0.0] * n
-        for i in range(n - 1, -1, -1):
-            pri[i] = cost(ops[i], pick[i], FIG) + way(ops[i], FIG) + max([pri[j] + FIG["lat"] for j, h in succ[i]], default=0.0)
-        order, start = lay(ops, deps, succ, [pri[i] + noise[i] for i in range(n)], pick, hold, FIG)
-        res = [replay(ops, deps, order, pick, P) for P in FIGS]
-        return sum(r[0] for r in res) / len(FIGS), order, start, [b for r in res for b in r[1]]
-    pick = [o["eng"][-1] if o["rd"] not in (["PTp"], ["PTq"]) else "V" for o in ops]
-    noise, hold = [EARLY if o["wr"][0][:2] in ("k.", "b.", "h.", "c.", "r.", "Se", "ln") else 0.0 for o in ops], [0.0] * n
-    cur = best = score(pick, noise, hold) + (pick,)
+    def both(key, price, rounds):
+        best = None
+        for k in range(rounds):
+            st, fin, pick = place(ops, fore, succ, cst, key, lat, price, [0.0] * n)
+            end = max(fin[i] + ways[i] for i in range(n))
+            if best is None or end < best[0]:
+                best = (end, st, pick, price)
+            if k < rounds - 1:
+                key = [-f for f in place(ops, back, pre, cst, [-f for f in fin], lat, price, ways)[1]]
+        return best
+    pri = [0.0] * n
+    for i in range(n - 1, -1, -1):
+        pri[i] = min(cst[i].values()) + max([pri[j] + x for j, x in back[i]], default=ways[i])
+    cur = best = both([-p for p in pri], [PRICE] * n, 10)
+    free = [i for i in range(n) if len(ops[i]["eng"]) > 1 and max(cst[i].values()) > 0.2]
     for it in range(tries):
-        p2, n2, h2 = list(pick), list(noise), list(hold)
-        for r in range(1 + int(rnd() * 2)):
-            x = rnd()
-            i, j = cur[3][int(rnd() * len(cur[3]))]
-            if x < 0.3:
-                c = [k for k in (i, j) if len(ops[k]["eng"]) > 1] or [free[int(rnd() * len(free))]]
-                k = c[int(rnd() * len(c))]
-                p2[k] = "V" if p2[k] == "S" else "S"
-            elif x < 0.55:
-                h2[j] += rnd() * 0.8
-            elif x < 0.75:
-                n2[i] += rnd() * 4
-                n2[j] -= rnd() * 4
-            elif x < 0.85:
-                k = free[int(rnd() * len(free))]
-                p2[k] = "V" if p2[k] == "S" else "S"
-            elif x < 0.92:
-                k = int(rnd() * n)
-                h2[k] = n2[k] = 0.0
-            else:
-                a, d = int(rnd() * n), (rnd() - 0.5) * 8
-                for k in range(a, min(n, a + int(rnd() * 60))):
-                    n2[k] += d
-        s2 = score(p2, n2, h2)
-        if s2[0] <= cur[0] + 0.6 * rnd() * rnd() * (1 - it / tries):
-            cur, pick, noise, hold = s2 + (p2,), p2, n2, h2
+        key, price, x = list(cur[1]), cur[3], rnd()
+        if x < 0.3:
+            price = list(price)
+            for r in range(1 + int(3 * rnd())):
+                price[free[int(rnd() * len(free))]] = ((0, 50), (50, 0), PRICE)[int(rnd() * 3)]
+        elif x < 0.7:
+            a, d = int(rnd() * n), (rnd() - 0.5) * 4
+            for k in range(a, min(n, a + 1 + int(rnd() * 40))):
+                key[k] += d
+        else:
+            a, w = rnd() * cur[0], rnd() * 6
+            for k in range(n):
+                if a <= key[k] < a + w:
+                    key[k] += rnd() - 0.5
+        s2 = both(key, price, 2)
+        if s2[0] <= cur[0] + 0.5 * rnd() * rnd() * (1 - it / tries):
+            cur = s2
             if cur[0] < best[0]:
                 best = cur
-    pre = [list(deps[i]) + ops[i]["soft"] for i in range(n)]
 
     def rate(order, pick):
-        opened = set()
-        for i in order:
-            o = ops[i]
-            if o["grp"]:
-                if o["grp"] & 1 and o["banks"][0] in opened:
-                    return None
-                if o["grp"] == 1:
-                    opened.add(o["banks"][0])
-                if o["grp"] == 2:
-                    opened.discard(o["banks"][0])
         res = [replay(ops, deps, order, pick, P) for P in FIGS]
         return sum(r[0] / w for r, w in zip(res, base)), [b for r in res for b in r[1]]
-    order, pick = best[1], best[4]
+    order, pick = sorted(range(n), key=lambda i: (best[1][i], i)), best[2]
     base = [replay(ops, deps, order, pick, P)[0] * len(FIGS) / best[0] for P in FIGS]
     cur = rate(order, pick)
     top = (cur[0], order, pick)
@@ -685,7 +645,7 @@ def plan(ops, deps, tries=TRIES, swaps=SWAPS):
             cur, order, pick = s2, o2, p2
             if cur[0] < top[0]:
                 top = (cur[0], order, pick)
-    return top[1], top[2], best[2], top[0]
+    return top[1], top[2]
 
 
 PLAN = {}

@@ -12,38 +12,40 @@ YB, WB = 160.0, 320.0
 U = 2048.0
 
 f32, bf, f16, i32, u16 = "float32", "bfloat16", "float16", "int32", "uint16"
-K32 = ["one", "t0", "BO", "ID", "LT", "LE", "SD", "SU", "A32", "H3", "t1", "t2", "t3", "t4"]
-KB = ["ID", "Mm", "OH", "Bm", "KW", "Ld", "Vu", "Qm", "Fl", "KI", "nKI", "Wm", "E8", "one", "BO", "BO3"]
-KH = ["ID", "IDu", "SDu", "SUu", "R0", "R15", "BOe", "Dm", "H1", "H2"]
+KB = ["one", "t0", "BO", "ID", "LT", "LE", "SD", "SU", "t1", "t2", "E8", "t4", "Mm", "OH", "Bm", "KW", "Ld", "Vu", "Qm", "Fl", "KI", "nKI",
+      "Wm", "BO3", "IDu", "SDu", "SUu", "R0", "Dm", "H1", "H2", "H3", "Um", "Sm"]
+KH, KF = ["R15", "BOe"], ["A32"]
 SCRATCH = {n: ("sbuf", [128, w], d) for n, w, d in [
     ("XA", W, bf), ("XB", W if TWO else 16, bf), ("cin", L, i32), ("stS", RO * L, bf), ("yin", L, bf), ("wS", 1, bf), ("thS", L, bf),
     ("cn", L, f16), ("cs", L, f16), ("yb", L, bf), ("ycS", L, f32), ("yyS", L, bf), ("P", 16 * L, bf),
-    ("PTs", 16 * L, bf), ("Ib", 16 * L, bf), ("mx", 16 * L, bf),
+    ("PTs", 16 * L, bf), ("Ib", 16 * L, bf),
     ("ui", L, i32), ("uu", L, i32), ("odd", L, i32), ("Ls", L, f32), ("L2", L, f32), ("va", L, i32), ("vb", L, i32),
     ("off1", L, u16), ("off2", L, u16), ("offv", NC * NB, u16), ("offr", 32, u16), ("sc", L, f32), ("cap", CL, f32),
     ("pw", L, bf), ("sg", 2 * L, bf), ("md", L, bf), ("fa", L, i32), ("fb", L, i32), ("Ms", L, f32),
-    ("ts", L, f32), ("zz", L, f32), ("eta", L, bf), ("qq", L, bf), ("qd", L, f32), ("ez", L, f32), ("Wn", L, bf), ("nx", 2 * L, bf),
-    ("ra", 16, i32), ("rb", 16, i32), ("rc", 16, i32), ("cnt", NC, f32), ("cj", NC, f32), ("col", 32, f32),
-    ("msg", RO * L, f16), ("land", RO * L, f16), ("msgv", 2 * RO * L, bf), ("landv", 2 * RO * L, bf), ("x2", 16 * L, bf),
-    ("k32", len(K32) * 128, f32), ("kb", len(KB) * 128, bf), ("kh", len(KH) * 128, f16),
-    ("Sel", 144, bf), ("SelN", 144, bf), ("SelW", 144, bf),
+    ("ts", L, f32), ("zz", L, f32), ("eta", L, bf), ("qq", L, bf), ("qd", 2 * L, f16), ("ez", L, f32), ("Wn", L, bf), ("nx", 2 * L, bf),
+    ("ra", 16, i32), ("rb", 16, i32), ("rc", 16, i32), ("cnt", NC, f32), ("cj", NC, f32), ("col", 40, f32),
+    ("msg", RO * L, f16), ("land", RO * L, f16), ("msgv", 2 * RO * L, bf), ("landv", 2 * RO * L, bf),
+    ("kf", len(KF) * 128, f32), ("kb", len(KB) * 128, bf), ("kh", len(KH) * 128, f16),
+    ("Sel", 144, bf), ("SelN", 144, bf), ("su", L, f32),
     ("crow", 2 * 128, bf), ("ramp", CL, bf), ("ln32", 16, f32), ("ln32c", 16, f32)]}
-SCRATCH.update({"R": ("psum", [128, 1024], f32), "Pa": ("psum", [128, 1024], bf), "Pb": ("psum", [128, 1024], bf)})
+SCRATCH.update({"R": ("psum", [128, 1024], f32), "Pa": ("psum", [128, HE, 2], bf), "Pb": ("psum", [128, HE, 2], bf)})
+SCRATCH.update({n: ("sbuf", [128, 8 * L, 2], bf) for n in ("x2", "mx")})
 SCRATCH.update({"B%d" % c: ("psum", [128, 512], f32) for c in range(NC)})
 SEMAPHORES = (["sV", "sS", "sT", "sG", "sent", "dX0", "dX1", "dXB", "dc", "dst0", "dst1", "dy", "dw", "dth", "oy"]
               + ["oc%d" % c for c in range(NC)] + ["arr%d%s" % (i, x) for i in range(RO * NC) for x in "ab"])
 
-FIG = dict(cy=0.00083, ga=1.56, sc=3.8, pe=0.00042, lat=0.18, ov=0.005, far=3.0)
-FIGS = [FIG, dict(FIG, lat=0.08, ov=0.025), dict(FIG, cy=0.0011, pe=0.00055, ga=1.2, sc=2.5, lat=0.15, ov=0.01, far=4.0),
-        dict(FIG, cy=0.0011, pe=0.00055, ga=1.9, sc=5.0, far=4.0)]
-MID = dict(FIG, lat=0.15, ov=0.012)
-TRIES, SWAPS, HEAT, SEED = 1500, 4000, 0.3, 12345
+FIG = dict(cy=0.00083, ga=1.56, sc=3.8, pe=0.00042, lat=0.18, ov=0.005, far=2.8, out=0.5, load=8.0)
+FIGS = [FIG, dict(FIG, cy=0.00112, pe=0.00056, ga=1.3, sc=2.5, lat=0.18, far=3.2, out=1.1, load=7.0),
+        dict(FIG, cy=0.0009, pe=0.00074, ga=1.6, sc=5.0, lat=0.2, far=3.5, out=0.9, load=9.0), dict(FIG, cy=0.001, pe=0.0005, ga=1.9, lat=0.29, ov=0.01, far=4.5, out=0.8)]
+MID = dict(FIG, cy=0.00096, pe=0.00056, lat=0.24, far=3.3, out=0.8, load=7.5)
+SIZE = (91.0, 108.0, 104.0, 124.0)
+TRIES, SWAPS, HEAT, SEED = 4600, 7000, 0.3, 12345
 PRICE = (4.0, 2.5)
 
 
 def cost(o, e, P):
     cy, ga, sc, pe, k, fix = o["c"][e]
-    return (cy + ga * P["ga"] + sc * P["sc"]) * P["cy"] + pe * P["pe"] + k * P["ov"] * (0.5 if e == "T" else 1) + fix
+    return (cy + ga * P["ga"] + sc * P["sc"]) * P["cy"] + pe * P["pe"] + k * P["ov"] * (0.5 if e == "T" else 1) + P.get(fix, fix)
 
 
 def bank_of(tok):
@@ -58,14 +60,19 @@ def bank_of(tok):
 
 def build(g, T, topo, core, rank):
     ops = []
+    at = [None, 0]
+
+    def part(name):
+        at[:] = [name, len(ops)]
     V, S, Pm = g.vector, g.scalar, g.tensor
 
     def op(c, rd, wr, fn, lat=0.0, sem=None, grp=0):
         banks = []
+        rd = ["k." + k[2:] if k[:2] in ("b.", "h.") else k for k in rd]
         for k in list(wr) + list(rd):
             if bank_of(k) is not None and bank_of(k) not in banks:
                 banks.append(bank_of(k))
-        ops.append(dict(eng="".join(c), c=c, rd=list(rd), wr=list(wr), fn=fn, banks=banks, lat=lat, sem=sem, grp=grp, soft=[]))
+        ops.append(dict(eng="".join(c), c=c, rd=list(rd), wr=list(wr), fn=fn, banks=banks, lat=lat, sem=sem, grp=grp, soft=[], at=(at[0], len(ops) - at[1])))
 
     def vop(n, rd, wr, fn, ga=0, sc=0):
         op({"V": (max(64, n) if n else 60, ga, sc, 0, 1, 0)}, rd, wr, lambda e: [fn()])
@@ -111,37 +118,35 @@ def build(g, T, topo, core, rank):
     def m128(buf, i):
         return buf[:, i * 128:(i + 1) * 128]
 
-    def mcl(buf, i):
-        return buf[:, i * CL:(i + 1) * CL]
+    def mcl(buf, i, n=1):
+        return buf[:, i * CL:(i + n) * CL]
 
     dma("Y", T.yin[:, :], T.y0[:, :], [], ["yin"], "dy", 2.0)
     dma("Y", T.wS[:, :], T.w[:, :], [], ["wS"], "dw", 2.0)
     dma("Y", T.cin[:, :], T.c0[:, :], [], ["cin"], "dc", 2.0)
-    dma("S", T.XA[:, 0:W // 2], T.x0[:, 0:W // 2], [], ["XA0"], "dX0", 8.0)
-    dma("Y", T.XA[:, W // 2:W], T.x0[:, W // 2:W], [], ["XA1"], "dX1", 8.0)
-    dma("Y", T.stS[:, 0:L], T.st[:, 0:L], [], ["st0"], "dst0", 8.5)
-    dma("Y", T.thS[0:8, :], T.th[:, :], [], ["th"], "dth", 8.5)
-    dma("Y", T.stS[:, L:RO * L], T.st[:, L:RO * L], [], ["st1"], "dst1", 9.0)
+    dma("S", T.XA[:, 0:W // 2], T.x0[:, 0:W // 2], [], ["XA0"], "dX0", "load")
+    dma("Y", T.XA[:, W // 2:W], T.x0[:, W // 2:W], [], ["XA1"], "dX1", "load")
+    dma("Y", T.stS[:, 0:L], T.st[:, 0:L], [], ["st0"], "dst0", "load")
+    dma("Y", T.thS[0:8, :], T.th[:, :], [], ["th"], "dth", "load")
+    dma("Y", T.stS[:, L:RO * L], T.st[:, L:RO * L], [], ["st1"], "dst1", 11.0)
     XX = [(T.XA, ["XA0", "XA1"])] * 2
     if TWO:
         dma("Y", T.XB[:, :], T.x0[:, :], ["XA0", "XA1"], ["XB0", "XB1"], "dXB", 8.0)
         XX[1] = (T.XB, ["XB0", "XB1"])
 
-    cols = {n: i for i, n in enumerate(["n", "r0", "r15", "cM", "rpos", "s", "mid", "c0", "dLd", "hVu", "kw", "kx", "thr", "bVu", "bQ", "e4",
-                                        "j32", "a32", "wf", "cU", "cA", "nr0", "fl", "e32", "e3", "dm", "h2", "ra", "rb", "dif"])}
-    K = lambda n: m128(T.k32, K32.index(n))
-    Kb = lambda n: m128(T.kb, KB.index(n))
-    Kh = lambda n: m128(T.kh, KH.index(n))
+    cols = {n: i for i, n in enumerate(["n", "r0", "r15", "cM", "rpos", "s", "mid", "c0", "dLd", "hVu", "kw", "thr", "bVu", "bQ", "e4",
+                                        "j32", "a32", "wf", "cU", "cA", "nr0", "e32", "e3", "dm", "h2", "ra", "rb", "dif", "kx", "fl",
+                                        "bv", "kp", "uv", "u15"])}
+    home = lambda n: (T.kh, KH.index(n)) if n in KH else (T.kf, KF.index(n)) if n in KF else (T.kb, KB.index(n))
+    K = lambda n: m128(*home(n))
     C = lambda n: T.col[:, cols[n]:cols[n] + 1]
-    K8 = lambda n: T.k32[:, K32.index(n) * 128:(K32.index(n) + 1) * 128:16]
-    kcol = lambda buf, i, k: buf[:, i * 128 + k:(i + 1) * 128:16]
+    kcol = lambda n, k=0: home(n)[0][:, home(n)[1] * 128 + k:(home(n)[1] + 1) * 128:16]
     top8 = lambda buf, i: buf[0:8, i * 128:(i + 1) * 128]
 
-    vop(128, [], ["k.one"], lambda: V.memset(K("one"), 1.0))
+    vop(64, [], ["k.one"], lambda: V.memset(K("one"), 1.0))
 
     def asel(out, in_, pat, cmp, fill, base, cm, view=m128):
-        gop(128, ["k." + in_], ["k." + out],
-            lambda: g.affine_select(view(T.k32, K32.index(out)), view(T.k32, K32.index(in_)), pat, cmp, fill, base, cm))
+        gop(128, ["k." + in_], ["k." + out], lambda: g.affine_select(view(*home(out)), view(*home(in_)), pat, cmp, fill, base, cm))
     asel("t0", "one", [[-16, 8], [0, 16]], A.is_ge, 0.0, 0, 1)
     asel("BO", "t0", [[16, 8], [0, 16]], A.is_ge, 0.0, 15, -1)
     asel("LT", "BO", [[1, 128]], A.is_ge, 0.0, -1, -1)
@@ -150,11 +155,10 @@ def build(g, T, topo, core, rank):
     asel("SD", "BO", [[1, 128]], A.is_equal, 0.0, -1, -1)
     asel("SU", "BO", [[1, 128]], A.is_equal, 0.0, 1, -1)
     gop(CL, [], ["ramp"], lambda: g.iota(T.ramp[0:1, :], [[16, CL]], 0, 0, allow_small_or_imprecise_dtypes=True))
-    asel("t3", "one", [[1, 128]], A.is_ge, 0.0, 0, -16, top8)
-    asel("t3", "t3", [[-1, 128]], A.is_ge, 0.0, 15, 16, top8)
-    E8 = top8(T.kb, KB.index("E8"))
-    scale(128, 128, E8, top8(T.k32, K32.index("t3")), 1.0, 0.0, ["k.t3"], ["b.E8"])
-    vop(256, ["k.LT", "k.ID"], ["k.LE"], lambda: V.tensor_tensor(K("LE"), K("LT"), K("ID"), A.add))
+    asel("E8", "one", [[1, 128]], A.is_ge, 0.0, 0, -16, top8)
+    asel("E8", "E8", [[-1, 128]], A.is_ge, 0.0, 15, 16, top8)
+    E8 = top8(*home("E8"))
+    vop(128, ["k.LT", "k.ID"], ["k.LE"], lambda: V.tensor_tensor(K("LE"), K("LT"), K("ID"), A.add))
 
     def cts(out, in_, s1, s2, o0, o1=None):
         if o1 is None:
@@ -162,16 +166,16 @@ def build(g, T, topo, core, rank):
         else:
             scale(1, 1, C(out), C(in_), s1, s2, ["c." + in_], ["c." + out])
 
-    def sc(out, otok, in_, by, half=False):
+    def sc(out, in_, by, k=None):
         col = isinstance(by, str)
         rd = ["k." + in_] + (["c." + by] if col else [])
-        if half:
-            vop(128, rd, [otok], lambda: V.tensor_scalar(out, K(in_), C(by) if col else by, None, A.mult))
+        o, i = (K(out), K(in_)) if k is None else (kcol(out, k), kcol(in_))
+        if out in KH:
+            vop(64, rd, ["k." + out], lambda: V.tensor_scalar(o, i, C(by) if col else by, None, A.mult))
         else:
-            scale(128, 128, out, K(in_), C(by) if col else by, 0.0, rd, [otok])
+            scale(128 if out in KF else 64, 128 if k is None else 8, o, i, C(by) if col else by, 0.0, rd, ["k." + out])
     scale(1, 1, C("wf"), T.wS[:, :], 1.0, 0.0, ["wS"], ["c.wf"])
-    sc(Kb("Wm"), "b.Wm", "BO", "wf")
-    vop(64, [], ["b.one"], lambda: V.memset(Kb("one"), 1.0))
+    sc("Wm", "BO", "wf")
     vop(1, [], ["c.cA"], lambda: V.memset(C("cA"), -262144.0))
     vop(128, ["k.LT"], ["c.n"], lambda: V.tensor_reduce(C("n"), K("LT"), AxisListType.X, A.add))
     cts("r0", "n", 15.0, None, A.is_equal)
@@ -182,59 +186,60 @@ def build(g, T, topo, core, rank):
     row0 = lambda by, add: (add - 15 * by, by)
     for out, in_, (a, b) in (("cM", "n", (0.125, 0.125)), ("rpos", "r0", (-1.0, 1.0)), ("mid", "s", (-0.5, 0.5)), ("c0", "r0", (-101.0, 1.0)),
                              ("nr0", "r0", (-1.0, 0.0)), ("thr", "e4", (1.0, -1.0)), ("dLd", "s", (-1.0, 0.0)), ("hVu", "dif", (-0.5, 0.0)),
-                             ("bVu", "dif", (0.5, -0.5)), ("kx", "n", (0.5, -7.5)), ("bQ", "n", (8.5, 180.0)), ("fl", "r15", (-300.0, 0.0)),
+                             ("bv", "r15", (0.5, -0.5)), ("kp", "r0", (-2 * U, 2 * U)), ("uv", "r15", (2 * U, 0.0)), ("kx", "n", (0.5, -7.5)), ("bQ", "n", (8.5, 180.0)), ("fl", "r15", (-300.0, 0.0)),
                              ("j32", "n", (-32.0, 480.0)), ("a32", "r15", (32.0, 0.0)), ("e32", "r0", row0(U, U + 32)),
                              ("e3", "r0", row0(3232 * U, 1441792.0)), ("dm", "r0", row0(-U, 0.0)), ("h2", "r0", row0(U / 2, 0.0)),
                              ("ra", "r0", row0(U, -2 * U)), ("rb", "r0", (-2 * U, 0.0))):
         cts(out, in_, a, b, A.mult, A.add)
-    scale(1, 1, C("kw"), C("r0"), 60.0, C("kx"), ["c.r0", "c.kx"], ["c.kw"])
-    for nm, in_, by in (("ID", "ID", 1.0), ("KI", "ID", 2 * U), ("nKI", "ID", -2 * U), ("KW", "BO", "kw"), ("Fl", "BO", "fl"),
-                        ("BO", "BO", 1.0), ("BO3", "BO", "e3")):
-        sc(Kb(nm), "b." + nm, in_, by)
-    for nm, in_, by in (("IDu", "ID", U), ("SDu", "SD", U), ("SUu", "SU", U), ("ID", "ID", 1.0), ("BOe", "BO", "e32"), ("Dm", "BO", "dm"),
-                        ("R0", "BO", "rb"), ("R15", "BO", 0.0), ("H2", "BO", 0.0)):
-        sc(Kh(nm), "h." + nm, in_, by, True)
+    for out, by, add in (("kw", 60.0, "kx"), ("bVu", 1.5, "bv"), ("u15", -3 * U, "uv")):
+        scale(1, 1, C(out), C("r0"), by, C(add), ["c.r0", "c." + add], ["c." + out])
+    for nm, in_, by in (("KI", "ID", 2 * U), ("nKI", "ID", -2 * U), ("KW", "BO", "kw"), ("Fl", "BO", "fl"), ("BO3", "BO", "e3"),
+                        ("IDu", "ID", U), ("SDu", "SD", U), ("SUu", "SU", U), ("BOe", "BO", "e32"), ("Dm", "BO", "dm"),
+                        ("R0", "BO", "rb"), ("R15", "BO", 0.0), ("H2", "BO", 0.0), ("A32", "one", "a32")):
+        sc(nm, in_, by)
     for nm, k, by in (("R0", 0, "ra"), ("R15", 15, "e32"), ("H2", 0, "h2")):
-        vop(8, ["k.BO", "c." + by], ["h." + nm],
-            lambda nm=nm, k=k, by=by: V.tensor_scalar(kcol(T.kh, KH.index(nm), k), K8("BO"), C(by), None, A.mult))
-    sc(K("A32"), "k.A32", "one", "a32")
+        sc(nm, "BO", by, k)
 
-    def inblock(out, otok, prim, a, b, tmp):
+    def inblock(out, prim, a, b):
         cv = lambda x: C(x) if isinstance(x, str) else x
-        scale(128, 128, K(tmp), K(prim), cv(a), cv(b), ["k." + prim] + ["c." + x for x in (a, b) if isinstance(x, str)], ["k." + tmp])
-        vop(256, ["k." + tmp, "k.BO"], [otok], lambda: V.tensor_tensor(out, K(tmp), K("BO"), A.mult))
-    inblock(K("t1"), "k.t1", "LT", -0.125, "cM", "t1")
-    asel("t1", "t1", [[-1, 128]], A.not_equal, 2.0, 0, 1)
-    sc(Kb("Mm"), "b.Mm", "t1", 1.0)
-    inblock(K("t4"), "k.t4", "LT", 63.0, 1.0, "t4")
+        scale(64, 128, K(out), K(prim), cv(a), cv(b), ["k." + prim] + ["c." + x for x in (a, b) if isinstance(x, str)], ["k." + out])
+        vop(128, ["k.BO"], ["k." + out], lambda: V.tensor_tensor(K(out), K(out), K("BO"), A.mult))
+    inblock("Mm", "LT", -0.125, "cM")
+    asel("Mm", "Mm", [[-1, 128]], A.not_equal, 2.0, 0, 1)
+    inblock("t4", "LT", 63.0, 1.0)
     asel("t4", "t4", [[-1, 128]], A.not_equal, -32.0, 0, 1)
-    sc(Kb("OH"), "b.OH", "t4", "rpos")
-    vop(8, [], ["b.OH"], lambda: V.memset(kcol(T.kb, KB.index("OH"), 0), 0.0))
-    inblock(K("t2"), "k.t2", "LE", 32.0, -1.0, "t2")
-    sc(Kb("Bm"), "b.Bm", "t2", "rpos")
-    scale(8, 8, kcol(T.kb, KB.index("Bm"), 0), K8("BO"), C("nr0"), 0.0, ["k.BO", "c.nr0"], ["b.Bm"])
-    scale(8, 8, kcol(T.kb, KB.index("Bm"), 15), K8("BO"), C("c0"), 0.0, ["k.BO", "c.c0"], ["b.Bm"])
-    inblock(Kb("Ld"), "b.Ld", "SD", "mid", "dLd", "t0")
-    inblock(Kb("Vu"), "b.Vu", "ID", "mid", "hVu", "t2")
-    inblock(Kb("Qm"), "b.Qm", "LT", -8.5, 0.5, "t1")
-    vop(256, ["k.ID", "k.SD"], ["k.t0"], lambda: V.tensor_tensor(K("t0"), K("ID"), K("SD"), A.add))
-    sc(Kh("H1"), "h.H1", "t0", 0.5, True)
-    vop(256, ["k.ID", "k.SD"], ["k.t2"], lambda: V.tensor_tensor(K("t2"), K("ID"), K("SD"), A.subtract))
-    sc(K("H3"), "k.H3", "t2", 0.5)
+    sc("OH", "t4", "rpos")
+    sc("OH", "BO", 0.0, 0)
+    inblock("t2", "LE", 32.0, -1.0)
+    sc("Bm", "t2", "rpos")
+    sc("Bm", "BO", "nr0", 0)
+    sc("Bm", "BO", "c0", 15)
+    inblock("Ld", "SD", "mid", "dLd")
+    inblock("Vu", "ID", "mid", "hVu")
+    sc("Vu", "BO", 0.0, 0)
+    inblock("Um", "ID", "kp", "rb")
+    sc("Um", "BO", "u15", 15)
+    sc("Sm", "nKI", "rpos")
+    inblock("Qm", "LT", -8.5, 0.5)
+    vop(128, ["k.ID", "k.SD"], ["k.t0"], lambda: V.tensor_tensor(K("t0"), K("ID"), K("SD"), A.add))
+    sc("H1", "t0", 0.5)
+    vop(128, ["k.ID", "k.SD"], ["k.t1"], lambda: V.tensor_tensor(K("t1"), K("ID"), K("SD"), A.subtract))
+    sc("H3", "t1", 0.5)
+    Kb = Kh = K
     sel = lambda buf, k: buf[:, 16 - k:144 - k]
     vop(72, [], ["Sel"], lambda: V.memset(T.Sel[:, :], 0.0))
-    scale(8, 8, T.Sel[:, 16:144:16], K8("BO"), 1.0, 0.0, ["k.BO"], ["Sel"])
-    scale(72, 144, T.SelW[:, :], T.Sel[:, :], C("wf"), 0.0, ["Sel", "c.wf"], ["SelW"])
+    scale(8, 8, T.Sel[:, 16:144:16], kcol("BO"), 1.0, 0.0, ["k.BO"], ["Sel"])
     scale(72, 144, T.SelN[:, :], T.Sel[:, :], -2.0, 0.0, ["Sel"], ["SelN"])
     scale(16, 16, T.ln32c[:, :], T.ln32[:, :], 1.0, C("j32"), ["ln32", "c.j32"], ["ln32c"])
     gop(CL, [], ["cap"], lambda: g.iota(T.cap[:, :], [[0, NB], [-1, 16]], 15, 0, allow_small_or_imprecise_dtypes=True))
-    vop(CL, ["c.n"], ["cap"], lambda: V.tensor_scalar(T.cap[:, :], T.cap[:, :], C("n"), 65536.0, A.is_equal, A.mult))
+    vop(CL, ["c.n"], ["cap"], lambda: V.tensor_scalar(T.cap[:, :], T.cap[:, :], C("n"), 2.0 ** 25, A.is_equal, A.mult))
     cr = {}
-    for i, (nm, val, ex) in enumerate([("Ld", 2.5, {0: 2.0, 1: 2.0}), ("Tu", -2 * U, {15: -3 * U})]):
+    for i, (nm, val, ex) in enumerate([("Ld", 2.5, {0: 2.0, 1: 2.0}), ("up", 16384.0, {})]):
         cr[nm] = T.crow[0:1, i * 128:(i + 1) * 128]
         vop(64, [], ["r." + nm], lambda nm=nm, val=val: V.memset(cr[nm], val))
-        vops(len(ex), 8, [], ["r." + nm],
-             lambda e, i=i, ex=ex: [V.memset(T.crow[0:1, i * 128 + kk:(i + 1) * 128:16], vv) for kk, vv in ex.items()])
+        if ex:
+            vops(len(ex), 8, [], ["r." + nm],
+                 lambda e, i=i, ex=ex: [V.memset(T.crow[0:1, i * 128 + kk:(i + 1) * 128:16], vv) for kk, vv in ex.items()])
     ob = KB.index("one") * 128
     one1 = T.kb[0:1, ob:ob + CL]
     every = lambda n: [n + str(c) for c in range(NC)]
@@ -256,20 +261,25 @@ def build(g, T, topo, core, rank):
             pick(out(2 * c + h), X[:, 0:W].indirect(off[:, c * CL + h * CL // 2:c * CL + (h + 1) * CL // 2]),
                  HE, xt + [ftok], ["%s.%d" % (otok, h)])
 
-    def index(c, Fp, ftok, Lb, ltok, off, otok):
+    def index(c, Fp, ftok, Lb, ltok, off, otok, n=1):
         vop(CL, [ftok, ltok], ["va%d" % c], lambda: V.tensor_tensor(mcl(T.va, c), Fp, mcl(Lb, c), A.add))
         vop(CL, ["va%d" % c], ["vb%d" % c], lambda: V.tensor_scalar(mcl(T.vb, c), mcl(T.va, c), 5, W - 1, A.arith_shift_right, A.bitwise_and))
-        vop(CL, ["vb%d" % c], [otok], lambda: V.tensor_copy(mcl(off, c), mcl(T.vb, c)))
+        vops(n, CL, ["vb%d" % c], [otok], lambda e: [V.tensor_copy(off[:, c * CL + i * CL // n:c * CL + (i + 1) * CL // n], T.vb[:, c * CL + i:(c + 1) * CL:n])
+                                                     for i in range(n)])
 
     def engines(a):
         to = [T.cores[(T.rank_of(a) + 1 + t % (N - 1)) % N] for t in range(RO)]
         return [q for q in topo.engines(a, to[0]) if all(q in topo.engines(a, b) for b in to)]
 
-    def numbers(c):
+    def numbers(t, c):
         B, tk = tiles(c)
         s = str(c)
         m = lambda buf: mcl(buf, c)
-        mm(B(2), [(Kb("Wm"), m(T.yb))], ["b.Wm", "yb" + s], [tk(2)])
+        if t < RO - 1:
+            mm(B(2), [(cr["up"], T.ramp[0:1, :]), (Kb("Wm"), m(T.yb))], ["r.up", "ramp", "b.Wm", "yb" + s], [tk(2)])
+            vop(CL, [tk(2), "cap"], ["su" + s], lambda: V.tensor_tensor_scan(m(T.su), T.cap[:, :], B(2), 0.0, A.add, A.min))
+        else:
+            mm(B(2), [(Kb("Wm"), m(T.yb))], ["b.Wm", "yb" + s], [tk(2)])
         vop(CL, [tk(2), "c.cU"], ["ui" + s], lambda: V.tensor_scalar(m(T.ui), B(2), C("cU"), None, A.add))
         vop(CL, ["ui" + s], ["uu" + s], lambda: V.tensor_scalar(m(T.uu), m(T.ui), 2047, None, A.bitwise_and))
         vop(CL, ["uu" + s], ["Ms" + s], lambda: V.tensor_scalar(m(T.Ms), m(T.uu), 2.0, 33.0, A.mult, A.add))
@@ -281,7 +291,7 @@ def build(g, T, topo, core, rank):
         rid, pid = topo.addr(dst)[0], topo.addr(dst)[1]
         mask, far = engines(core), engines(src)
         sem = "arr%d%s" % (t * NC + c, x)
-        op({"G": (0, 0, 0, 0, 0, 0.3)}, rd, ["land%d%s" % (t * NC + c, x)],
+        op({"G": (0, 0, 0, 0, 0, "out")}, rd, ["land%d%s" % (t * NC + c, x)],
            lambda e: [g.remote_dma(out, in_, T.sem[sem], T.sem.sent, pid, rid, sum(1 << q for q in mask))], lat="far", sem=(sem, len(far)))
         ops[-1]["sent"] = len(mask)
 
@@ -289,18 +299,20 @@ def build(g, T, topo, core, rank):
         B, tk = tiles(c)
         s = str(c)
         m = lambda buf: mcl(buf, c)
-        scale(CL, CL, m(T.Ls), m(T.Ms), 2048.0, C("cA"), ["Ms" + s, "c.cA"], ["Ls" + s])
+        if c < 2:
+            cs_ = [0] if c == 0 else list(range(1, NC))
+            scale(len(cs_) * CL, len(cs_) * CL, mcl(T.Ls, c, len(cs_)), mcl(T.Ms, c, len(cs_)), 2048.0, C("cA"),
+                  ["Ms%d" % i for i in cs_] + ["c.cA"], ["Ls%d" % i for i in cs_])
         vop(CL, [tk(4), "Ms" + s], [tk(3)], lambda: V.tensor_tensor(B(3), B(4), m(T.Ms), A.mult))
-        if t:
-            vop(CL, [tk(4)], ["cs" + s], lambda: V.tensor_scalar(m(T.cs), B(4), 1 / U, None, A.mult))
+        vop(CL, [tk(4)], ["cs" + s], lambda: V.tensor_scalar(m(T.cs), B(4), 1 / U, None, A.mult)) if t else at.append(at.pop() - 1)
         index(c, B(3), tk(3), T.Ls, "Ls" + s, T.off1, "off1" + s)
         gather(t, lambda h: T.P[:, h * HE:(h + 1) * HE], T.off1, c, "P" + s, "off1" + s)
         for h in range(2):
             pp, pt = (T.Pa, T.Pb)[h], ("Pa", "Pb")[h]
             o = c * CE + h * HE
             top(4, 512, ["b.ID", "P%s.%d" % (s, h)], [pt],
-                lambda e, o=o, pp=pp: [Pm.transpose(m128(pp, b), T.P[:, o + b * 128:o + (b + 1) * 128], Kb("ID")) for b in range(4)])
-            scale(HE // 2, HE, T.PTs[:, o:o + HE], pp[:, 0:HE], 1.0, 0.0, [pt], ["PT%s.%d" % (s, h)])
+                lambda e, o=o, pp=pp: [Pm.transpose(pp[:, 64 * b:64 * b + 64, :], T.P[:, o + b * 128:o + (b + 1) * 128], Kb("ID")) for b in range(4)])
+            scale(HE // 2, HE, T.PTs[:, o:o + HE], pp[:, 0:HE // 2, :], 1.0, 0.0, [pt], ["PT%s.%d" % (s, h)])
             top(4, 512, ["b.Mm", "PT%s.%d" % (s, h)], ["R%d" % h],
                 lambda e, o=o, h=h: [Pm.matmul(m128(T.R, 4 * h + b), T.PTs[:, o + b * 128:o + (b + 1) * 128], Kb("Mm"), True, True) for b in range(4)])
         RT = ["R0", "R1"]
@@ -323,27 +335,27 @@ def build(g, T, topo, core, rank):
         ohc, mu = mcl(T.msg, mi), mcl(T.msgv, 2 * mi + 1)
         vop(CL, ["sg" + s, "cs" + s], [mt + "a"], lambda: V.tensor_tensor(ohc, cs, noh, A.max))
         send(t, c, "a", mcl(T.land, mi), ohc, [mt + "a"])
+        mm(B(4), [(Kb("Vu"), sg)], ["b.Vu", "sg" + s], [tk(4)])
+        sop(CL, [tk(4), "c.bVu"], [mt + "c", "cnt" + s], lambda: S.activation(mu, B(4), F.Relu, bias=C("bVu"), accum_out=T.cnt[:, c:c + 1]), 0.07)
         mm(B(3), [(T.kb[0:1, ob:ob + 128], T.ramp[0:1, :]), (Kb("KW"), noh)], ["b.KW", "b.one", "ramp", "sg" + s], [tk(3)])
         vop(CL, [tk(3), "cap"], ["sc" + s], lambda: V.tensor_tensor_scan(m(T.sc), T.cap[:, :], B(3), 0.0, A.add, A.min))
         ov = T.offv[:, NB * c:NB * (c + 1)]
         vop(NB, ["sc" + s], ["offv" + s], lambda: V.tensor_copy(ov, T.sc[:, c * CL + 15:(c + 1) * CL:16]))
         pick(mcl(T.msgv, 2 * mi), T.P[:, c * CE:(c + 1) * CE].indirect(ov), CL, ["offv" + s, "P%s.0" % s, "P%s.1" % s], [mt + "b"])
-        mm(B(4), [(Kb("Vu"), sg)], ["b.Vu", "sg" + s], [tk(4)])
-        sop(CL, [tk(4), "c.bVu"], [mt + "c", "cnt" + s], lambda: S.activation(mu, B(4), F.Relu, bias=C("bVu"), accum_out=T.cnt[:, c:c + 1]), 0.07)
         send(t, c, "b", m128(T.landv, mi), m128(T.msgv, mi), [mt + "b", mt + "c"])
         mm(B(0), [(cr["Ld"], one1), (Kb("Ld"), sg)], ["b.Ld", "r.Ld", "b.one", "sg" + s], [tk(0)])
         vop(CL, [tk(0), "odd" + s], ["md" + s], lambda: V.tensor_tensor(m(T.md), m(T.odd), B(0), A.is_ge))
         mm(B(5), [(Kh("R15"), ohc)], ["h.R15", mt + "a"], [tk(5)])
         vop(CL, [tk(5), "uu" + s], ["fa" + s], lambda: V.tensor_tensor(m(T.fa), m(T.uu), B(5), A.mult))
         vop(CL, ["fa" + s], ["fb" + s], lambda: V.tensor_scalar(m(T.fb), m(T.fa), 5, 4095, A.arith_shift_right, A.bitwise_and))
-        mm(B(4), [(Kh("SUu"), cs), (cr["Tu"], one1), (Kb("KI"), mu)], ["h.SUu", "b.KI", "r.Tu", "b.one", "cs" + s, mt + "c"], [tk(4)])
-        mm(B(0), [(Kh("IDu"), cs), (Kb("nKI"), mu), (Kb("nKI"), m(T.md))], ["h.IDu", "b.nKI", "cs" + s, "md" + s, mt + "c"], [tk(0)])
+        mm(B(4), [(Kh("SUu"), cs), (Kb("Um"), mu)], ["h.SUu", "b.Um", "cs" + s, mt + "c"], [tk(4)])
+        mm(B(0), [(Kh("IDu"), cs), (Kb("Sm"), mu), (Kb("nKI"), m(T.md))], ["h.IDu", "b.Sm", "b.nKI", "cs" + s, "md" + s, mt + "c"], [tk(0)])
         mm(B(1), [(Kh("SDu"), cs), (Kh("R0"), ohc), (Kb("KI"), m(T.md))], ["h.SDu", "h.R0", "b.KI", "cs" + s, "md" + s, mt + "a"], [tk(1)])
         vop(CL, [tk(4), "fb" + s], ["ts" + s], lambda: V.tensor_tensor(m(T.ts), m(T.fb), B(4), A.add))
         vop(CL, [tk(0), "ts" + s], ["zz" + s], lambda: V.tensor_tensor(m(T.zz), m(T.ts), B(0), A.max))
         vop(CL, [tk(1), "zz" + s], ["cn" + s], lambda: V.tensor_tensor(m(T.cn), m(T.zz), B(1), A.max))
         if t < RO - 1:
-            numbers(c)
+            numbers(t + 1, c)
 
     def phase_q(t, c):
         B, tk = tiles(c)
@@ -355,24 +367,28 @@ def build(g, T, topo, core, rank):
         top(2, 2 * CL, ["h.BOe", "b.BO3", lt], [tk(3), tk(5)],
             lambda e: [Pm.matmul(B(3), Kh("BOe"), le, True, True), Pm.matmul(B(5), Kb("BO3"), le, True, True)])
         vop(CL, ["cn" + s, tk(3)], ["L2" + s], lambda: V.tensor_tensor(m(T.L2), m(T.cn), B(3), A.mult))
-        index(c, B(5), tk(5), T.L2, "L2" + s, T.off2, "off2" + s)
-        gather(t, lambda h: T.x2[:, h * HE:(h + 1) * HE], T.off2, c, "x2" + s, "off2" + s)
-        mm(B(6), [(Kh("ID"), m(T.cn)), (Kh("Dm"), le)], ["h.ID", "h.Dm", "cn" + s, lt], [tk(6)])
+        index(c, B(5), tk(5), T.L2, "L2" + s, T.off2, "off2" + s, 2)
+        gather(t, lambda h: T.x2[:, c * HE:(c + 1) * HE, h % 2], T.off2, c, "x2" + s, "off2" + s)
+        mm(B(6), [(Kh("Dm"), le)], ["h.Dm", lt], [tk(6)])
         xt = ["x2%s.0" % s, "x2%s.1" % s]
-        xk = lambda k: T.x2[:, c * CE + k:(c + 1) * CE:16]
-        mk = lambda k: T.mx[:, c * CE + k * CL:c * CE + (k + 1) * CL]
-        mm(B(1), [(E8, T.thS[0:8, c * CL:(c + 1) * CL]), (Kb("BO"), lv)] + [(sel(T.Sel, k), xk(k)) for k in range(16)],
+        x2 = lambda k, step: T.x2[:, c * HE + k:(c + 1) * HE:step, :]
+        pp, pt = (T.Pa, T.Pb)[c % 2], ("Pa", "Pb")[c % 2] + s
+        o = HE // 2 + (c // 2) * CL
+        vops(2, CL, [lw], [pt], lambda e: [V.tensor_copy(pp[:, o + i:o + CL:2, :], lv) for i in range(2)])
+        mm(B(1), [(E8, T.thS[0:8, c * CL:(c + 1) * CL]), (Kb("BO"), lv)] + [(sel(T.Sel, k), x2(k, 16)) for k in range(16)],
            ["b.E8", "th", "b.BO", lw, "Sel"] + xt, [tk(1)], True, False)
-        for kq in range(0, 16, KQ):
-            it = "mx%s.%d" % (s, kq)
-            ks = range(kq, kq + KQ)
-            vops(KQ, CL, xt + [lw], [it], lambda e, ks=ks: [V.tensor_tensor(mk(k), xk(k), lv, A.max) for k in ks])
-            mm(B(1), [(sel(T.SelN, k), mk(k)) for k in ks], ["SelN", it], [tk(1)], False, kq + KQ == 16)
+        for h in range(2):
+            ks = range(4 * h, 4 * h + 4)
+            mk = lambda k, i=0, step=1: T.mx[:, c * HE + k * CL + i:c * HE + (k + 1) * CL:step, :]
+            vops(4, CL, xt + [pt], ["mx%s.%d" % (s, h)], lambda e, ks=ks: [V.tensor_tensor(mk(k), x2(k, 8), pp[:, o:o + CL, :], A.max) for k in ks])
+            mm(B(1), [(sel(T.SelN, k + 8 * i), mk(k, i, 2)) for k in ks for i in range(2)], ["SelN", "mx%s.%d" % (s, h)], [tk(1)], False, h == 1)
         sop(CL, [tk(1)], ["eta" + s], lambda: S.activation(m(T.eta), B(1), F.Sign, bias=0.5))
         mm(B(0), [(Kb("Fl"), lg), (Kb("Qm"), m(T.eta))], ["b.Qm", "b.Fl", "eta" + s, lw], [tk(0)])
         sop(CL, [tk(0), "c.bQ"], ["qq" + s], lambda: S.activation(m(T.qq), B(0), F.Sign, bias=C("bQ")))
-        vop(CL, [tk(6), "qq" + s], ["qd" + s], lambda: V.tensor_tensor(m(T.qd), m(T.qq), B(6), A.mult))
-        mm(B(4), [(Kh("H1"), m(T.cn)), (Kh("H2"), le), (K("H3"), m(T.qd))], ["h.H1", "h.H2", "k.H3", "cn" + s, lt, "qd" + s], [tk(4)], more=3)
+        qc, qe = mcl(T.qd, 2 * c), mcl(T.qd, 2 * c + 1)
+        vops(2, CL, [tk(6), "qq" + s, "cn" + s], ["qd" + s],
+             lambda e: [V.tensor_tensor(qe, m(T.qq), B(6), A.mult), V.tensor_tensor(qc, m(T.qq), m(T.cn), A.mult)])
+        mm(B(4), [(Kh("H1"), m(T.cn)), (Kh("H2"), le), (K("H3"), qe), (K("H3"), qc)], ["h.H1", "h.H2", "k.H3", "cn" + s, lt, "qd" + s], [tk(4)])
         if t == RO - 1:
             scale(CL, CL, m(T.ycS), B(4), 1.0, U, [tk(4)], ["yc" + s])
             dma("Y", mcl(T.yc, c), m(T.ycS), ["yc" + s], ["o.yc" + s], "oc" + s, 2.0)
@@ -384,26 +400,27 @@ def build(g, T, topo, core, rank):
             lambda: V.tensor_copy(X[:, 0:W].indirect(T.offr[:, 16 * p:16 * p + 16]), T.nx[:, p * L:(p + 1) * L]), sc=L)
 
     for c in range(NC):
-        numbers(c)
+        numbers(0, c)
     for t in range(RO):
         p = t % 2
+        part("start")
         if t < RO - 1:
-            r7 = T.B0[:, 7 * CL:7 * CL + 16]
-            mm(r7, [(sel(T.SelW, r), T.yb[:, r:L:16]) for r in range(16)], ["SelW"] + every("yb"), ["B0.7"], n=16)
-            vop(16, ["B0.7", "c.cU"], ["ra"], lambda: V.tensor_scalar(T.ra[:, :], r7, C("cU"), None, A.add))
+            vop(16, every("su") + ["c.cU"], ["ra"], lambda: V.tensor_scalar(T.ra[:, :], T.su[:, 15:L:16], C("cU"), None, A.add))
             vop(16, ["ra"], ["rb"], lambda: V.tensor_scalar(T.rb[:, :], T.ra[:, :], 31, None, A.bitwise_and))
             vop(32, ["rb", "ln32c"], ["rc"], lambda: V.tensor_tensor(T.rc[:, :], T.rb[:, :], T.ln32c[:, :], A.add))
             vop(16, ["rc"], ["offr%d" % p], lambda p=p: V.tensor_copy(T.offr[:, 16 * p:16 * p + 16], T.rc[:, :]))
         for c in range(NC):
+            part("p%d" % c)
             phase_p(t, c)
+        part("mid")
         if t == RO - 1:
             scale(L // 2, L, T.yyS[:, :], T.yb[:, :], 1.0, -YB, every("yb"), ["yy"])
             dma("Y", T.yy[:, :], T.yyS[:, :], ["yy"], ["o.yy"], "oy", 2.0)
         else:
             a7 = T["B%d" % (NC - 1)][:, 7 * CL:7 * CL + NC]
-            at = "B%d.7" % (NC - 1)
-            mm(a7, [(K("A32"), T.cnt[:, :])], ["k.A32"] + every("cnt"), [at], n=256)
-            sop(NC, [at], ["c.cA"], lambda: S.activation(T.cj[:, :], a7, F.Identity, bias=-262144.0 / NC, accum_out=C("cA")), 0.07)
+            ak = "B%d.7" % (NC - 1)
+            mm(a7, [(K("A32"), T.cnt[:, :])], ["k.A32"] + every("cnt"), [ak], n=256)
+            sop(NC, [ak], ["c.cA"], lambda: S.activation(T.cj[:, :], a7, F.Identity, bias=-262144.0 / NC, accum_out=C("cA")), 0.07)
             scale(L // 1, L, T.ez[:, :], T.yb[:, :], 0.25, WB - YB / 4 - 0.875, every("yb"), ["ez"])
             vop(0, XX[p][1] + ["offr%d" % p, "ez"], ["Wn"],
                 lambda p=p: V.tensor_tensor(T.Wn[:, :], XX[p][0][:, 0:W].indirect(T.offr[:, 16 * p:16 * p + 16]), T.ez[:, :], A.add), ga=L)
@@ -413,7 +430,9 @@ def build(g, T, topo, core, rank):
                     scatter(t - 1, 1 - p)
                 scatter(t, 1 - p)
         for c in range(NC):
+            part("q%d" % c)
             phase_q(t, c)
+        part("end")
         if not TWO and t < RO - 1:
             scatter(t, 0)
     return ops
@@ -450,11 +469,13 @@ def depend(ops):
 
 
 def way(o, P):
-    return P["far"] if o["lat"] == "far" else o["lat"] + (0.06 if o["eng"] == "T" else 0.0)
+    return P.get(o["lat"], o["lat"]) + (0.06 if o["eng"] == "T" else 0.0)
 
 
 def after(xs, t):
     k = len(xs)
+    while k > 8 and xs[k - 8] > t:
+        k -= 8
     while k and xs[k - 1] > t:
         k -= 1
     return k
@@ -552,8 +573,50 @@ def replay(ops, deps, order, pick, P):
     return end, pairs
 
 
+def rater(ops, deps):
+    tab = [{e: [cost(o, e, P) for P in FIGS] for e in o["eng"]} for o in ops]
+    far = [[way(o, P) + P["lat"] for P in FIGS] for o in ops]
+    l0, l1, l2, l3 = [P["lat"] for P in FIGS]
+    wait = [[d for d in deps[i] if not o["eng"] == "T" == ops[d]["eng"]] for i, o in enumerate(ops)]
+
+    def rate(order, pick):
+        free = {e: (0.0, 0.0, 0.0, 0.0) for e in "VSTGY"}
+        bank = [("", (0.0, 0.0, 0.0, 0.0))] * 8
+        fin = [None] * len(ops)
+        for i in order:
+            e = pick[i]
+            a, b, c, d = free[e]
+            for x in [fin[k] for k in wait[i]] + [bank[k][1] for k in ops[i]["banks"] if bank[k][0] != e]:
+                if x[0] > a:
+                    a = x[0]
+                if x[1] > b:
+                    b = x[1]
+                if x[2] > c:
+                    c = x[2]
+                if x[3] > d:
+                    d = x[3]
+            x = tab[i][e]
+            a, b, c, d = free[e] = (a + x[0], b + x[1], c + x[2], d + x[3])
+            for k in ops[i]["banks"]:
+                bank[k] = (e, (a + l0, b + l1, c + l2, d + l3))
+            x = far[i]
+            fin[i] = (a + x[0], b + x[1], c + x[2], d + x[3])
+        return sum(max(f[k] for f in fin) * 25.0 / SIZE[k] for k in range(4))
+    return rate
+
+
 def plan(ops, deps, tries=TRIES, swaps=SWAPS):
     n = len(ops)
+    above, short = [0] * n, []
+    for i in range(n):
+        a = 0
+        for d in deps[i]:
+            a |= above[d]
+        short.append([d for d in deps[i] if not a >> d & 1])
+        for d in deps[i]:
+            a |= 1 << d
+        above[i] = a
+    deps = short
     seed = [SEED]
 
     def rnd():
@@ -570,51 +633,61 @@ def plan(ops, deps, tries=TRIES, swaps=SWAPS):
             back[d].append((i, gap))
     pre, succ = [[j for j, x in p] for p in fore], [[j for j, x in p] for p in back]
 
+    rate = rater(ops, deps)
+
     def both(key, price, rounds):
-        best = None
-        for k in range(rounds):
+        st, fin, pick = place(ops, fore, succ, cst, key, lat, price, [0.0] * n)
+        for k in range(rounds - 1):
+            key = [-f for f in place(ops, back, pre, cst, [-f for f in fin], lat, price, ways)[1]]
             st, fin, pick = place(ops, fore, succ, cst, key, lat, price, [0.0] * n)
-            end = max(fin[i] + ways[i] for i in range(n))
-            if best is None or end < best[0]:
-                best = (end, st, pick, price)
-            if k < rounds - 1:
-                key = [-f for f in place(ops, back, pre, cst, [-f for f in fin], lat, price, ways)[1]]
-        return best
+        return rate(sorted(range(n), key=lambda i: st[i]), pick), st, pick, price
     pri = [0.0] * n
     for i in range(n - 1, -1, -1):
         pri[i] = min(cst[i].values()) + max([pri[j] + x for j, x in back[i]], default=ways[i])
-    cur = best = both([-p for p in pri], [PRICE] * n, 10)
-    free = [i for i in range(n) if len(ops[i]["eng"]) > 1 and max(cst[i].values()) > 0.2]
+    cur = best = both([-p for p in pri], [PRICE] * n, 8)
+    free = [i for i in range(n) if len(ops[i]["eng"]) > 1 and ops[i]["at"][0]]
+    like = {}
+    for i, o in enumerate(ops):
+        like.setdefault(o["at"], []).append(i)
     for it in range(tries):
         key, price, x = list(cur[1]), cur[3], rnd()
-        if x < 0.3:
+        same = (lambda k: like[ops[k]["at"]]) if rnd() < 0.6 else (lambda k: [k])
+        if x < 0.25:
             price = list(price)
-            for r in range(1 + int(3 * rnd())):
-                price[free[int(rnd() * len(free))]] = ((0, 50), (50, 0), PRICE)[int(rnd() * 3)]
-        elif x < 0.7:
+            for r in range(1 + int(2 * rnd())):
+                v = ((0, 50), (50, 0), (50, 0), PRICE)[int(rnd() * 4)]
+                for j in same(free[int(rnd() * len(free))]):
+                    price[j] = v
+        elif x < 0.6:
             a, d = int(rnd() * n), (rnd() - 0.5) * 4
-            for k in range(a, min(n, a + 1 + int(rnd() * 40))):
-                key[k] += d
+            for k in range(a, min(n, a + 1 + int(rnd() * rnd() * 60))):
+                for j in same(k):
+                    key[j] += d
+        elif x < 0.75:
+            a, d, step = int(rnd() * n), (rnd() - 0.5) * 3, 1 if rnd() < 0.5 else -1
+            k = a
+            while 0 <= k < n and ops[k]["at"][0] == ops[a]["at"][0]:
+                for j in same(k):
+                    key[j] += d
+                k += step
         else:
-            a, w = rnd() * cur[0], rnd() * 6
+            a, w = rnd() * max(cur[1]), rnd() * 6
             for k in range(n):
-                if a <= key[k] < a + w:
-                    key[k] += rnd() - 0.5
+                if a <= cur[1][k] < a + w:
+                    d = rnd() - 0.5
+                    for j in same(k):
+                        key[j] += d
         s2 = both(key, price, 2)
         if s2[0] <= cur[0] + 0.5 * rnd() * rnd() * (1 - it / tries):
             cur = s2
             if cur[0] < best[0]:
                 best = cur
-
-    def rate(order, pick):
-        res = [replay(ops, deps, order, pick, P) for P in FIGS]
-        return sum(r[0] / w for r, w in zip(res, base)), [b for r in res for b in r[1]]
-    order, pick = sorted(range(n), key=lambda i: (best[1][i], i)), best[2]
-    base = [replay(ops, deps, order, pick, P)[0] * len(FIGS) / best[0] for P in FIGS]
-    cur = rate(order, pick)
-    top = (cur[0], order, pick)
+    order, pick = sorted(range(n), key=lambda i: best[1][i]), best[2]
+    behind = lambda: [b for P in FIGS for b in replay(ops, deps, order, pick, P)[1]]
+    cur, pairs = best[0], behind()
+    top = (cur, order, pick)
     for it in range(swaps):
-        i, j = cur[1][int(rnd() * len(cur[1]))]
+        i, j = pairs[int(rnd() * len(pairs))]
         o2, p2, x = order, pick, rnd()
         c = [k for k in (i, j) if len(ops[k]["eng"]) > 1]
         if x < 0.25 and c:
@@ -641,10 +714,11 @@ def plan(ops, deps, tries=TRIES, swaps=SWAPS):
                     continue
                 o2 = order[:a] + [k for k in win if k not in mv] + [k for k in win if k in mv] + order[b + 1:]
         s2 = rate(o2, p2)
-        if s2 and s2[0] <= cur[0] + HEAT * rnd() * rnd() * (1 - it / swaps):
+        if s2 <= cur + HEAT * rnd() * rnd() * (1 - it / swaps):
             cur, order, pick = s2, o2, p2
-            if cur[0] < top[0]:
-                top = (cur[0], order, pick)
+            pairs = behind()
+            if cur < top[0]:
+                top = (cur, order, pick)
     return top[1], top[2]
 
 

@@ -1,4 +1,4 @@
-from concourse.mybir import AluOpType as A, AxisListType, ActivationFunctionType as F
+from concourse.mybir import AluOpType as A, ActivationFunctionType as F
 
 N, L, W, RO = 8, 256, 8192, 4
 NC = 4
@@ -6,32 +6,35 @@ CL = L // NC
 CE = 16 * CL
 HE = CE // 2
 NB = CL // 16
-KQ = 8
-TWO = False
-YB, WB = 160.0, 320.0
+KQ = 4
+TWO = True
+BIG, KV, PAR = 4096.0, 1988.0, 2 ** 18
+YB, WB = 160.0, 128.0
 U = 2048.0
 
 f32, bf, f16, i32, u16 = "float32", "bfloat16", "float16", "int32", "uint16"
 KB = ["one", "t0", "BO", "ID", "LT", "LE", "SD", "SU", "t1", "t2", "E8", "t4", "Mm", "OH", "Bm", "KW", "Ld", "Vu", "Qm", "Fl", "KI", "nKI",
-      "Wm", "BO3", "IDu", "SDu", "SUu", "R0", "Dm", "H1", "H2", "H3", "Um", "Sm"]
+      "Wm", "BO3", "IDu", "SDu", "SUu", "R0", "Dm", "G3", "Qm2", "Mp", "Um", "Sm"]
 KH, KF = ["R15", "BOe"], ["A32"]
 SCRATCH = {n: ("sbuf", [128, w], d) for n, w, d in [
-    ("XA", W, bf), ("XB", W if TWO else 16, bf), ("cin", L, i32), ("stS", RO * L, bf), ("yin", L, bf), ("wS", 1, bf), ("thS", L, bf),
+    ("XA", W, bf), ("XB", W if TWO else 16, bf), ("cin", L, i32), ("yin", L, bf), ("wS", 1, bf), ("thS", L, bf),
     ("cn", L, f16), ("cs", L, f16), ("yb", L, bf), ("ycS", L, f32), ("yyS", L, bf), ("P", 16 * L, bf),
-    ("PTs", 16 * L, bf), ("Ib", 16 * L, bf),
+    ("PTs", 16 * L, bf),
     ("ui", L, i32), ("uu", L, i32), ("odd", L, i32), ("Ls", L, f32), ("L2", L, f32), ("va", L, i32), ("vb", L, i32),
-    ("off1", L, u16), ("off2", L, u16), ("offv", NC * NB, u16), ("offr", 32, u16), ("sc", L, f32), ("cap", CL, f32),
+    ("off1", L, u16), ("off2", L, u16), ("offv", NC * NB, u16), ("offr", 32, u16), ("sc", L, f32),
+    ("cap", CL + 16, f32), ("capv", CL, f32), ("ramp", CL, f32),
     ("pw", L, bf), ("sg", 2 * L, bf), ("md", L, bf), ("fa", L, i32), ("fb", L, i32), ("Ms", L, f32),
-    ("ts", L, f32), ("zz", L, f32), ("eta", L, bf), ("qq", L, bf), ("qd", 2 * L, f16), ("ez", L, f32), ("Wn", L, bf), ("nx", 2 * L, bf),
+    ("ts", L, f32), ("zz", L, f32), ("eta", L, bf), ("qq", L, bf), ("qd", 2 * L, f16), ("ez", L, bf), ("low", L, bf), ("Wn", L, bf), ("nx", 2 * L, bf),
     ("ra", 16, i32), ("rb", 16, i32), ("rc", 16, i32), ("cnt", NC, f32), ("cj", NC, f32), ("col", 40, f32),
     ("msg", RO * L, f16), ("land", RO * L, f16), ("msgv", 2 * RO * L, bf), ("landv", 2 * RO * L, bf),
     ("kf", len(KF) * 128, f32), ("kb", len(KB) * 128, bf), ("kh", len(KH) * 128, f16),
-    ("Sel", 144, bf), ("SelN", 144, bf), ("su", L, f32),
-    ("crow", 2 * 128, bf), ("ramp", CL, bf), ("ln32", 16, f32), ("ln32c", 16, f32)]}
-SCRATCH.update({"R": ("psum", [128, 1024], f32), "Pa": ("psum", [128, HE, 2], bf), "Pb": ("psum", [128, HE, 2], bf)})
+    ("Sel", 144, bf), ("SelN", 144, bf), ("SelW", 144, bf), ("row", 2, i32),
+    ("ln32", 16, f32), ("ln32c", 16, f32)]}
+SCRATCH.update({"stS": ("sbuf", [128, 2, RO * L], bf), "Ib": ("sbuf", [128, 8 * NC, 2, CL], bf), "Mq": ("sbuf", [128, 8, 16], bf)})
+SCRATCH.update({"R": ("psum", [128, 2, 2, HE // 2], f32), "Pa": ("psum", [128, HE, 2], bf), "Pb": ("psum", [128, HE, 2], bf)})
 SCRATCH.update({n: ("sbuf", [128, 8 * L, 2], bf) for n in ("x2", "mx")})
 SCRATCH.update({"B%d" % c: ("psum", [128, 512], f32) for c in range(NC)})
-SEMAPHORES = (["sV", "sS", "sT", "sG", "sent", "dX0", "dX1", "dXB", "dc", "dst0", "dst1", "dy", "dw", "dth", "oy"]
+SEMAPHORES = (["sV", "sS", "sT", "sG", "sent", "dX0", "dX1", "dXB", "dc", "dst00", "dst01", "dst10", "dst11", "dy", "dw", "dth", "oy"]
               + ["oc%d" % c for c in range(NC)] + ["arr%d%s" % (i, x) for i in range(RO * NC) for x in "ab"])
 
 FIG = dict(cy=0.00083, ga=1.56, sc=3.8, pe=0.00042, lat=0.18, ov=0.005, far=2.8, out=0.5, load=8.0)
@@ -39,7 +42,7 @@ FIGS = [FIG, dict(FIG, cy=0.00112, pe=0.00056, ga=1.3, sc=2.5, lat=0.18, far=3.2
         dict(FIG, cy=0.0009, pe=0.00074, ga=1.6, sc=5.0, lat=0.2, far=3.5, out=0.9, load=9.0), dict(FIG, cy=0.001, pe=0.0005, ga=1.9, lat=0.29, ov=0.01, far=4.5, out=0.8)]
 MID = dict(FIG, cy=0.00096, pe=0.00056, lat=0.24, far=3.3, out=0.8, load=7.5)
 SIZE = (91.0, 108.0, 104.0, 124.0)
-TRIES, SWAPS, HEAT, SEED = 4600, 7000, 0.3, 12345
+STARTS, TRIES, SWEEPS, HEAT, NEAR, SEED = 4, 300, 1500, 0.06, 0.3, 1
 PRICE = (4.0, 2.5)
 
 
@@ -126,16 +129,18 @@ def build(g, T, topo, core, rank):
     dma("Y", T.cin[:, :], T.c0[:, :], [], ["cin"], "dc", 2.0)
     dma("S", T.XA[:, 0:W // 2], T.x0[:, 0:W // 2], [], ["XA0"], "dX0", "load")
     dma("Y", T.XA[:, W // 2:W], T.x0[:, W // 2:W], [], ["XA1"], "dX1", "load")
-    dma("Y", T.stS[:, 0:L], T.st[:, 0:L], [], ["st0"], "dst0", "load")
+    for i in range(2):
+        dma("Y", T.stS[:, i, 0:L], T.st[:, 0:L], [], ["st0%d" % i], "dst0%d" % i, "load")
     dma("Y", T.thS[0:8, :], T.th[:, :], [], ["th"], "dth", "load")
-    dma("Y", T.stS[:, L:RO * L], T.st[:, L:RO * L], [], ["st1"], "dst1", 11.0)
+    for i in range(2):
+        dma("Y", T.stS[:, i, L:RO * L], T.st[:, L:RO * L], [], ["st1%d" % i], "dst1%d" % i, 11.0)
     XX = [(T.XA, ["XA0", "XA1"])] * 2
     if TWO:
         dma("Y", T.XB[:, :], T.x0[:, :], ["XA0", "XA1"], ["XB0", "XB1"], "dXB", 8.0)
         XX[1] = (T.XB, ["XB0", "XB1"])
 
     cols = {n: i for i, n in enumerate(["n", "r0", "r15", "cM", "rpos", "s", "mid", "c0", "dLd", "hVu", "kw", "thr", "bVu", "bQ", "e4",
-                                        "j32", "a32", "wf", "cU", "cA", "nr0", "e32", "e3", "dm", "h2", "ra", "rb", "dif", "kx", "fl",
+                                        "j32", "a32", "wf", "cU", "cA", "nr0", "e32", "e3", "dm", "mid2", "big0", "ra", "rb", "dif", "kx", "fl",
                                         "bv", "kp", "uv", "u15"])}
     home = lambda n: (T.kh, KH.index(n)) if n in KH else (T.kf, KF.index(n)) if n in KF else (T.kb, KB.index(n))
     K = lambda n: m128(*home(n))
@@ -144,6 +149,7 @@ def build(g, T, topo, core, rank):
     top8 = lambda buf, i: buf[0:8, i * 128:(i + 1) * 128]
 
     vop(64, [], ["k.one"], lambda: V.memset(K("one"), 1.0))
+    gop(1, [], ["row0"], lambda: g.iota(T.row[:, 0:1], [[0, 1]], 127, -1))
 
     def asel(out, in_, pat, cmp, fill, base, cm, view=m128):
         gop(128, ["k." + in_], ["k." + out], lambda: g.affine_select(view(*home(out)), view(*home(in_)), pat, cmp, fill, base, cm))
@@ -154,7 +160,7 @@ def build(g, T, topo, core, rank):
     gop(16, [], ["ln32"], lambda: g.iota(T.ln32[:, :], [[512, 16]], 0, 0, allow_small_or_imprecise_dtypes=True))
     asel("SD", "BO", [[1, 128]], A.is_equal, 0.0, -1, -1)
     asel("SU", "BO", [[1, 128]], A.is_equal, 0.0, 1, -1)
-    gop(CL, [], ["ramp"], lambda: g.iota(T.ramp[0:1, :], [[16, CL]], 0, 0, allow_small_or_imprecise_dtypes=True))
+    gop(CL, [], ["ramp"], lambda: g.iota(T.ramp[:, :], [[16, CL]], -int(KV), 0, allow_small_or_imprecise_dtypes=True))
     asel("E8", "one", [[1, 128]], A.is_ge, 0.0, 0, -16, top8)
     asel("E8", "E8", [[-1, 128]], A.is_ge, 0.0, 15, 16, top8)
     E8 = top8(*home("E8"))
@@ -177,7 +183,8 @@ def build(g, T, topo, core, rank):
     scale(1, 1, C("wf"), T.wS[:, :], 1.0, 0.0, ["wS"], ["c.wf"])
     sc("Wm", "BO", "wf")
     vop(1, [], ["c.cA"], lambda: V.memset(C("cA"), -262144.0))
-    vop(128, ["k.LT"], ["c.n"], lambda: V.tensor_reduce(C("n"), K("LT"), AxisListType.X, A.add))
+    vop(1, ["row0"], ["row1"], lambda: V.tensor_scalar(T.row[:, 1:2], T.row[:, 0:1], 15, None, A.bitwise_and))
+    vop(1, ["row1"], ["c.n"], lambda: V.tensor_copy(C("n"), T.row[:, 1:2]))
     cts("r0", "n", 15.0, None, A.is_equal)
     cts("r15", "n", 0.0, None, A.is_equal)
     vop(1, ["c.r0", "c.r15"], ["c.s"], lambda: V.tensor_tensor(C("s"), C("r0"), C("r15"), A.add))
@@ -185,19 +192,20 @@ def build(g, T, topo, core, rank):
     sop(1, ["c.r0"], ["c.e4"], lambda: S.activation(C("e4"), C("r0"), F.Exp, scale=4.0), 1.3)
     row0 = lambda by, add: (add - 15 * by, by)
     for out, in_, (a, b) in (("cM", "n", (0.125, 0.125)), ("rpos", "r0", (-1.0, 1.0)), ("mid", "s", (-0.5, 0.5)), ("c0", "r0", (-101.0, 1.0)),
-                             ("nr0", "r0", (-1.0, 0.0)), ("thr", "e4", (1.0, -1.0)), ("dLd", "s", (-1.0, 0.0)), ("hVu", "dif", (-0.5, 0.0)),
-                             ("bv", "r15", (0.5, -0.5)), ("kp", "r0", (-2 * U, 2 * U)), ("uv", "r15", (2 * U, 0.0)), ("kx", "n", (0.5, -7.5)), ("bQ", "n", (8.5, 180.0)), ("fl", "r15", (-300.0, 0.0)),
+                             ("nr0", "r0", (-1.0, 0.0)), ("thr", "e4", (1.0, -1.0)), ("dLd", "s", (-PAR / 2, 0.0)), ("mid2", "s", (-1.0, 1.0)),
+                             ("big0", "r0", (-BIG, 0.0)), ("hVu", "dif", (-0.5, 0.0)),
+                             ("bv", "r15", (0.5, -0.5)), ("kp", "r0", (-2 * U, 2 * U)), ("uv", "r15", (2 * U, 0.0)), ("kx", "n", (0.5, -7.5)), ("bQ", "n", (-8.5, -180.0)), ("fl", "r15", (-300.0, 0.0)),
                              ("j32", "n", (-32.0, 480.0)), ("a32", "r15", (32.0, 0.0)), ("e32", "r0", row0(U, U + 32)),
-                             ("e3", "r0", row0(3232 * U, 1441792.0)), ("dm", "r0", row0(-U, 0.0)), ("h2", "r0", row0(U / 2, 0.0)),
+                             ("e3", "r0", row0(3232 * U, 1441792.0)), ("dm", "r0", row0(-U, 0.0)),
                              ("ra", "r0", row0(U, -2 * U)), ("rb", "r0", (-2 * U, 0.0))):
         cts(out, in_, a, b, A.mult, A.add)
-    for out, by, add in (("kw", 60.0, "kx"), ("bVu", 1.5, "bv"), ("u15", -3 * U, "uv")):
+    for out, by, add in (("kw", KV + 60.0, "kx"), ("bVu", 1.5, "bv"), ("u15", -3 * U, "uv")):
         scale(1, 1, C(out), C("r0"), by, C(add), ["c.r0", "c." + add], ["c." + out])
     for nm, in_, by in (("KI", "ID", 2 * U), ("nKI", "ID", -2 * U), ("KW", "BO", "kw"), ("Fl", "BO", "fl"), ("BO3", "BO", "e3"),
                         ("IDu", "ID", U), ("SDu", "SD", U), ("SUu", "SU", U), ("BOe", "BO", "e32"), ("Dm", "BO", "dm"),
-                        ("R0", "BO", "rb"), ("R15", "BO", 0.0), ("H2", "BO", 0.0), ("A32", "one", "a32")):
+                        ("R0", "BO", "rb"), ("R15", "BO", 0.0), ("A32", "one", "a32")):
         sc(nm, in_, by)
-    for nm, k, by in (("R0", 0, "ra"), ("R15", 15, "e32"), ("H2", 0, "h2")):
+    for nm, k, by in (("R0", 0, "ra"), ("R15", 15, "e32")):
         sc(nm, "BO", by, k)
 
     def inblock(out, prim, a, b):
@@ -206,6 +214,9 @@ def build(g, T, topo, core, rank):
         vop(128, ["k.BO"], ["k." + out], lambda: V.tensor_tensor(K(out), K(out), K("BO"), A.mult))
     inblock("Mm", "LT", -0.125, "cM")
     asel("Mm", "Mm", [[-1, 128]], A.not_equal, 2.0, 0, 1)
+    scale(64, 128, T.Mq[:, :, :], K("Mm"), 1.0, 0.0, ["k.Mm"], ["Mq"])
+    vops(2, 64, ["Mq"], ["k.Mp"], lambda e: [V.tensor_copy(T.kb[:, KB.index("Mp") * 128 + 64 * i:KB.index("Mp") * 128 + 64 * i + 64],
+                                                           T.Mq[:, :, 8 * i:8 * i + 8]) for i in range(2)])
     inblock("t4", "LT", 63.0, 1.0)
     asel("t4", "t4", [[-1, 128]], A.not_equal, -32.0, 0, 1)
     sc("OH", "t4", "rpos")
@@ -214,34 +225,29 @@ def build(g, T, topo, core, rank):
     sc("Bm", "t2", "rpos")
     sc("Bm", "BO", "nr0", 0)
     sc("Bm", "BO", "c0", 15)
-    inblock("Ld", "SD", "mid", "dLd")
+    inblock("Ld", "SD", "mid2", "dLd")
     inblock("Vu", "ID", "mid", "hVu")
     sc("Vu", "BO", 0.0, 0)
     inblock("Um", "ID", "kp", "rb")
     sc("Um", "BO", "u15", 15)
     sc("Sm", "nKI", "rpos")
     inblock("Qm", "LT", -8.5, 0.5)
-    vop(128, ["k.ID", "k.SD"], ["k.t0"], lambda: V.tensor_tensor(K("t0"), K("ID"), K("SD"), A.add))
-    sc("H1", "t0", 0.5)
-    vop(128, ["k.ID", "k.SD"], ["k.t1"], lambda: V.tensor_tensor(K("t1"), K("ID"), K("SD"), A.subtract))
-    sc("H3", "t1", 0.5)
+    sc("Qm2", "Qm", 2.0)
+    vop(128, ["k.ID", "k.SD"], ["k.G3"], lambda: V.tensor_tensor(K("G3"), K("SD"), K("ID"), A.subtract))
     Kb = Kh = K
     sel = lambda buf, k: buf[:, 16 - k:144 - k]
     vop(72, [], ["Sel"], lambda: V.memset(T.Sel[:, :], 0.0))
     scale(8, 8, T.Sel[:, 16:144:16], kcol("BO"), 1.0, 0.0, ["k.BO"], ["Sel"])
     scale(72, 144, T.SelN[:, :], T.Sel[:, :], -2.0, 0.0, ["Sel"], ["SelN"])
     scale(16, 16, T.ln32c[:, :], T.ln32[:, :], 1.0, C("j32"), ["ln32", "c.j32"], ["ln32c"])
-    gop(CL, [], ["cap"], lambda: g.iota(T.cap[:, :], [[0, NB], [-1, 16]], 15, 0, allow_small_or_imprecise_dtypes=True))
-    vop(CL, ["c.n"], ["cap"], lambda: V.tensor_scalar(T.cap[:, :], T.cap[:, :], C("n"), 2.0 ** 25, A.is_equal, A.mult))
-    cr = {}
-    for i, (nm, val, ex) in enumerate([("Ld", 2.5, {0: 2.0, 1: 2.0}), ("up", 16384.0, {})]):
-        cr[nm] = T.crow[0:1, i * 128:(i + 1) * 128]
-        vop(64, [], ["r." + nm], lambda nm=nm, val=val: V.memset(cr[nm], val))
-        if ex:
-            vops(len(ex), 8, [], ["r." + nm],
-                 lambda e, i=i, ex=ex: [V.memset(T.crow[0:1, i * 128 + kk:(i + 1) * 128:16], vv) for kk, vv in ex.items()])
+    scale(72, 144, T.SelW[:, :], T.Sel[:, :], C("wf"), 0.0, ["Sel", "c.wf"], ["SelW"])
+    vop(L // 2, [], ["low"], lambda: V.memset(T.low[:, :], -YB))
+    gop(CL + 16, [], ["cap"], lambda: g.iota(T.cap[:, :], [[0, NB + 1], [-1, 16]], 15, 0, allow_small_or_imprecise_dtypes=True))
+    vop(CL + 16, ["c.n"], ["cap"], lambda: V.tensor_scalar(T.cap[:, :], T.cap[:, :], C("n"), None, A.is_equal))
+    scale(CL, CL, T.capv[:, :], T.cap[:, 1:CL + 1], BIG, 0.0, ["cap"], ["capv"])
+    vop(2 * CL, ["cap"], ["ramp"], lambda: V.tensor_tensor(T.ramp[:, :], T.ramp[:, :], T.cap[:, 0:CL], A.mult))
+    vop(2 * CL, ["ramp"], ["capv"], lambda: V.tensor_tensor(T.capv[:, :], T.capv[:, :], T.ramp[:, :], A.add))
     ob = KB.index("one") * 128
-    one1 = T.kb[0:1, ob:ob + CL]
     every = lambda n: [n + str(c) for c in range(NC)]
 
     def tiles(c):
@@ -251,7 +257,7 @@ def build(g, T, topo, core, rank):
     scale(L // 2, L, T.yb[:, :], T.yin[:, :], 1.0, YB, ["yin"], every("yb"))
     x7 = T.B2[:, 7 * CL:7 * CL + 2]
     mm(x7, [(Kb("Wm"), T.kb[:, ob:ob + 2])], ["b.Wm", "b.one"], ["B2.7"], n=2)
-    scale(1, 1, C("cU"), T.B2[:, 7 * CL:7 * CL + 1], -YB, 0.0, ["B2.7"], ["c.cU"])
+    scale(1, 1, C("cU"), T.B2[:, 7 * CL:7 * CL + 1], -YB, -PAR / 2, ["B2.7"], ["c.cU"])
     for c in range(NC):
         mm(tiles(c)[0](4), [(Kh("IDu"), mcl(T.cs, c))], ["h.IDu", "cs%d" % c], ["B%d.4" % c])
 
@@ -275,15 +281,11 @@ def build(g, T, topo, core, rank):
         B, tk = tiles(c)
         s = str(c)
         m = lambda buf: mcl(buf, c)
-        if t < RO - 1:
-            mm(B(2), [(cr["up"], T.ramp[0:1, :]), (Kb("Wm"), m(T.yb))], ["r.up", "ramp", "b.Wm", "yb" + s], [tk(2)])
-            vop(CL, [tk(2), "cap"], ["su" + s], lambda: V.tensor_tensor_scan(m(T.su), T.cap[:, :], B(2), 0.0, A.add, A.min))
-        else:
-            mm(B(2), [(Kb("Wm"), m(T.yb))], ["b.Wm", "yb" + s], [tk(2)])
+        mm(B(2), [(Kb("Wm"), m(T.yb))], ["b.Wm", "yb" + s], [tk(2)])
         vop(CL, [tk(2), "c.cU"], ["ui" + s], lambda: V.tensor_scalar(m(T.ui), B(2), C("cU"), None, A.add))
         vop(CL, ["ui" + s], ["uu" + s], lambda: V.tensor_scalar(m(T.uu), m(T.ui), 2047, None, A.bitwise_and))
         vop(CL, ["uu" + s], ["Ms" + s], lambda: V.tensor_scalar(m(T.Ms), m(T.uu), 2.0, 33.0, A.mult, A.add))
-        vop(CL, ["ui" + s], ["odd" + s], lambda: V.tensor_scalar(m(T.odd), m(T.ui), 1, None, A.bitwise_and))
+        vop(CL, ["ui" + s], ["odd" + s], lambda: V.tensor_scalar(m(T.odd), m(T.ui), 1 - PAR, None, A.bitwise_and))
 
     def send(t, c, x, out, in_, rd):
         dst = T.cores[(rank + 1 + t % (N - 1)) % N]
@@ -313,18 +315,18 @@ def build(g, T, topo, core, rank):
             top(4, 512, ["b.ID", "P%s.%d" % (s, h)], [pt],
                 lambda e, o=o, pp=pp: [Pm.transpose(pp[:, 64 * b:64 * b + 64, :], T.P[:, o + b * 128:o + (b + 1) * 128], Kb("ID")) for b in range(4)])
             scale(HE // 2, HE, T.PTs[:, o:o + HE], pp[:, 0:HE // 2, :], 1.0, 0.0, [pt], ["PT%s.%d" % (s, h)])
-            top(4, 512, ["b.Mm", "PT%s.%d" % (s, h)], ["R%d" % h],
-                lambda e, o=o, h=h: [Pm.matmul(m128(T.R, 4 * h + b), T.PTs[:, o + b * 128:o + (b + 1) * 128], Kb("Mm"), True, True) for b in range(4)])
-        RT = ["R0", "R1"]
-        Rk = lambda k: T.R[:, k:CE:16]
-        stv = mcl(T.stS, t * NC + c)
-        Ik = lambda k: T.Ib[:, c * CE + k * CL:c * CE + (k + 1) * CL]
-        for kq in range(0, 16, KQ):
-            it = "I%s.%d" % (s, kq)
-            vops(KQ, CL, RT + ["st%d" % min(t, 1)], [it],
-                 lambda e, kq=kq: [V.tensor_tensor(Ik(k), Rk(k), stv, A.is_ge) for k in range(kq, kq + KQ)])
-            mm(B(0), [(sel(T.Sel, k), Ik(k)) for k in range(kq, kq + KQ)], ["Sel", it], [tk(0)], kq == 0, kq + KQ == 16)
-        scale(CL, CL, m(T.yb), Rk(0), 0.25, YB - 0.484375, RT, ["yb" + s])
+            top(4, 512, ["b.Mp", "PT%s.%d" % (s, h)], ["R%d" % h],
+                lambda e, o=o, h=h: [Pm.matmul(T.R[:, h, :, 64 * b:64 * b + 64], T.PTs[:, o + b * 128:o + (b + 1) * 128], Kb("Mp"), True, True)
+                                     for b in range(4)])
+            a = t * L + c * CL + h * CL // 2
+            for kq in range(0, 8, KQ):
+                vops(KQ, CL, ["R%d" % h, "st%d0" % min(t, 1), "st%d1" % min(t, 1)], ["I%s.%d.%d" % (s, h, kq)],
+                     lambda e, kq=kq, h=h, a=a: [V.tensor_tensor(T.Ib[:, 8 * c + k, :, h * CL // 2:(h + 1) * CL // 2], T.R[:, h, :, k:HE // 2:8],
+                                                                 T.stS[:, :, a:a + CL // 2], A.is_ge) for k in range(kq, kq + KQ)])
+        for kq in range(0, 8, KQ):
+            mm(B(0), [(sel(T.Sel, k + 8 * i), T.Ib[:, 8 * c + k, i, :]) for k in range(kq, kq + KQ) for i in range(2)],
+               ["Sel"] + ["I%s.%d.%d" % (s, h, kq) for h in range(2)], [tk(0)], kq == 0, kq + KQ == 8)
+        scale(CL, CL, m(T.yb), T.R[:, :, 0, 0:HE // 2:8], 0.25, YB - 0.484375, ["R0", "R1"], ["yb" + s])
         sop(CL, [tk(0)], ["pw" + s], lambda: S.activation(m(T.pw), B(0), F.Exp, bias=-64.0, scale=8.0))
         top(2, 2 * CL, ["b.OH", "b.Bm", "pw" + s], [tk(1), tk(2)],
             lambda e: [Pm.matmul(B(1), Kb("OH"), m(T.pw), True, True), Pm.matmul(B(2), Kb("Bm"), m(T.pw), True, True)])
@@ -337,13 +339,13 @@ def build(g, T, topo, core, rank):
         send(t, c, "a", mcl(T.land, mi), ohc, [mt + "a"])
         mm(B(4), [(Kb("Vu"), sg)], ["b.Vu", "sg" + s], [tk(4)])
         sop(CL, [tk(4), "c.bVu"], [mt + "c", "cnt" + s], lambda: S.activation(mu, B(4), F.Relu, bias=C("bVu"), accum_out=T.cnt[:, c:c + 1]), 0.07)
-        mm(B(3), [(T.kb[0:1, ob:ob + 128], T.ramp[0:1, :]), (Kb("KW"), noh)], ["b.KW", "b.one", "ramp", "sg" + s], [tk(3)])
-        vop(CL, [tk(3), "cap"], ["sc" + s], lambda: V.tensor_tensor_scan(m(T.sc), T.cap[:, :], B(3), 0.0, A.add, A.min))
+        mm(B(3), [(Kb("KW"), noh)], ["b.KW", "sg" + s], [tk(3)])
+        vop(CL, [tk(3), "capv"], ["sc" + s], lambda: V.tensor_tensor_scan(m(T.sc), B(3), T.capv[:, :], BIG, A.min, A.add))
         ov = T.offv[:, NB * c:NB * (c + 1)]
-        vop(NB, ["sc" + s], ["offv" + s], lambda: V.tensor_copy(ov, T.sc[:, c * CL + 15:(c + 1) * CL:16]))
+        vop(NB, ["sc" + s, "c.big0"], ["offv" + s], lambda: V.tensor_scalar(ov, T.sc[:, c * CL + 15:(c + 1) * CL:16], C("big0"), None, A.add))
         pick(mcl(T.msgv, 2 * mi), T.P[:, c * CE:(c + 1) * CE].indirect(ov), CL, ["offv" + s, "P%s.0" % s, "P%s.1" % s], [mt + "b"])
         send(t, c, "b", m128(T.landv, mi), m128(T.msgv, mi), [mt + "b", mt + "c"])
-        mm(B(0), [(cr["Ld"], one1), (Kb("Ld"), sg)], ["b.Ld", "r.Ld", "b.one", "sg" + s], [tk(0)])
+        mm(B(0), [(Kb("Ld"), sg)], ["b.Ld", "sg" + s], [tk(0)])
         vop(CL, [tk(0), "odd" + s], ["md" + s], lambda: V.tensor_tensor(m(T.md), m(T.odd), B(0), A.is_ge))
         mm(B(5), [(Kh("R15"), ohc)], ["h.R15", mt + "a"], [tk(5)])
         vop(CL, [tk(5), "uu" + s], ["fa" + s], lambda: V.tensor_tensor(m(T.fa), m(T.uu), B(5), A.mult))
@@ -356,6 +358,8 @@ def build(g, T, topo, core, rank):
         vop(CL, [tk(1), "zz" + s], ["cn" + s], lambda: V.tensor_tensor(m(T.cn), m(T.zz), B(1), A.max))
         if t < RO - 1:
             numbers(t + 1, c)
+
+    weigh = {}
 
     def phase_q(t, c):
         B, tk = tiles(c)
@@ -375,20 +379,25 @@ def build(g, T, topo, core, rank):
         pp, pt = (T.Pa, T.Pb)[c % 2], ("Pa", "Pb")[c % 2] + s
         o = HE // 2 + (c // 2) * CL
         vops(2, CL, [lw], [pt], lambda e: [V.tensor_copy(pp[:, o + i:o + CL:2, :], lv) for i in range(2)])
-        mm(B(1), [(E8, T.thS[0:8, c * CL:(c + 1) * CL]), (Kb("BO"), lv)] + [(sel(T.Sel, k), x2(k, 16)) for k in range(16)],
-           ["b.E8", "th", "b.BO", lw, "Sel"] + xt, [tk(1)], True, False)
+        for h in range(2):
+            mm(B(1), [(sel(T.Sel, k), x2(k, 16)) for k in range(8 * h, 8 * h + 8)], ["Sel"] + xt, [tk(1)], h == 0, False)
+        mm(B(1), [(E8, T.thS[0:8, c * CL:(c + 1) * CL]), (Kb("BO"), lv)], ["b.E8", "th", "b.BO", lw], [tk(1)], False, False)
         for h in range(2):
             ks = range(4 * h, 4 * h + 4)
             mk = lambda k, i=0, step=1: T.mx[:, c * HE + k * CL + i:c * HE + (k + 1) * CL:step, :]
             vops(4, CL, xt + [pt], ["mx%s.%d" % (s, h)], lambda e, ks=ks: [V.tensor_tensor(mk(k), x2(k, 8), pp[:, o:o + CL, :], A.max) for k in ks])
             mm(B(1), [(sel(T.SelN, k + 8 * i), mk(k, i, 2)) for k in ks for i in range(2)], ["SelN", "mx%s.%d" % (s, h)], [tk(1)], False, h == 1)
-        sop(CL, [tk(1)], ["eta" + s], lambda: S.activation(m(T.eta), B(1), F.Sign, bias=0.5))
-        mm(B(0), [(Kb("Fl"), lg), (Kb("Qm"), m(T.eta))], ["b.Qm", "b.Fl", "eta" + s, lw], [tk(0)])
-        sop(CL, [tk(0), "c.bQ"], ["qq" + s], lambda: S.activation(m(T.qq), B(0), F.Sign, bias=C("bQ")))
+        def hit(e):
+            weigh[mi] = "Qm" if e == "S" else "Qm2"
+            return [S.activation(m(T.eta), B(1), F.Sign, bias=0.5) if e == "S" else V.tensor_scalar(m(T.eta), B(1), 0.0, 0.5, A.is_ge, A.subtract)]
+        op({"V": (CL, 0, 0, 0, 1, 0), "S": (CL, 0, 0, 0, 1, 0.05)}, [tk(1)], ["eta" + s], hit)
+        top(2, 2 * CL, ["b.Qm", "b.Qm2", "b.Fl", "eta" + s, lw], [tk(0)],
+            lambda e: [Pm.matmul(B(0), Kb("Fl"), lg, True, False), Pm.matmul(B(0), Kb(weigh[mi]), m(T.eta), False, True)])
+        vop(CL, [tk(0), "c.bQ"], ["qq" + s], lambda: V.tensor_scalar(m(T.qq), B(0), C("bQ"), None, A.is_lt))
         qc, qe = mcl(T.qd, 2 * c), mcl(T.qd, 2 * c + 1)
         vops(2, CL, [tk(6), "qq" + s, "cn" + s], ["qd" + s],
              lambda e: [V.tensor_tensor(qe, m(T.qq), B(6), A.mult), V.tensor_tensor(qc, m(T.qq), m(T.cn), A.mult)])
-        mm(B(4), [(Kh("H1"), m(T.cn)), (Kh("H2"), le), (K("H3"), qe), (K("H3"), qc)], ["h.H1", "h.H2", "k.H3", "cn" + s, lt, "qd" + s], [tk(4)])
+        mm(B(4), [(Kh("ID"), m(T.cn)), (K("G3"), qe), (K("G3"), qc)], ["k.ID", "k.G3", "cn" + s, "qd" + s], [tk(4)])
         if t == RO - 1:
             scale(CL, CL, m(T.ycS), B(4), 1.0, U, [tk(4)], ["yc" + s])
             dma("Y", mcl(T.yc, c), m(T.ycS), ["yc" + s], ["o.yc" + s], "oc" + s, 2.0)
@@ -396,8 +405,8 @@ def build(g, T, topo, core, rank):
     def scatter(t, to):
         X, xt = XX[to]
         p = t % 2
-        vop(0, ["nx%d" % p, "offr%d" % p], xt,
-            lambda: V.tensor_copy(X[:, 0:W].indirect(T.offr[:, 16 * p:16 * p + 16]), T.nx[:, p * L:(p + 1) * L]), sc=L)
+        vop(0, ["nx%d" % p, "offr%d" % p, "low"], xt,
+            lambda: V.tensor_tensor(X[:, 0:W].indirect(T.offr[:, 16 * p:16 * p + 16]), T.nx[:, p * L:(p + 1) * L], T.low[:, :], A.add), sc=L)
 
     for c in range(NC):
         numbers(0, c)
@@ -405,7 +414,9 @@ def build(g, T, topo, core, rank):
         p = t % 2
         part("start")
         if t < RO - 1:
-            vop(16, every("su") + ["c.cU"], ["ra"], lambda: V.tensor_scalar(T.ra[:, :], T.su[:, 15:L:16], C("cU"), None, A.add))
+            su = T.B2[:, 7 * CL:7 * CL + 16]
+            mm(su, [(sel(T.SelW, k), T.yb[:, k:L:16]) for k in range(16)], ["SelW"] + every("yb"), ["B2.7"], n=16)
+            vop(16, ["B2.7", "c.cU"], ["ra"], lambda su=su: V.tensor_scalar(T.ra[:, :], su, C("cU"), None, A.add))
             vop(16, ["ra"], ["rb"], lambda: V.tensor_scalar(T.rb[:, :], T.ra[:, :], 31, None, A.bitwise_and))
             vop(32, ["rb", "ln32c"], ["rc"], lambda: V.tensor_tensor(T.rc[:, :], T.rb[:, :], T.ln32c[:, :], A.add))
             vop(16, ["rc"], ["offr%d" % p], lambda p=p: V.tensor_copy(T.offr[:, 16 * p:16 * p + 16], T.rc[:, :]))
@@ -421,10 +432,12 @@ def build(g, T, topo, core, rank):
             ak = "B%d.7" % (NC - 1)
             mm(a7, [(K("A32"), T.cnt[:, :])], ["k.A32"] + every("cnt"), [ak], n=256)
             sop(NC, [ak], ["c.cA"], lambda: S.activation(T.cj[:, :], a7, F.Identity, bias=-262144.0 / NC, accum_out=C("cA")), 0.07)
-            scale(L // 1, L, T.ez[:, :], T.yb[:, :], 0.25, WB - YB / 4 - 0.875, every("yb"), ["ez"])
-            vop(0, XX[p][1] + ["offr%d" % p, "ez"], ["Wn"],
-                lambda p=p: V.tensor_tensor(T.Wn[:, :], XX[p][0][:, 0:W].indirect(T.offr[:, 16 * p:16 * p + 16]), T.ez[:, :], A.add), ga=L)
-            scale(L // 2, L, T.nx[:, p * L:(p + 1) * L], T.Wn[:, :], 0.5, -WB / 2, ["Wn"], ["nx%d" % p])
+            old = XX[p][0][:, 0:W].indirect(T.offr[:, 16 * p:16 * p + 16])
+            op({"V": (60, L, 0, 0, 1, 0), "S": (78, L, 0, 0, 1, 0)}, XX[p][1] + ["offr%d" % p], ["ez"],
+               lambda e, old=old: [V.tensor_scalar(T.ez[:, :], old, 4.0, -WB, A.mult, A.add) if e == "V" else
+                                   S.activation(T.ez[:, :], old, F.Identity, bias=-WB, scale=4.0)])
+            vop(L, every("yb") + ["ez"], ["Wn"], lambda: V.tensor_tensor(T.Wn[:, :], T.ez[:, :], T.yb[:, :], A.add))
+            scale(L // 2, L, T.nx[:, p * L:(p + 1) * L], T.Wn[:, :], 0.125, YB - (YB - WB) / 8 - 0.4375, ["Wn"], ["nx%d" % p])
             if TWO:
                 if t > 0:
                     scatter(t - 1, 1 - p)
@@ -537,75 +550,188 @@ def place(ops, pre, succ, cst, key, lat, price, t00):
     return st, fin, pick
 
 
-def replay(ops, deps, order, pick, P):
-    free = {e: (0.0, -1) for e in "VSTGY"}
-    bank = [("", 0.0, -1)] * 8
-    fin = [0.0] * len(ops)
-    why = [(-1, False)] * len(ops)
-    key = ("tab", len(ops)) + tuple(P.values())
-    if key not in PLAN:
-        PLAN[key] = [dict({e: cost(o, e, P) for e in o["eng"]}, way=way(o, P)) for o in ops]
-    tab = PLAN[key]
-    lat = P["lat"]
-    for i in order:
-        o, e = ops[i], pick[i]
-        t, w = free[e]
-        w = (w, True)
-        for b in o["banks"]:
-            if bank[b][0] != e and bank[b][1] + lat > t:
-                t, w = bank[b][1] + lat, (bank[b][2], True)
-        for d in deps[i]:
-            x = fin[d] + (0.0 if e == "T" and pick[d] == "T" else lat)
-            if x >= t:
-                t, w = x, (d, False)
-        why[i] = w
-        t += tab[i][e]
-        free[e] = (t, i)
-        for b in o["banks"]:
-            bank[b] = (e, t, i)
-        fin[i] = t + tab[i]["way"]
-    end = max(fin)
-    i, pairs = fin.index(end), []
-    while why[i][0] >= 0:
-        if why[i][1]:
-            pairs.append((i, why[i][0]))
-        i = why[i][0]
-    return end, pairs
-
-
-def rater(ops, deps):
+def polisher(ops, deps, pre, rnd):
+    n = len(ops)
     tab = [{e: [cost(o, e, P) for P in FIGS] for e in o["eng"]} for o in ops]
     far = [[way(o, P) + P["lat"] for P in FIGS] for o in ops]
     l0, l1, l2, l3 = [P["lat"] for P in FIGS]
+    w0, w1, w2, w3 = [25.0 / x for x in SIZE]
     wait = [[d for d in deps[i] if not o["eng"] == "T" == ops[d]["eng"]] for i, o in enumerate(ops)]
+    used = set(d for p in deps for d in p)
+    users = [[] if i in used else [n] for i in range(n)]
+    for i in range(n):
+        for d in wait[i]:
+            users[d].append(i)
+    banks = [o["banks"] for o in ops]
+    zero = (0.0, 0.0, 0.0, 0.0)
+    end, fin, tail, pos = [zero] * n, [zero] * n, [zero] * (n + 1), [0] * n + [n]
+    order, pick = [], []
 
-    def rate(order, pick):
-        free = {e: (0.0, 0.0, 0.0, 0.0) for e in "VSTGY"}
-        bank = [("", (0.0, 0.0, 0.0, 0.0))] * 8
-        fin = [None] * len(ops)
-        for i in order:
+    def ahead(win, free, bank):
+        for i in win:
             e = pick[i]
             a, b, c, d = free[e]
-            for x in [fin[k] for k in wait[i]] + [bank[k][1] for k in ops[i]["banks"] if bank[k][0] != e]:
-                if x[0] > a:
-                    a = x[0]
-                if x[1] > b:
-                    b = x[1]
-                if x[2] > c:
-                    c = x[2]
-                if x[3] > d:
-                    d = x[3]
-            x = tab[i][e]
-            a, b, c, d = free[e] = (a + x[0], b + x[1], c + x[2], d + x[3])
-            for k in ops[i]["banks"]:
-                bank[k] = (e, (a + l0, b + l1, c + l2, d + l3))
-            x = far[i]
-            fin[i] = (a + x[0], b + x[1], c + x[2], d + x[3])
-        return sum(max(f[k] for f in fin) * 25.0 / SIZE[k] for k in range(4))
-    return rate
+            for k in wait[i]:
+                x0, x1, x2, x3 = fin[k]
+                if x0 > a:
+                    a = x0
+                if x1 > b:
+                    b = x1
+                if x2 > c:
+                    c = x2
+                if x3 > d:
+                    d = x3
+            for k in banks[i]:
+                j = bank[k]
+                bank[k] = i
+                if j >= 0 and pick[j] != e:
+                    x0, x1, x2, x3 = end[j]
+                    if x0 + l0 > a:
+                        a = x0 + l0
+                    if x1 + l1 > b:
+                        b = x1 + l1
+                    if x2 + l2 > c:
+                        c = x2 + l2
+                    if x3 + l3 > d:
+                        d = x3 + l3
+            x0, x1, x2, x3 = tab[i][e]
+            a, b, c, d = end[i] = free[e] = (a + x0, b + x1, c + x2, d + x3)
+            x0, x1, x2, x3 = far[i]
+            fin[i] = (a + x0, b + x1, c + x2, d + x3)
+
+    def back(win, queue, bank):
+        for i in reversed(win):
+            e = pick[i]
+            a, b, c, d = tail[queue[e]]
+            queue[e] = i
+            y0, y1, y2, y3 = far[i]
+            for k in users[i]:
+                x0, x1, x2, x3 = tail[k]
+                if x0 + y0 > a:
+                    a = x0 + y0
+                if x1 + y1 > b:
+                    b = x1 + y1
+                if x2 + y2 > c:
+                    c = x2 + y2
+                if x3 + y3 > d:
+                    d = x3 + y3
+            for k in banks[i]:
+                j = bank[k]
+                bank[k] = i
+                if j < n and pick[j] != e:
+                    x0, x1, x2, x3 = tail[j]
+                    if x0 + l0 > a:
+                        a = x0 + l0
+                    if x1 + l1 > b:
+                        b = x1 + l1
+                    if x2 + l2 > c:
+                        c = x2 + l2
+                    if x3 + l3 > d:
+                        d = x3 + l3
+            x0, x1, x2, x3 = tab[i][e]
+            tail[i] = (a + x0, b + x1, c + x2, d + x3)
+
+    def behind(b):
+        queue, bank, left = {e: n for e in "VSTGY"}, [n] * 8, 12
+        for i in order[b + 1:b + 150]:
+            if queue[pick[i]] == n:
+                queue[pick[i]] = i
+                left -= pick[i] != "Y"
+            for k in banks[i]:
+                if bank[k] == n:
+                    bank[k] = i
+                    left -= 1
+            if not left:
+                break
+        return queue, bank
+
+    def through(win, b, free, bank, queue, nbank, arcs):
+        free, bank = dict(free), list(bank)
+        ahead(win, free, bank)
+        x = [(fin[i], tail[j]) for i in win for j in users[i] if pos[j] > b] + [(free[e], tail[queue[e]]) for e in free]
+        x += [(fin[i], tail[j]) for i, j in arcs if pos[j] > b]
+        for i, j in zip(bank, nbank):
+            if i >= 0 and j < n and pick[i] != pick[j]:
+                x0, x1, x2, x3 = end[i]
+                x.append(((x0 + l0, x1 + l1, x2 + l2, x3 + l3), tail[j]))
+        return (max([u[0] + v[0] for u, v in x]), max([u[1] + v[1] for u, v in x]), max([u[2] + v[2] for u, v in x]),
+                max([u[3] + v[3] for u, v in x]))
+
+    def move(a, near):
+        j, x = order[a], rnd()
+        if x < 0.15:
+            if near[j] and len(ops[j]["eng"]) > 1:
+                pick[j] = "V" if pick[j] == "S" else "S"
+                return [j], a
+        elif x < 0.75:
+            skip, on = int(4 * rnd() * rnd()), banks[j] if rnd() < 0.3 else None
+            for b in range(a + 1, min(n, a + 50)):
+                i = order[b]
+                if (pick[i] != pick[j] and on[0] in banks[i]) if on else pick[i] == pick[j]:
+                    skip -= 1
+                    if skip < 0:
+                        break
+            if skip < 0 and near[i]:
+                win = order[a:b + 1]
+                if x < 0.5:
+                    mv = {i}
+                    for k in reversed(win):
+                        if k in mv:
+                            mv.update(pre[k])
+                    if j not in mv:
+                        return [k for k in win if k in mv] + [k for k in win if k not in mv], b
+                else:
+                    mv = {j}
+                    for k in win:
+                        if any(d in mv for d in pre[k]):
+                            mv.add(k)
+                    if i not in mv:
+                        return [k for k in win if k not in mv] + [k for k in win if k in mv], b
+        return None, a
+
+    def polish(first, engines, sweeps, heat):
+        order[:], pick[:] = first, engines
+        top = None
+        for it in range(sweeps + 1):
+            for p, i in enumerate(order):
+                pos[i] = p
+            back(order, {e: n for e in "VSTGY"}, [n] * 8)
+            m = [max(tail[i][f] for i in order[:40]) for f in range(4)]
+            cur = m[0] * w0 + m[1] * w1 + m[2] * w2 + m[3] * w3
+            if top is None or cur < top[0]:
+                top = (cur, list(order), list(pick))
+            if it == sweeps:
+                return top
+            ahead(order, {e: zero for e in "VSTGY"}, [-1] * 8)
+            f = int(4 * rnd())
+            near = [end[i][f] - tab[i][pick[i]][f] + tail[i][f] > m[f] - NEAR for i in range(n)]
+            free, bank, arcs = {e: zero for e in "VSTGY"}, [-1] * 8, []
+            for a in range(n):
+                j = order[a]
+                e = pick[j]
+                win, b = move(a, near)
+                if win:
+                    queue, nbank = behind(b)
+                    arcs = [x for x in arcs if pos[x[1]] >= a]
+                    m2 = through(win, b, free, bank, queue, nbank, arcs)
+                    s2 = m2[0] * w0 + m2[1] * w1 + m2[2] * w2 + m2[3] * w3
+                    if s2 <= cur + 1e-9 + heat * (1 - it / sweeps) * rnd() * rnd():
+                        cur, m = s2, m2
+                        order[a:b + 1] = win
+                        for p, i in enumerate(win):
+                            pos[i] = a + p
+                        back(win, queue, nbank)
+                    else:
+                        pick[j] = e
+                j = order[a]
+                ahead([j], free, bank)
+                x0, x1, x2, x3 = fin[j]
+                arcs += [(j, i) for i in users[j] if x0 + tail[i][0] > m[0] - 2 or x1 + tail[i][1] > m[1] - 2
+                         or x2 + tail[i][2] > m[2] - 2 or x3 + tail[i][3] > m[3] - 2]
+    return polish
 
 
-def plan(ops, deps, tries=TRIES, swaps=SWAPS):
+def plan(ops, deps, starts=STARTS, tries=TRIES, sweeps=SWEEPS):
     n = len(ops)
     above, short = [0] * n, []
     for i in range(n):
@@ -633,23 +759,27 @@ def plan(ops, deps, tries=TRIES, swaps=SWAPS):
             back[d].append((i, gap))
     pre, succ = [[j for j, x in p] for p in fore], [[j for j, x in p] for p in back]
 
-    rate = rater(ops, deps)
+    polish = polisher(ops, deps, pre, rnd)
 
     def both(key, price, rounds):
         st, fin, pick = place(ops, fore, succ, cst, key, lat, price, [0.0] * n)
         for k in range(rounds - 1):
             key = [-f for f in place(ops, back, pre, cst, [-f for f in fin], lat, price, ways)[1]]
             st, fin, pick = place(ops, fore, succ, cst, key, lat, price, [0.0] * n)
-        return rate(sorted(range(n), key=lambda i: st[i]), pick), st, pick, price
+        return polish(sorted(range(n), key=lambda i: st[i]), pick, 0, 0.0)[0], st, pick, price
     pri = [0.0] * n
     for i in range(n - 1, -1, -1):
         pri[i] = min(cst[i].values()) + max([pri[j] + x for j, x in back[i]], default=ways[i])
-    cur = best = both([-p for p in pri], [PRICE] * n, 8)
+    first = both([-p for p in pri], [PRICE] * n, 8)
     free = [i for i in range(n) if len(ops[i]["eng"]) > 1 and ops[i]["at"][0]]
     like = {}
     for i, o in enumerate(ops):
         like.setdefault(o["at"], []).append(i)
-    for it in range(tries):
+    done = []
+    for run in range(starts * tries):
+        it = run % tries
+        if it == 0:
+            cur = best = first
         key, price, x = list(cur[1]), cur[3], rnd()
         same = (lambda k: like[ops[k]["at"]]) if rnd() < 0.6 else (lambda k: [k])
         if x < 0.25:
@@ -682,44 +812,9 @@ def plan(ops, deps, tries=TRIES, swaps=SWAPS):
             cur = s2
             if cur[0] < best[0]:
                 best = cur
-    order, pick = sorted(range(n), key=lambda i: best[1][i]), best[2]
-    behind = lambda: [b for P in FIGS for b in replay(ops, deps, order, pick, P)[1]]
-    cur, pairs = best[0], behind()
-    top = (cur, order, pick)
-    for it in range(swaps):
-        i, j = pairs[int(rnd() * len(pairs))]
-        o2, p2, x = order, pick, rnd()
-        c = [k for k in (i, j) if len(ops[k]["eng"]) > 1]
-        if x < 0.25 and c:
-            p2 = list(pick)
-            k = c[int(rnd() * len(c))]
-            p2[k] = "V" if p2[k] == "S" else "S"
-        else:
-            a, b = order.index(j), order.index(i)
-            win = order[a:b + 1]
-            if x < 0.65:
-                mv = {i}
-                for k in reversed(win):
-                    if k in mv:
-                        mv.update(pre[k])
-                if j in mv:
-                    continue
-                o2 = order[:a] + [k for k in win if k in mv] + [k for k in win if k not in mv] + order[b + 1:]
-            else:
-                mv = {j}
-                for k in win:
-                    if any(d in mv for d in pre[k]):
-                        mv.add(k)
-                if i in mv:
-                    continue
-                o2 = order[:a] + [k for k in win if k not in mv] + [k for k in win if k in mv] + order[b + 1:]
-        s2 = rate(o2, p2)
-        if s2 <= cur + HEAT * rnd() * rnd() * (1 - it / swaps):
-            cur, order, pick = s2, o2, p2
-            pairs = behind()
-            if cur < top[0]:
-                top = (cur, order, pick)
-    return top[1], top[2]
+        if it == tries - 1:
+            done.append(polish(sorted(range(n), key=lambda i: best[1][i]), best[2], sweeps // 6, HEAT))
+    return polish(*min(done)[1:], sweeps, HEAT * 0.7)[1:]
 
 
 PLAN = {}

from concourse.mybir import AluOpType as A, ActivationFunctionType as F

N, L, W, RO = 8, 256, 8192, 4
NC = 4
CL = L // NC
CE = 16 * CL
HE = CE // 2
NB = CL // 16
KQ = 4
TWO = True
BIG, KV, PAR = 4096.0, 1988.0, 2 ** 18
YB, WB = 160.0, 128.0
U = 2048.0

f32, bf, f16, i32, u16 = "float32", "bfloat16", "float16", "int32", "uint16"
KB = ["one", "t0", "BO", "ID", "LT", "LE", "SD", "SU", "t1", "t2", "E8", "t4", "Mm", "OH", "Bm", "KW", "Ld", "Vu", "Qm", "Fl", "KI", "nKI",
      "Wm", "BO3", "IDu", "SDu", "SUu", "R0", "Dm", "G3", "Qm2", "Mp", "Um", "Sm"]
KH, KF = ["R15", "BOe"], ["A32"]
SCRATCH = {n: ("sbuf", [128, w], d) for n, w, d in [
    ("XA", W, bf), ("XB", W if TWO else 16, bf), ("cin", L, i32), ("yin", L, bf), ("wS", 1, bf), ("thS", L, bf),
    ("cn", L, f16), ("cs", L, f16), ("yb", L, bf), ("ycS", L, f32), ("yyS", L, bf), ("P", 16 * L, bf),
    ("PTs", 16 * L, bf),
    ("ui", L, i32), ("uu", L, i32), ("odd", L, i32), ("Ls", L, f32), ("L2", L, f32), ("va", L, i32), ("vb", L, i32),
    ("off1", L, u16), ("off2", L, u16), ("offv", NC * NB, u16), ("offr", 32, u16), ("sc", L, f32),
    ("cap", CL + 16, f32), ("capv", CL, f32), ("ramp", CL, f32),
    ("pw", L, bf), ("sg", 2 * L, bf), ("md", L, bf), ("fa", L, i32), ("fb", L, i32), ("Ms", L, f32),
    ("ts", L, f32), ("zz", L, f32), ("eta", L, bf), ("qq", L, bf), ("qd", 2 * L, f16), ("ez", L, bf), ("low", L, bf), ("Wn", L, bf), ("nx", 2 * L, bf),
    ("ra", 16, i32), ("rb", 16, i32), ("rc", 16, i32), ("cnt", NC, f32), ("cj", NC, f32), ("col", 40, f32),
    ("msg", RO * L, f16), ("land", RO * L, f16), ("msgv", 2 * RO * L, bf), ("landv", 2 * RO * L, bf),
    ("kf", len(KF) * 128, f32), ("kb", len(KB) * 128, bf), ("kh", len(KH) * 128, f16),
    ("Sel", 144, bf), ("SelN", 144, bf), ("SelW", 144, bf), ("row", 2, i32),
    ("ln32", 16, f32), ("ln32c", 16, f32)]}
SCRATCH.update({"stS": ("sbuf", [128, 2, RO * L], bf), "Ib": ("sbuf", [128, 8 * NC, 2, CL], bf), "Mq": ("sbuf", [128, 8, 16], bf)})
SCRATCH.update({"R": ("psum", [128, 2, 2, HE // 2], f32), "Pa": ("psum", [128, HE, 2], bf), "Pb": ("psum", [128, HE, 2], bf)})
SCRATCH.update({n: ("sbuf", [128, 8 * L, 2], bf) for n in ("x2", "mx")})
SCRATCH.update({"B%d" % c: ("psum", [128, 512], f32) for c in range(NC)})
SEMAPHORES = (["sV", "sS", "sT", "sG", "sent", "dX0", "dX1", "dXB", "dc", "dst00", "dst01", "dst10", "dst11", "dy", "dw", "dth", "oy"]
              + ["oc%d" % c for c in range(NC)] + ["arr%d%s" % (i, x) for i in range(RO * NC) for x in "ab"])

FIG = dict(cy=0.00083, ga=1.56, sc=3.8, pe=0.00042, lat=0.18, ov=0.005, far=2.8, out=0.5, load=8.0)
FIGS = [FIG, dict(FIG, cy=0.00112, pe=0.00056, ga=1.3, sc=2.5, lat=0.18, far=3.2, out=1.1, load=7.0),
        dict(FIG, cy=0.0009, pe=0.00074, ga=1.6, sc=5.0, lat=0.2, far=3.5, out=0.9, load=9.0), dict(FIG, cy=0.001, pe=0.0005, ga=1.9, lat=0.29, ov=0.01, far=4.5, out=0.8)]
MID = dict(FIG, cy=0.00096, pe=0.00056, lat=0.24, far=3.3, out=0.8, load=7.5)
SIZE = (91.0, 108.0, 104.0, 124.0)
STARTS, TRIES, SWEEPS, HEAT, NEAR, SEED = 4, 300, 1500, 0.06, 0.3, 1
PRICE = (4.0, 2.5)


def cost(o, e, P):
    cy, ga, sc, pe, k, fix = o["c"][e]
    return (cy + ga * P["ga"] + sc * P["sc"]) * P["cy"] + pe * P["pe"] + k * P["ov"] * (0.5 if e == "T" else 1) + P.get(fix, fix)


def bank_of(tok):
    if tok[0] == "R" and tok[1:].isdigit():
        return int(tok[1])
    if tok[:2] in ("Pa", "Pb"):
        return 2 + (tok[1] == "b")
    if tok[0] == "B" and tok[1].isdigit():
        return 4 + int(tok[1])
    return None


def build(g, T, topo, core, rank):
    ops = []
    at = [None, 0]

    def part(name):
        at[:] = [name, len(ops)]
    V, S, Pm = g.vector, g.scalar, g.tensor

    def op(c, rd, wr, fn, lat=0.0, sem=None, grp=0):
        banks = []
        rd = ["k." + k[2:] if k[:2] in ("b.", "h.") else k for k in rd]
        for k in list(wr) + list(rd):
            if bank_of(k) is not None and bank_of(k) not in banks:
                banks.append(bank_of(k))
        ops.append(dict(eng="".join(c), c=c, rd=list(rd), wr=list(wr), fn=fn, banks=banks, lat=lat, sem=sem, grp=grp, soft=[], at=(at[0], len(ops) - at[1])))

    def vop(n, rd, wr, fn, ga=0, sc=0):
        op({"V": (max(64, n) if n else 60, ga, sc, 0, 1, 0)}, rd, wr, lambda e: [fn()])

    def vops(k, n, rd, wr, fn):
        op({"V": (k * max(64, n), 0, 0, 0, k, 0)}, rd, wr, fn)

    def sop(n, rd, wr, fn, fix=0.05):
        op({"S": (max(64, n), 0, 0, 0, 1, fix)}, rd, wr, lambda e: [fn()])

    def scale(nv, ns, out, in_, by, add, rd, wr):
        def fn(e):
            if e == "S":
                return [S.activation(out, in_, F.Identity, bias=add, scale=by)]
            if by == 1.0 and add == 0.0:
                return [V.tensor_copy(out, in_)]
            return [V.tensor_scalar(out, in_, by, add, A.mult, A.add)]
        op({"V": (max(64, nv), 0, 0, 0, 1, 0), "S": (max(64, ns), 0, 0, 0, 1, 0.05)}, rd, wr, fn)

    def pick(out, src, n, rd, wr):
        op({"V": (60, n, 0, 0, 1, 0), "S": (78, n, 0, 0, 1, 0)}, rd, wr,
           lambda e: [V.tensor_copy(out, src) if e == "V" else S.activation(out, src, F.Copy)])

    def gop(n, rd, wr, fn):
        op({"G": (2 * n, 0, 0, 0, 0, 0.17)}, rd, wr, lambda e: [fn()])

    def top(k, n, rd, wr, fn, grp=3):
        op({"T": (0, 0, 0, n, k, 0.0)}, rd, wr, fn, grp=grp)

    def mm(out, terms, rd, wr, first=True, last=True, n=CL, more=0):
        def fn(e):
            return [Pm.matmul(out, l, r, first and i == 0, last and i == len(terms) - 1) for i, (l, r) in enumerate(terms)]
        top(len(terms), (len(terms) + more) * max(64, n), rd, wr, fn, first + 2 * last)

    lastd = []

    def dma(q, out, in_, rd, wr, sem, lat):
        op({q: (0, 0, 0, 0, 0, 0.05)}, rd, wr, lambda e: [(g.sync if q == "Y" else g.scalar).dma_start(out, in_)], lat=lat, sem=(sem, 16))
        if q == "Y":
            ops[-1]["soft"] = lastd[-1:]
            lastd.append(len(ops) - 1)

    def m128(buf, i):
        return buf[:, i * 128:(i + 1) * 128]

    def mcl(buf, i, n=1):
        return buf[:, i * CL:(i + n) * CL]

    dma("Y", T.yin[:, :], T.y0[:, :], [], ["yin"], "dy", 2.0)
    dma("Y", T.wS[:, :], T.w[:, :], [], ["wS"], "dw", 2.0)
    dma("Y", T.cin[:, :], T.c0[:, :], [], ["cin"], "dc", 2.0)
    dma("S", T.XA[:, 0:W // 2], T.x0[:, 0:W // 2], [], ["XA0"], "dX0", "load")
    dma("Y", T.XA[:, W // 2:W], T.x0[:, W // 2:W], [], ["XA1"], "dX1", "load")
    for i in range(2):
        dma("Y", T.stS[:, i, 0:L], T.st[:, 0:L], [], ["st0%d" % i], "dst0%d" % i, "load")
    dma("Y", T.thS[0:8, :], T.th[:, :], [], ["th"], "dth", "load")
    for i in range(2):
        dma("Y", T.stS[:, i, L:RO * L], T.st[:, L:RO * L], [], ["st1%d" % i], "dst1%d" % i, 11.0)
    XX = [(T.XA, ["XA0", "XA1"])] * 2
    if TWO:
        dma("Y", T.XB[:, :], T.x0[:, :], ["XA0", "XA1"], ["XB0", "XB1"], "dXB", 8.0)
        XX[1] = (T.XB, ["XB0", "XB1"])

    cols = {n: i for i, n in enumerate(["n", "r0", "r15", "cM", "rpos", "s", "mid", "c0", "dLd", "hVu", "kw", "thr", "bVu", "bQ", "e4",
                                        "j32", "a32", "wf", "cU", "cA", "nr0", "e32", "e3", "dm", "mid2", "big0", "ra", "rb", "dif", "kx", "fl",
                                        "bv", "kp", "uv", "u15"])}
    home = lambda n: (T.kh, KH.index(n)) if n in KH else (T.kf, KF.index(n)) if n in KF else (T.kb, KB.index(n))
    K = lambda n: m128(*home(n))
    C = lambda n: T.col[:, cols[n]:cols[n] + 1]
    kcol = lambda n, k=0: home(n)[0][:, home(n)[1] * 128 + k:(home(n)[1] + 1) * 128:16]
    top8 = lambda buf, i: buf[0:8, i * 128:(i + 1) * 128]

    vop(64, [], ["k.one"], lambda: V.memset(K("one"), 1.0))
    gop(1, [], ["row0"], lambda: g.iota(T.row[:, 0:1], [[0, 1]], 127, -1))

    def asel(out, in_, pat, cmp, fill, base, cm, view=m128):
        gop(128, ["k." + in_], ["k." + out], lambda: g.affine_select(view(*home(out)), view(*home(in_)), pat, cmp, fill, base, cm))
    asel("t0", "one", [[-16, 8], [0, 16]], A.is_ge, 0.0, 0, 1)
    asel("BO", "t0", [[16, 8], [0, 16]], A.is_ge, 0.0, 15, -1)
    asel("LT", "BO", [[1, 128]], A.is_ge, 0.0, -1, -1)
    asel("ID", "one", [[-1, 128]], A.is_equal, 0.0, 0, 1)
    gop(16, [], ["ln32"], lambda: g.iota(T.ln32[:, :], [[512, 16]], 0, 0, allow_small_or_imprecise_dtypes=True))
    asel("SD", "BO", [[1, 128]], A.is_equal, 0.0, -1, -1)
    asel("SU", "BO", [[1, 128]], A.is_equal, 0.0, 1, -1)
    gop(CL, [], ["ramp"], lambda: g.iota(T.ramp[:, :], [[16, CL]], -int(KV), 0, allow_small_or_imprecise_dtypes=True))
    asel("E8", "one", [[1, 128]], A.is_ge, 0.0, 0, -16, top8)
    asel("E8", "E8", [[-1, 128]], A.is_ge, 0.0, 15, 16, top8)
    E8 = top8(*home("E8"))
    vop(128, ["k.LT", "k.ID"], ["k.LE"], lambda: V.tensor_tensor(K("LE"), K("LT"), K("ID"), A.add))

    def cts(out, in_, s1, s2, o0, o1=None):
        if o1 is None:
            vop(1, ["c." + in_], ["c." + out], lambda: V.tensor_scalar(C(out), C(in_), s1, None, o0))
        else:
            scale(1, 1, C(out), C(in_), s1, s2, ["c." + in_], ["c." + out])

    def sc(out, in_, by, k=None):
        col = isinstance(by, str)
        rd = ["k." + in_] + (["c." + by] if col else [])
        o, i = (K(out), K(in_)) if k is None else (kcol(out, k), kcol(in_))
        if out in KH:
            vop(64, rd, ["k." + out], lambda: V.tensor_scalar(o, i, C(by) if col else by, None, A.mult))
        else:
            scale(128 if out in KF else 64, 128 if k is None else 8, o, i, C(by) if col else by, 0.0, rd, ["k." + out])
    scale(1, 1, C("wf"), T.wS[:, :], 1.0, 0.0, ["wS"], ["c.wf"])
    sc("Wm", "BO", "wf")
    vop(1, [], ["c.cA"], lambda: V.memset(C("cA"), -262144.0))
    vop(1, ["row0"], ["row1"], lambda: V.tensor_scalar(T.row[:, 1:2], T.row[:, 0:1], 15, None, A.bitwise_and))
    vop(1, ["row1"], ["c.n"], lambda: V.tensor_copy(C("n"), T.row[:, 1:2]))
    cts("r0", "n", 15.0, None, A.is_equal)
    cts("r15", "n", 0.0, None, A.is_equal)
    vop(1, ["c.r0", "c.r15"], ["c.s"], lambda: V.tensor_tensor(C("s"), C("r0"), C("r15"), A.add))
    vop(1, ["c.r0", "c.r15"], ["c.dif"], lambda: V.tensor_tensor(C("dif"), C("r15"), C("r0"), A.subtract))
    sop(1, ["c.r0"], ["c.e4"], lambda: S.activation(C("e4"), C("r0"), F.Exp, scale=4.0), 1.3)
    row0 = lambda by, add: (add - 15 * by, by)
    for out, in_, (a, b) in (("cM", "n", (0.125, 0.125)), ("rpos", "r0", (-1.0, 1.0)), ("mid", "s", (-0.5, 0.5)), ("c0", "r0", (-101.0, 1.0)),
                             ("nr0", "r0", (-1.0, 0.0)), ("thr", "e4", (1.0, -1.0)), ("dLd", "s", (-PAR / 2, 0.0)), ("mid2", "s", (-1.0, 1.0)),
                             ("big0", "r0", (-BIG, 0.0)), ("hVu", "dif", (-0.5, 0.0)),
                             ("bv", "r15", (0.5, -0.5)), ("kp", "r0", (-2 * U, 2 * U)), ("uv", "r15", (2 * U, 0.0)), ("kx", "n", (0.5, -7.5)), ("bQ", "n", (-8.5, -180.0)), ("fl", "r15", (-300.0, 0.0)),
                             ("j32", "n", (-32.0, 480.0)), ("a32", "r15", (32.0, 0.0)), ("e32", "r0", row0(U, U + 32)),
                             ("e3", "r0", row0(3232 * U, 1441792.0)), ("dm", "r0", row0(-U, 0.0)),
                             ("ra", "r0", row0(U, -2 * U)), ("rb", "r0", (-2 * U, 0.0))):
        cts(out, in_, a, b, A.mult, A.add)
    for out, by, add in (("kw", KV + 60.0, "kx"), ("bVu", 1.5, "bv"), ("u15", -3 * U, "uv")):
        scale(1, 1, C(out), C("r0"), by, C(add), ["c.r0", "c." + add], ["c." + out])
    for nm, in_, by in (("KI", "ID", 2 * U), ("nKI", "ID", -2 * U), ("KW", "BO", "kw"), ("Fl", "BO", "fl"), ("BO3", "BO", "e3"),
                        ("IDu", "ID", U), ("SDu", "SD", U), ("SUu", "SU", U), ("BOe", "BO", "e32"), ("Dm", "BO", "dm"),
                        ("R0", "BO", "rb"), ("R15", "BO", 0.0), ("A32", "one", "a32")):
        sc(nm, in_, by)
    for nm, k, by in (("R0", 0, "ra"), ("R15", 15, "e32")):
        sc(nm, "BO", by, k)

    def inblock(out, prim, a, b):
        cv = lambda x: C(x) if isinstance(x, str) else x
        scale(64, 128, K(out), K(prim), cv(a), cv(b), ["k." + prim] + ["c." + x for x in (a, b) if isinstance(x, str)], ["k." + out])
        vop(128, ["k.BO"], ["k." + out], lambda: V.tensor_tensor(K(out), K(out), K("BO"), A.mult))
    inblock("Mm", "LT", -0.125, "cM")
    asel("Mm", "Mm", [[-1, 128]], A.not_equal, 2.0, 0, 1)
    scale(64, 128, T.Mq[:, :, :], K("Mm"), 1.0, 0.0, ["k.Mm"], ["Mq"])
    vops(2, 64, ["Mq"], ["k.Mp"], lambda e: [V.tensor_copy(T.kb[:, KB.index("Mp") * 128 + 64 * i:KB.index("Mp") * 128 + 64 * i + 64],
                                                           T.Mq[:, :, 8 * i:8 * i + 8]) for i in range(2)])
    inblock("t4", "LT", 63.0, 1.0)
    asel("t4", "t4", [[-1, 128]], A.not_equal, -32.0, 0, 1)
    sc("OH", "t4", "rpos")
    sc("OH", "BO", 0.0, 0)
    inblock("t2", "LE", 32.0, -1.0)
    sc("Bm", "t2", "rpos")
    sc("Bm", "BO", "nr0", 0)
    sc("Bm", "BO", "c0", 15)
    inblock("Ld", "SD", "mid2", "dLd")
    inblock("Vu", "ID", "mid", "hVu")
    sc("Vu", "BO", 0.0, 0)
    inblock("Um", "ID", "kp", "rb")
    sc("Um", "BO", "u15", 15)
    sc("Sm", "nKI", "rpos")
    inblock("Qm", "LT", -8.5, 0.5)
    sc("Qm2", "Qm", 2.0)
    vop(128, ["k.ID", "k.SD"], ["k.G3"], lambda: V.tensor_tensor(K("G3"), K("SD"), K("ID"), A.subtract))
    Kb = Kh = K
    sel = lambda buf, k: buf[:, 16 - k:144 - k]
    vop(72, [], ["Sel"], lambda: V.memset(T.Sel[:, :], 0.0))
    scale(8, 8, T.Sel[:, 16:144:16], kcol("BO"), 1.0, 0.0, ["k.BO"], ["Sel"])
    scale(72, 144, T.SelN[:, :], T.Sel[:, :], -2.0, 0.0, ["Sel"], ["SelN"])
    scale(16, 16, T.ln32c[:, :], T.ln32[:, :], 1.0, C("j32"), ["ln32", "c.j32"], ["ln32c"])
    scale(72, 144, T.SelW[:, :], T.Sel[:, :], C("wf"), 0.0, ["Sel", "c.wf"], ["SelW"])
    vop(L // 2, [], ["low"], lambda: V.memset(T.low[:, :], -YB))
    gop(CL + 16, [], ["cap"], lambda: g.iota(T.cap[:, :], [[0, NB + 1], [-1, 16]], 15, 0, allow_small_or_imprecise_dtypes=True))
    vop(CL + 16, ["c.n"], ["cap"], lambda: V.tensor_scalar(T.cap[:, :], T.cap[:, :], C("n"), None, A.is_equal))
    scale(CL, CL, T.capv[:, :], T.cap[:, 1:CL + 1], BIG, 0.0, ["cap"], ["capv"])
    vop(2 * CL, ["cap"], ["ramp"], lambda: V.tensor_tensor(T.ramp[:, :], T.ramp[:, :], T.cap[:, 0:CL], A.mult))
    vop(2 * CL, ["ramp"], ["capv"], lambda: V.tensor_tensor(T.capv[:, :], T.capv[:, :], T.ramp[:, :], A.add))
    ob = KB.index("one") * 128
    every = lambda n: [n + str(c) for c in range(NC)]

    def tiles(c):
        return (lambda i, n=1: T["B%d" % c][:, i * CL:(i + n) * CL]), (lambda i: "B%d.%d" % (c, i))

    vop(L, ["cin"], every("cs"), lambda: V.tensor_scalar(T.cs[:, :], T.cin[:, :], 1 / U, -1.0, A.mult, A.add))
    scale(L // 2, L, T.yb[:, :], T.yin[:, :], 1.0, YB, ["yin"], every("yb"))
    x7 = T.B2[:, 7 * CL:7 * CL + 2]
    mm(x7, [(Kb("Wm"), T.kb[:, ob:ob + 2])], ["b.Wm", "b.one"], ["B2.7"], n=2)
    scale(1, 1, C("cU"), T.B2[:, 7 * CL:7 * CL + 1], -YB, -PAR / 2, ["B2.7"], ["c.cU"])
    for c in range(NC):
        mm(tiles(c)[0](4), [(Kh("IDu"), mcl(T.cs, c))], ["h.IDu", "cs%d" % c], ["B%d.4" % c])

    def gather(t, out, off, c, otok, ftok):
        X, xt = XX[t % 2]
        for h in range(2):
            pick(out(2 * c + h), X[:, 0:W].indirect(off[:, c * CL + h * CL // 2:c * CL + (h + 1) * CL // 2]),
                 HE, xt + [ftok], ["%s.%d" % (otok, h)])

    def index(c, Fp, ftok, Lb, ltok, off, otok, n=1):
        vop(CL, [ftok, ltok], ["va%d" % c], lambda: V.tensor_tensor(mcl(T.va, c), Fp, mcl(Lb, c), A.add))
        vop(CL, ["va%d" % c], ["vb%d" % c], lambda: V.tensor_scalar(mcl(T.vb, c), mcl(T.va, c), 5, W - 1, A.arith_shift_right, A.bitwise_and))
        vops(n, CL, ["vb%d" % c], [otok], lambda e: [V.tensor_copy(off[:, c * CL + i * CL // n:c * CL + (i + 1) * CL // n], T.vb[:, c * CL + i:(c + 1) * CL:n])
                                                     for i in range(n)])

    def engines(a):
        to = [T.cores[(T.rank_of(a) + 1 + t % (N - 1)) % N] for t in range(RO)]
        return [q for q in topo.engines(a, to[0]) if all(q in topo.engines(a, b) for b in to)]

    def numbers(t, c):
        B, tk = tiles(c)
        s = str(c)
        m = lambda buf: mcl(buf, c)
        mm(B(2), [(Kb("Wm"), m(T.yb))], ["b.Wm", "yb" + s], [tk(2)])
        vop(CL, [tk(2), "c.cU"], ["ui" + s], lambda: V.tensor_scalar(m(T.ui), B(2), C("cU"), None, A.add))
        vop(CL, ["ui" + s], ["uu" + s], lambda: V.tensor_scalar(m(T.uu), m(T.ui), 2047, None, A.bitwise_and))
        vop(CL, ["uu" + s], ["Ms" + s], lambda: V.tensor_scalar(m(T.Ms), m(T.uu), 2.0, 33.0, A.mult, A.add))
        vop(CL, ["ui" + s], ["odd" + s], lambda: V.tensor_scalar(m(T.odd), m(T.ui), 1 - PAR, None, A.bitwise_and))

    def send(t, c, x, out, in_, rd):
        dst = T.cores[(rank + 1 + t % (N - 1)) % N]
        src = T.cores[(rank - 1 - t % (N - 1)) % N]
        rid, pid = topo.addr(dst)[0], topo.addr(dst)[1]
        mask, far = engines(core), engines(src)
        sem = "arr%d%s" % (t * NC + c, x)
        op({"G": (0, 0, 0, 0, 0, "out")}, rd, ["land%d%s" % (t * NC + c, x)],
           lambda e: [g.remote_dma(out, in_, T.sem[sem], T.sem.sent, pid, rid, sum(1 << q for q in mask))], lat="far", sem=(sem, len(far)))
        ops[-1]["sent"] = len(mask)

    def phase_p(t, c):
        B, tk = tiles(c)
        s = str(c)
        m = lambda buf: mcl(buf, c)
        if c < 2:
            cs_ = [0] if c == 0 else list(range(1, NC))
            scale(len(cs_) * CL, len(cs_) * CL, mcl(T.Ls, c, len(cs_)), mcl(T.Ms, c, len(cs_)), 2048.0, C("cA"),
                  ["Ms%d" % i for i in cs_] + ["c.cA"], ["Ls%d" % i for i in cs_])
        vop(CL, [tk(4), "Ms" + s], [tk(3)], lambda: V.tensor_tensor(B(3), B(4), m(T.Ms), A.mult))
        vop(CL, [tk(4)], ["cs" + s], lambda: V.tensor_scalar(m(T.cs), B(4), 1 / U, None, A.mult)) if t else at.append(at.pop() - 1)
        index(c, B(3), tk(3), T.Ls, "Ls" + s, T.off1, "off1" + s)
        gather(t, lambda h: T.P[:, h * HE:(h + 1) * HE], T.off1, c, "P" + s, "off1" + s)
        for h in range(2):
            pp, pt = (T.Pa, T.Pb)[h], ("Pa", "Pb")[h]
            o = c * CE + h * HE
            top(4, 512, ["b.ID", "P%s.%d" % (s, h)], [pt],
                lambda e, o=o, pp=pp: [Pm.transpose(pp[:, 64 * b:64 * b + 64, :], T.P[:, o + b * 128:o + (b + 1) * 128], Kb("ID")) for b in range(4)])
            scale(HE // 2, HE, T.PTs[:, o:o + HE], pp[:, 0:HE // 2, :], 1.0, 0.0, [pt], ["PT%s.%d" % (s, h)])
            top(4, 512, ["b.Mp", "PT%s.%d" % (s, h)], ["R%d" % h],
                lambda e, o=o, h=h: [Pm.matmul(T.R[:, h, :, 64 * b:64 * b + 64], T.PTs[:, o + b * 128:o + (b + 1) * 128], Kb("Mp"), True, True)
                                     for b in range(4)])
            a = t * L + c * CL + h * CL // 2
            for kq in range(0, 8, KQ):
                vops(KQ, CL, ["R%d" % h, "st%d0" % min(t, 1), "st%d1" % min(t, 1)], ["I%s.%d.%d" % (s, h, kq)],
                     lambda e, kq=kq, h=h, a=a: [V.tensor_tensor(T.Ib[:, 8 * c + k, :, h * CL // 2:(h + 1) * CL // 2], T.R[:, h, :, k:HE // 2:8],
                                                                 T.stS[:, :, a:a + CL // 2], A.is_ge) for k in range(kq, kq + KQ)])
        for kq in range(0, 8, KQ):
            mm(B(0), [(sel(T.Sel, k + 8 * i), T.Ib[:, 8 * c + k, i, :]) for k in range(kq, kq + KQ) for i in range(2)],
               ["Sel"] + ["I%s.%d.%d" % (s, h, kq) for h in range(2)], [tk(0)], kq == 0, kq + KQ == 8)
        scale(CL, CL, m(T.yb), T.R[:, :, 0, 0:HE // 2:8], 0.25, YB - 0.484375, ["R0", "R1"], ["yb" + s])
        sop(CL, [tk(0)], ["pw" + s], lambda: S.activation(m(T.pw), B(0), F.Exp, bias=-64.0, scale=8.0))
        top(2, 2 * CL, ["b.OH", "b.Bm", "pw" + s], [tk(1), tk(2)],
            lambda e: [Pm.matmul(B(1), Kb("OH"), m(T.pw), True, True), Pm.matmul(B(2), Kb("Bm"), m(T.pw), True, True)])
        sop(2 * CL, [tk(1), tk(2), "c.thr"], ["sg" + s], lambda: S.activation(m128(T.sg, c), B(1, 2), F.Sign, bias=C("thr")))
        noh, sg, cs = mcl(T.sg, 2 * c), mcl(T.sg, 2 * c + 1), m(T.cs)
        mi = t * NC + c
        mt = "msg%d" % mi
        ohc, mu = mcl(T.msg, mi), mcl(T.msgv, 2 * mi + 1)
        vop(CL, ["sg" + s, "cs" + s], [mt + "a"], lambda: V.tensor_tensor(ohc, cs, noh, A.max))
        send(t, c, "a", mcl(T.land, mi), ohc, [mt + "a"])
        mm(B(4), [(Kb("Vu"), sg)], ["b.Vu", "sg" + s], [tk(4)])
        sop(CL, [tk(4), "c.bVu"], [mt + "c", "cnt" + s], lambda: S.activation(mu, B(4), F.Relu, bias=C("bVu"), accum_out=T.cnt[:, c:c + 1]), 0.07)
        mm(B(3), [(Kb("KW"), noh)], ["b.KW", "sg" + s], [tk(3)])
        vop(CL, [tk(3), "capv"], ["sc" + s], lambda: V.tensor_tensor_scan(m(T.sc), B(3), T.capv[:, :], BIG, A.min, A.add))
        ov = T.offv[:, NB * c:NB * (c + 1)]
        vop(NB, ["sc" + s, "c.big0"], ["offv" + s], lambda: V.tensor_scalar(ov, T.sc[:, c * CL + 15:(c + 1) * CL:16], C("big0"), None, A.add))
        pick(mcl(T.msgv, 2 * mi), T.P[:, c * CE:(c + 1) * CE].indirect(ov), CL, ["offv" + s, "P%s.0" % s, "P%s.1" % s], [mt + "b"])
        send(t, c, "b", m128(T.landv, mi), m128(T.msgv, mi), [mt + "b", mt + "c"])
        mm(B(0), [(Kb("Ld"), sg)], ["b.Ld", "sg" + s], [tk(0)])
        vop(CL, [tk(0), "odd" + s], ["md" + s], lambda: V.tensor_tensor(m(T.md), m(T.odd), B(0), A.is_ge))
        mm(B(5), [(Kh("R15"), ohc)], ["h.R15", mt + "a"], [tk(5)])
        vop(CL, [tk(5), "uu" + s], ["fa" + s], lambda: V.tensor_tensor(m(T.fa), m(T.uu), B(5), A.mult))
        vop(CL, ["fa" + s], ["fb" + s], lambda: V.tensor_scalar(m(T.fb), m(T.fa), 5, 4095, A.arith_shift_right, A.bitwise_and))
        mm(B(4), [(Kh("SUu"), cs), (Kb("Um"), mu)], ["h.SUu", "b.Um", "cs" + s, mt + "c"], [tk(4)])
        mm(B(0), [(Kh("IDu"), cs), (Kb("Sm"), mu), (Kb("nKI"), m(T.md))], ["h.IDu", "b.Sm", "b.nKI", "cs" + s, "md" + s, mt + "c"], [tk(0)])
        mm(B(1), [(Kh("SDu"), cs), (Kh("R0"), ohc), (Kb("KI"), m(T.md))], ["h.SDu", "h.R0", "b.KI", "cs" + s, "md" + s, mt + "a"], [tk(1)])
        vop(CL, [tk(4), "fb" + s], ["ts" + s], lambda: V.tensor_tensor(m(T.ts), m(T.fb), B(4), A.add))
        vop(CL, [tk(0), "ts" + s], ["zz" + s], lambda: V.tensor_tensor(m(T.zz), m(T.ts), B(0), A.max))
        vop(CL, [tk(1), "zz" + s], ["cn" + s], lambda: V.tensor_tensor(m(T.cn), m(T.zz), B(1), A.max))
        if t < RO - 1:
            numbers(t + 1, c)

    weigh = {}

    def phase_q(t, c):
        B, tk = tiles(c)
        s = str(c)
        m = lambda buf: mcl(buf, c)
        mi = t * NC + c
        lt, lw = "land%da" % mi, "land%db" % mi
        le, lv, lg = mcl(T.land, mi), mcl(T.landv, 2 * mi), mcl(T.landv, 2 * mi + 1)
        top(2, 2 * CL, ["h.BOe", "b.BO3", lt], [tk(3), tk(5)],
            lambda e: [Pm.matmul(B(3), Kh("BOe"), le, True, True), Pm.matmul(B(5), Kb("BO3"), le, True, True)])
        vop(CL, ["cn" + s, tk(3)], ["L2" + s], lambda: V.tensor_tensor(m(T.L2), m(T.cn), B(3), A.mult))
        index(c, B(5), tk(5), T.L2, "L2" + s, T.off2, "off2" + s, 2)
        gather(t, lambda h: T.x2[:, c * HE:(c + 1) * HE, h % 2], T.off2, c, "x2" + s, "off2" + s)
        mm(B(6), [(Kh("Dm"), le)], ["h.Dm", lt], [tk(6)])
        xt = ["x2%s.0" % s, "x2%s.1" % s]
        x2 = lambda k, step: T.x2[:, c * HE + k:(c + 1) * HE:step, :]
        pp, pt = (T.Pa, T.Pb)[c % 2], ("Pa", "Pb")[c % 2] + s
        o = HE // 2 + (c // 2) * CL
        vops(2, CL, [lw], [pt], lambda e: [V.tensor_copy(pp[:, o + i:o + CL:2, :], lv) for i in range(2)])
        for h in range(2):
            mm(B(1), [(sel(T.Sel, k), x2(k, 16)) for k in range(8 * h, 8 * h + 8)], ["Sel"] + xt, [tk(1)], h == 0, False)
        mm(B(1), [(E8, T.thS[0:8, c * CL:(c + 1) * CL]), (Kb("BO"), lv)], ["b.E8", "th", "b.BO", lw], [tk(1)], False, False)
        for h in range(2):
            ks = range(4 * h, 4 * h + 4)
            mk = lambda k, i=0, step=1: T.mx[:, c * HE + k * CL + i:c * HE + (k + 1) * CL:step, :]
            vops(4, CL, xt + [pt], ["mx%s.%d" % (s, h)], lambda e, ks=ks: [V.tensor_tensor(mk(k), x2(k, 8), pp[:, o:o + CL, :], A.max) for k in ks])
            mm(B(1), [(sel(T.SelN, k + 8 * i), mk(k, i, 2)) for k in ks for i in range(2)], ["SelN", "mx%s.%d" % (s, h)], [tk(1)], False, h == 1)
        def hit(e):
            weigh[mi] = "Qm" if e == "S" else "Qm2"
            return [S.activation(m(T.eta), B(1), F.Sign, bias=0.5) if e == "S" else V.tensor_scalar(m(T.eta), B(1), 0.0, 0.5, A.is_ge, A.subtract)]
        op({"V": (CL, 0, 0, 0, 1, 0), "S": (CL, 0, 0, 0, 1, 0.05)}, [tk(1)], ["eta" + s], hit)
        top(2, 2 * CL, ["b.Qm", "b.Qm2", "b.Fl", "eta" + s, lw], [tk(0)],
            lambda e: [Pm.matmul(B(0), Kb("Fl"), lg, True, False), Pm.matmul(B(0), Kb(weigh[mi]), m(T.eta), False, True)])
        vop(CL, [tk(0), "c.bQ"], ["qq" + s], lambda: V.tensor_scalar(m(T.qq), B(0), C("bQ"), None, A.is_lt))
        qc, qe = mcl(T.qd, 2 * c), mcl(T.qd, 2 * c + 1)
        vops(2, CL, [tk(6), "qq" + s, "cn" + s], ["qd" + s],
             lambda e: [V.tensor_tensor(qe, m(T.qq), B(6), A.mult), V.tensor_tensor(qc, m(T.qq), m(T.cn), A.mult)])
        mm(B(4), [(Kh("ID"), m(T.cn)), (K("G3"), qe), (K("G3"), qc)], ["k.ID", "k.G3", "cn" + s, "qd" + s], [tk(4)])
        if t == RO - 1:
            scale(CL, CL, m(T.ycS), B(4), 1.0, U, [tk(4)], ["yc" + s])
            dma("Y", mcl(T.yc, c), m(T.ycS), ["yc" + s], ["o.yc" + s], "oc" + s, 2.0)

    def scatter(t, to):
        X, xt = XX[to]
        p = t % 2
        vop(0, ["nx%d" % p, "offr%d" % p, "low"], xt,
            lambda: V.tensor_tensor(X[:, 0:W].indirect(T.offr[:, 16 * p:16 * p + 16]), T.nx[:, p * L:(p + 1) * L], T.low[:, :], A.add), sc=L)

    for c in range(NC):
        numbers(0, c)
    for t in range(RO):
        p = t % 2
        part("start")
        if t < RO - 1:
            su = T.B2[:, 7 * CL:7 * CL + 16]
            mm(su, [(sel(T.SelW, k), T.yb[:, k:L:16]) for k in range(16)], ["SelW"] + every("yb"), ["B2.7"], n=16)
            vop(16, ["B2.7", "c.cU"], ["ra"], lambda su=su: V.tensor_scalar(T.ra[:, :], su, C("cU"), None, A.add))
            vop(16, ["ra"], ["rb"], lambda: V.tensor_scalar(T.rb[:, :], T.ra[:, :], 31, None, A.bitwise_and))
            vop(32, ["rb", "ln32c"], ["rc"], lambda: V.tensor_tensor(T.rc[:, :], T.rb[:, :], T.ln32c[:, :], A.add))
            vop(16, ["rc"], ["offr%d" % p], lambda p=p: V.tensor_copy(T.offr[:, 16 * p:16 * p + 16], T.rc[:, :]))
        for c in range(NC):
            part("p%d" % c)
            phase_p(t, c)
        part("mid")
        if t == RO - 1:
            scale(L // 2, L, T.yyS[:, :], T.yb[:, :], 1.0, -YB, every("yb"), ["yy"])
            dma("Y", T.yy[:, :], T.yyS[:, :], ["yy"], ["o.yy"], "oy", 2.0)
        else:
            a7 = T["B%d" % (NC - 1)][:, 7 * CL:7 * CL + NC]
            ak = "B%d.7" % (NC - 1)
            mm(a7, [(K("A32"), T.cnt[:, :])], ["k.A32"] + every("cnt"), [ak], n=256)
            sop(NC, [ak], ["c.cA"], lambda: S.activation(T.cj[:, :], a7, F.Identity, bias=-262144.0 / NC, accum_out=C("cA")), 0.07)
            old = XX[p][0][:, 0:W].indirect(T.offr[:, 16 * p:16 * p + 16])
            op({"V": (60, L, 0, 0, 1, 0), "S": (78, L, 0, 0, 1, 0)}, XX[p][1] + ["offr%d" % p], ["ez"],
               lambda e, old=old: [V.tensor_scalar(T.ez[:, :], old, 4.0, -WB, A.mult, A.add) if e == "V" else
                                   S.activation(T.ez[:, :], old, F.Identity, bias=-WB, scale=4.0)])
            vop(L, every("yb") + ["ez"], ["Wn"], lambda: V.tensor_tensor(T.Wn[:, :], T.ez[:, :], T.yb[:, :], A.add))
            scale(L // 2, L, T.nx[:, p * L:(p + 1) * L], T.Wn[:, :], 0.125, YB - (YB - WB) / 8 - 0.4375, ["Wn"], ["nx%d" % p])
            if TWO:
                if t > 0:
                    scatter(t - 1, 1 - p)
                scatter(t, 1 - p)
        for c in range(NC):
            part("q%d" % c)
            phase_q(t, c)
        part("end")
        if not TWO and t < RO - 1:
            scatter(t, 0)
    return ops


def depend(ops):
    lastw, readers, deps = {}, {}, []
    for i, o in enumerate(ops):
        d = set()
        for k in o["rd"] + o["wr"]:
            if k in lastw:
                d.add(lastw[k])
        for k in o["wr"]:
            d.update(readers.get(k, ()))
        d.discard(i)
        deps.append(sorted(d))
        for k in o["rd"]:
            readers.setdefault(k, []).append(i)
        for k in o["wr"]:
            lastw[k] = i
            readers[k] = []
    whole, closed = {}, {}
    for i, o in enumerate(ops):
        if o["eng"] == "T":
            b = o["banks"][0]
            if o["grp"] == 1:
                deps[i] = sorted(set(deps[i]) | set(whole.pop(b, [])))
            elif o["grp"] == 2:
                closed[b] = i
            elif o["grp"] == 3:
                deps[i] = sorted(set(deps[i]) | ({closed[b]} if b in closed else set()))
                whole.setdefault(b, []).append(i)
    return deps


def way(o, P):
    return P.get(o["lat"], o["lat"]) + (0.06 if o["eng"] == "T" else 0.0)


def after(xs, t):
    k = len(xs)
    while k > 8 and xs[k - 8] > t:
        k -= 8
    while k and xs[k - 1] > t:
        k -= 1
    return k


def place(ops, pre, succ, cst, key, lat, price, t00):
    n = len(ops)
    left = [len(p) for p in pre]
    ready = [(key[i], i) for i in range(n) if not left[i]]
    es = {e: ([], []) for e in "VSTGY"}
    bs = [([], [], []) for _ in range(8)]
    st, fin, pick = [0.0] * n, [0.0] * n, [""] * n
    while ready:
        x = min(ready)
        ready.remove(x)
        i = x[1]
        t0 = t00[i]
        for j, gap in pre[i]:
            if fin[j] + gap > t0:
                t0 = fin[j] + gap
        best = None
        for e in ops[i]["eng"]:
            c, t = cst[i][e], t0
            S, Fn = es[e]
            while True:
                k = after(Fn, t)
                while k < len(S) and S[k] < t + c - 1e-9:
                    t = max(t, Fn[k])
                    k += 1
                t1 = t
                for b in ops[i]["banks"]:
                    s, f, w = bs[b]
                    k = after(f, t - lat)
                    while k < len(s) and s[k] < t + c + lat - 1e-9:
                        if w[k] != e and f[k] + lat > t:
                            t = f[k] + lat
                        k += 1
                if t == t1:
                    break
            v = t + c + price[i][e == "S"] * c
            if best is None or v < best[0]:
                best = (v, t, e, c)
        v, t, e, c = best
        st[i], fin[i], pick[i] = t, t + c, e
        S, Fn = es[e]
        k = after(Fn, t)
        S.insert(k, t)
        Fn.insert(k, t + c)
        for b in ops[i]["banks"]:
            s, f, w = bs[b]
            k = after(s, t)
            s.insert(k, t)
            f.insert(k, t + c)
            w.insert(k, e)
        for j in succ[i]:
            left[j] -= 1
            if not left[j]:
                ready.append((key[j], j))
    return st, fin, pick


def polisher(ops, deps, pre, rnd):
    n = len(ops)
    tab = [{e: [cost(o, e, P) for P in FIGS] for e in o["eng"]} for o in ops]
    far = [[way(o, P) + P["lat"] for P in FIGS] for o in ops]
    l0, l1, l2, l3 = [P["lat"] for P in FIGS]
    w0, w1, w2, w3 = [25.0 / x for x in SIZE]
    wait = [[d for d in deps[i] if not o["eng"] == "T" == ops[d]["eng"]] for i, o in enumerate(ops)]
    used = set(d for p in deps for d in p)
    users = [[] if i in used else [n] for i in range(n)]
    for i in range(n):
        for d in wait[i]:
            users[d].append(i)
    banks = [o["banks"] for o in ops]
    zero = (0.0, 0.0, 0.0, 0.0)
    end, fin, tail, pos = [zero] * n, [zero] * n, [zero] * (n + 1), [0] * n + [n]
    order, pick = [], []

    def ahead(win, free, bank):
        for i in win:
            e = pick[i]
            a, b, c, d = free[e]
            for k in wait[i]:
                x0, x1, x2, x3 = fin[k]
                if x0 > a:
                    a = x0
                if x1 > b:
                    b = x1
                if x2 > c:
                    c = x2
                if x3 > d:
                    d = x3
            for k in banks[i]:
                j = bank[k]
                bank[k] = i
                if j >= 0 and pick[j] != e:
                    x0, x1, x2, x3 = end[j]
                    if x0 + l0 > a:
                        a = x0 + l0
                    if x1 + l1 > b:
                        b = x1 + l1
                    if x2 + l2 > c:
                        c = x2 + l2
                    if x3 + l3 > d:
                        d = x3 + l3
            x0, x1, x2, x3 = tab[i][e]
            a, b, c, d = end[i] = free[e] = (a + x0, b + x1, c + x2, d + x3)
            x0, x1, x2, x3 = far[i]
            fin[i] = (a + x0, b + x1, c + x2, d + x3)

    def back(win, queue, bank):
        for i in reversed(win):
            e = pick[i]
            a, b, c, d = tail[queue[e]]
            queue[e] = i
            y0, y1, y2, y3 = far[i]
            for k in users[i]:
                x0, x1, x2, x3 = tail[k]
                if x0 + y0 > a:
                    a = x0 + y0
                if x1 + y1 > b:
                    b = x1 + y1
                if x2 + y2 > c:
                    c = x2 + y2
                if x3 + y3 > d:
                    d = x3 + y3
            for k in banks[i]:
                j = bank[k]
                bank[k] = i
                if j < n and pick[j] != e:
                    x0, x1, x2, x3 = tail[j]
                    if x0 + l0 > a:
                        a = x0 + l0
                    if x1 + l1 > b:
                        b = x1 + l1
                    if x2 + l2 > c:
                        c = x2 + l2
                    if x3 + l3 > d:
                        d = x3 + l3
            x0, x1, x2, x3 = tab[i][e]
            tail[i] = (a + x0, b + x1, c + x2, d + x3)

    def behind(b):
        queue, bank, left = {e: n for e in "VSTGY"}, [n] * 8, 12
        for i in order[b + 1:b + 150]:
            if queue[pick[i]] == n:
                queue[pick[i]] = i
                left -= pick[i] != "Y"
            for k in banks[i]:
                if bank[k] == n:
                    bank[k] = i
                    left -= 1
            if not left:
                break
        return queue, bank

    def through(win, b, free, bank, queue, nbank, arcs):
        free, bank = dict(free), list(bank)
        ahead(win, free, bank)
        x = [(fin[i], tail[j]) for i in win for j in users[i] if pos[j] > b] + [(free[e], tail[queue[e]]) for e in free]
        x += [(fin[i], tail[j]) for i, j in arcs if pos[j] > b]
        for i, j in zip(bank, nbank):
            if i >= 0 and j < n and pick[i] != pick[j]:
                x0, x1, x2, x3 = end[i]
                x.append(((x0 + l0, x1 + l1, x2 + l2, x3 + l3), tail[j]))
        return (max([u[0] + v[0] for u, v in x]), max([u[1] + v[1] for u, v in x]), max([u[2] + v[2] for u, v in x]),
                max([u[3] + v[3] for u, v in x]))

    def move(a, near):
        j, x = order[a], rnd()
        if x < 0.15:
            if near[j] and len(ops[j]["eng"]) > 1:
                pick[j] = "V" if pick[j] == "S" else "S"
                return [j], a
        elif x < 0.75:
            skip, on = int(4 * rnd() * rnd()), banks[j] if rnd() < 0.3 else None
            for b in range(a + 1, min(n, a + 50)):
                i = order[b]
                if (pick[i] != pick[j] and on[0] in banks[i]) if on else pick[i] == pick[j]:
                    skip -= 1
                    if skip < 0:
                        break
            if skip < 0 and near[i]:
                win = order[a:b + 1]
                if x < 0.5:
                    mv = {i}
                    for k in reversed(win):
                        if k in mv:
                            mv.update(pre[k])
                    if j not in mv:
                        return [k for k in win if k in mv] + [k for k in win if k not in mv], b
                else:
                    mv = {j}
                    for k in win:
                        if any(d in mv for d in pre[k]):
                            mv.add(k)
                    if i not in mv:
                        return [k for k in win if k not in mv] + [k for k in win if k in mv], b
        return None, a

    def polish(first, engines, sweeps, heat):
        order[:], pick[:] = first, engines
        top = None
        for it in range(sweeps + 1):
            for p, i in enumerate(order):
                pos[i] = p
            back(order, {e: n for e in "VSTGY"}, [n] * 8)
            m = [max(tail[i][f] for i in order[:40]) for f in range(4)]
            cur = m[0] * w0 + m[1] * w1 + m[2] * w2 + m[3] * w3
            if top is None or cur < top[0]:
                top = (cur, list(order), list(pick))
            if it == sweeps:
                return top
            ahead(order, {e: zero for e in "VSTGY"}, [-1] * 8)
            f = int(4 * rnd())
            near = [end[i][f] - tab[i][pick[i]][f] + tail[i][f] > m[f] - NEAR for i in range(n)]
            free, bank, arcs = {e: zero for e in "VSTGY"}, [-1] * 8, []
            for a in range(n):
                j = order[a]
                e = pick[j]
                win, b = move(a, near)
                if win:
                    queue, nbank = behind(b)
                    arcs = [x for x in arcs if pos[x[1]] >= a]
                    m2 = through(win, b, free, bank, queue, nbank, arcs)
                    s2 = m2[0] * w0 + m2[1] * w1 + m2[2] * w2 + m2[3] * w3
                    if s2 <= cur + 1e-9 + heat * (1 - it / sweeps) * rnd() * rnd():
                        cur, m = s2, m2
                        order[a:b + 1] = win
                        for p, i in enumerate(win):
                            pos[i] = a + p
                        back(win, queue, nbank)
                    else:
                        pick[j] = e
                j = order[a]
                ahead([j], free, bank)
                x0, x1, x2, x3 = fin[j]
                arcs += [(j, i) for i in users[j] if x0 + tail[i][0] > m[0] - 2 or x1 + tail[i][1] > m[1] - 2
                         or x2 + tail[i][2] > m[2] - 2 or x3 + tail[i][3] > m[3] - 2]
    return polish


def plan(ops, deps, starts=STARTS, tries=TRIES, sweeps=SWEEPS):
    n = len(ops)
    above, short = [0] * n, []
    for i in range(n):
        a = 0
        for d in deps[i]:
            a |= above[d]
        short.append([d for d in deps[i] if not a >> d & 1])
        for d in deps[i]:
            a |= 1 << d
        above[i] = a
    deps = short
    seed = [SEED]

    def rnd():
        seed[0] = (seed[0] * 1103515245 + 12345) % 2147483648
        return seed[0] / 2147483648.0
    P = MID
    lat = P["lat"]
    cst = [{e: cost(o, e, P) for e in o["eng"]} for o in ops]
    ways = [way(o, P) for o in ops]
    fore, back = [[] for _ in range(n)], [[] for _ in range(n)]
    for i in range(n):
        for d, gap in [(d, ways[d] + (0.0 if ops[i]["eng"] == "T" == ops[d]["eng"] else lat)) for d in deps[i]] + [(d, 0.0) for d in ops[i]["soft"]]:
            fore[i].append((d, gap))
            back[d].append((i, gap))
    pre, succ = [[j for j, x in p] for p in fore], [[j for j, x in p] for p in back]

    polish = polisher(ops, deps, pre, rnd)

    def both(key, price, rounds):
        st, fin, pick = place(ops, fore, succ, cst, key, lat, price, [0.0] * n)
        for k in range(rounds - 1):
            key = [-f for f in place(ops, back, pre, cst, [-f for f in fin], lat, price, ways)[1]]
            st, fin, pick = place(ops, fore, succ, cst, key, lat, price, [0.0] * n)
        return polish(sorted(range(n), key=lambda i: st[i]), pick, 0, 0.0)[0], st, pick, price
    pri = [0.0] * n
    for i in range(n - 1, -1, -1):
        pri[i] = min(cst[i].values()) + max([pri[j] + x for j, x in back[i]], default=ways[i])
    first = both([-p for p in pri], [PRICE] * n, 8)
    free = [i for i in range(n) if len(ops[i]["eng"]) > 1 and ops[i]["at"][0]]
    like = {}
    for i, o in enumerate(ops):
        like.setdefault(o["at"], []).append(i)
    done = []
    for run in range(starts * tries):
        it = run % tries
        if it == 0:
            cur = best = first
        key, price, x = list(cur[1]), cur[3], rnd()
        same = (lambda k: like[ops[k]["at"]]) if rnd() < 0.6 else (lambda k: [k])
        if x < 0.25:
            price = list(price)
            for r in range(1 + int(2 * rnd())):
                v = ((0, 50), (50, 0), (50, 0), PRICE)[int(rnd() * 4)]
                for j in same(free[int(rnd() * len(free))]):
                    price[j] = v
        elif x < 0.6:
            a, d = int(rnd() * n), (rnd() - 0.5) * 4
            for k in range(a, min(n, a + 1 + int(rnd() * rnd() * 60))):
                for j in same(k):
                    key[j] += d
        elif x < 0.75:
            a, d, step = int(rnd() * n), (rnd() - 0.5) * 3, 1 if rnd() < 0.5 else -1
            k = a
            while 0 <= k < n and ops[k]["at"][0] == ops[a]["at"][0]:
                for j in same(k):
                    key[j] += d
                k += step
        else:
            a, w = rnd() * max(cur[1]), rnd() * 6
            for k in range(n):
                if a <= cur[1][k] < a + w:
                    d = rnd() - 0.5
                    for j in same(k):
                        key[j] += d
        s2 = both(key, price, 2)
        if s2[0] <= cur[0] + 0.5 * rnd() * rnd() * (1 - it / tries):
            cur = s2
            if cur[0] < best[0]:
                best = cur
        if it == tries - 1:
            done.append(polish(sorted(range(n), key=lambda i: best[1][i]), best[2], sweeps // 6, HEAT))
    return polish(*min(done)[1:], sweeps, HEAT * 0.7)[1:]


PLAN = {}


def rank_program(g, core, T, topo):
    rank = T.rank_of(core)
    if rank is None:
        return
    ops = build(g, T, topo, core, rank)
    deps = depend(ops)
    if "p" not in PLAN:
        PLAN["p"] = plan(ops, deps)
    order, eng = PLAN["p"][0], PLAN["p"][1]
    Q = {"V": g.vector, "S": g.scalar, "T": g.tensor, "G": g, "Y": g.sync}
    count = {"sV": 0, "sS": 0, "sT": 0, "sG": 0, "sent": 0}
    known = {e: {} for e in Q}
    mark, clock = {}, {}
    lastb = {}
    for i in order:
        o, e = ops[i], eng[i]
        need = set(deps[i])
        for b in o["banks"]:
            if b in lastb and eng[lastb[b]] != e:
                need.add(lastb[b])
            lastb[b] = i
        kn = known[e]
        for d in sorted(need, key=lambda d: -clock[d]["#"]):
            if e == "T" and eng[d] == "T":
                continue
            sem, val = mark[d]
            if kn.get(sem, 0) >= val:
                continue
            Q[e].wait_ge(T.sem[sem], val)
            for k, v in clock[d].items():
                if k != "#" and kn.get(k, 0) < v:
                    kn[k] = v
        ins = o["fn"](e)
        if o["sem"] is None:
            sem = "s" + e
            for x in ins:
                x.then_inc(T.sem[sem], 1)
            count[sem] += len(ins)
            mark[i] = (sem, count[sem])
        else:
            mark[i] = o["sem"]
            count[o["sem"][0]] = o["sem"][1]
            if "sent" in o:
                count["sent"] += o["sent"]
            else:
                ins[0].then_inc(T.sem[o["sem"][0]], 16)
        ck = {} if "sent" in o else dict(kn)
        ck[mark[i][0]] = mark[i][1]
        ck["#"] = len(clock)
        clock[i] = ck
    for sem, val in count.items():
        if val:
            g.wait_ge(T.sem[sem], val)
